import numpy as np, ml_dtypes
CORES = [10,34,74,98]
N = 4
BF = ml_dtypes.bfloat16
L, S, ST, GENS, K = 256, 8, 5, 2, 64
GW, XW = S * L, 16 * L
def parts(rng):
    g = rng.integers(0, XW, (N, 8, 16, GW)); h = rng.integers(0, GW, (N, 8, 16, GW)); x = rng.integers(0, 256, (N, 8, 16, XW))
    return g, h, x, rng.integers(0, 256, (N, 8, 16, L)), rng.integers(800, 1151, (N, 8))
def pack(g, h, x, a, t):
    return {"gn": np.ascontiguousarray(g.reshape(N, 128, GW)).astype(np.int32), "nb": np.ascontiguousarray(h.reshape(N, 128, GW)).astype(np.int32),
            "x": x.reshape(N, 128, XW).astype(np.float32).astype(BF), "th": np.repeat(t, 16, axis=1).reshape(N, 128, 1).astype(np.int32), "a0": a.reshape(N, 128, L).astype(np.float32).astype(BF)}
def setup_inputs(rng):
    return pack(*parts(rng))
def uneven(rng, n):
    v = np.floor(256 * rng.random((N, 8, 16, n)) * np.exp2(-rng.integers(0, 8, (N, 8, 1, n)).astype(np.float64))).astype(np.int64)
    return np.where(rng.random((N, 8, 1, n)) < 0.5, 255 - v, v)
def setup_inputs_spread(rng):
    g = (XW * rng.random((N, 8, 16, GW)) ** 3).astype(np.int64); h = (GW * rng.random((N, 8, 16, GW)) ** 2).astype(np.int64)
    g[:, 1::2] = XW - 1 - g[:, 1::2]; h[:, :, ::2] = GW - 1 - h[:, :, ::2]
    t = np.argsort(rng.random((N, 8)), axis=1) * 510 + rng.integers(0, 510, (N, 8))
    return pack(g, h, uneven(rng, XW), uneven(rng, L), t)
def twoends(rng, n):
    return np.where(rng.random((N, 8, 1, n)) < 0.7, 255 * rng.integers(0, 2, (N, 8, 1, n)), 255 * rng.integers(0, 2, (N, 8, 16, n)))
def setup_inputs_ends(rng):
    g, h, x, a, t = parts(rng)
    g = np.where(rng.random(g.shape) < 0.8, (XW - 1) * rng.integers(0, 2, g.shape), g); h = np.where(rng.random(h.shape) < 0.8, (GW - 1) * rng.integers(0, 2, h.shape), h)
    x = twoends(rng, XW); a = twoends(rng, L); x[..., 0] = 0; x[..., XW - 1] = 255
    for q in range(N): t[q, :7] = rng.permutation(np.array([0, 0, 4080, 4080, 4080, 2294, 2294]))
    t[:, 7] = 0
    for i in (0, 1, L - 2, L - 1):
        g[:, 7, 0, S * i] = XW - 1; h[:, 7, :, S * i] = GW - 1; a[:, 7, :, i] = 0
    g[:, 7, :15, GW - 1] = XW - 1; g[:, 7, 15, GW - 1] = 0
    return pack(g, h, x, a, t)
def setup_inputs_corners(rng):
    g, h, x, a, t = parts(rng); o = rng.permutation(8); t[:, o[0]] = 0; t[:, o[1]] = 4080
    for q in range(N):
        w = rng.permutation(o[2:])
        h[q, w[0]] = np.arange(GW); h[q, w[1]] = (GW - 1) * rng.integers(0, 2, (16, GW)); h[q, w[2]] = np.roll(np.arange(GW), -1)
        g[q, w[3]] = (XW - 1) * rng.integers(0, 2, (16, GW))
        b = w[4]; t[q, b] = 0; x[q, b, :, XW - 1] = 255; g[q, b, 15] = XW - 1
        i = rng.permutation(L)[:L // 2]; a[q, b][:, i] = x[q, b][:, g[q, b, 0, S * i]]
        x[q, w[5]] = 255 * rng.integers(0, 2, (16, XW))
    return pack(g, h, x, a, t)
def setup_inputs_ties(rng):
    g, h, x, a, t = parts(rng)
    x = 8 * rng.integers(0, 32, (N, 8, 1, XW)) + ((np.arange(16)[:, None] == rng.integers(0, 16, (N, 8, 1, XW))) & (rng.random((N, 8, 1, XW)) < 0.5))
    a = 8 * rng.integers(0, 32, (N, 8, 1, L)) + np.zeros((16, 1), np.int64)
    h[:, ::2] = h[:, ::2, :1]
    return pack(g, h, x, a, 16 * (8 * rng.integers(0, 6, (N, 8)) + 1))
def setup_inputs_counts(rng):
    g, h, x, a, t = parts(rng); q = rng.permutation(N); o = rng.permutation(8); w = int(o[0])
    t[q[0]] = 0; t[q[1]] = 4080; t[q[2]] = 4080; t[q[2], o[1:4]] = 0; t[q[3]] = 0
    if N > 4: t[q[4]] = 1170
    if N > 5: t[q[5], o[1:5]] = 0
    t[:, w] = 0; t[q[1], w] = 4080
    u = np.floor(rng.integers(2, 7, (N, 1, XW)) * rng.random((N, 16, XW))).astype(np.int64); u[:, 0] = 0
    x[:, w] = u; x[q[1], w] = 255 - u[q[1]]; x[q[1], w, 0] = 254
    a[:, w] = 255; a[:, w, 0] = 254
    for r, n in ((q[2], 64), (q[3], 8 * int(rng.integers(3, 5)) + int(rng.choice(np.array([2, 3, 5, 6]))))):
        i = rng.permutation(L)[:n]; a[r, w, 0, i] = 255; h[r, w, 0, S * i] = S * i
    return pack(g, h, x, a, t)
def check_inputs(d):
    bad = []
    for k, lo, hi in (("gn", 0, XW - 1), ("nb", 0, GW - 1), ("x", 0, 255), ("th", 0, 4080), ("a0", 0, 255)):
        v = np.asarray(d[k]).astype(np.float64)
        if not (np.min(v) >= lo and np.max(v) <= hi): bad.append("range of " + k)
        elif np.any(v != np.floor(v)): bad.append("whole numbers of " + k)
    v = np.asarray(d["th"]).reshape(-1, 16)
    if np.any(v != v[:, :1]): bad.append("equal rows of th in a group")
    return bad
def reference(gn, nb, x, th, a0):
    G = gn.astype(np.int64).reshape(N, 8, 16, GW); H = nb.astype(np.int64).reshape(N, 8, 16, GW); X = x.astype(np.float32).astype(np.int64).reshape(N, 8, 16, XW)
    lim = th.astype(np.int64).reshape(N, 8, 16)[:, :, :1]; a = a0.astype(np.float32).astype(np.int64).reshape(N, 8, 16, L)
    A = np.zeros(N, np.int64); lane = np.arange(L); kk = np.arange(16)[None, :, None]
    for gen in range(GENS):
        h = np.zeros((N, 8, L), np.int64) + S * lane; p = np.zeros((N, 8, L), np.int64); err = np.zeros((N, 8, L), np.int64)
        dau = G[..., ::S].copy()
        for t in range(ST):
            now = np.zeros(N, np.int64)
            for r in range(N):
                q = (r + t) % N; hr = h[r][:, None, :]; pr = p[r]
                n = np.take_along_axis(np.take_along_axis(G[q], hr, 2), pr[:, None, :], 1)[:, 0]
                T = np.abs(np.take_along_axis(X[q], n[:, None, :], 2) - a[r])
                ho = np.take_along_axis(H[q], hr, 2)
                at = ((pr[:, None, :] + kk) & 15) * GW + ho
                e = np.take_along_axis(G[q].reshape(8, 16 * GW), at.reshape(8, 16 * L), 1)
                v = np.take_along_axis(X[q], e[:, None, :], 2).reshape(8, 16, 16, L)
                D = np.add.reduce(np.abs(v + T[:, :, None, :] - 255), axis=1)
                ok = D <= (lim[q] + (A[q] & 63))[:, :, None]
                found = np.any(ok, axis=1); m = np.argmax(ok, axis=1)
                em = np.take_along_axis(e.reshape(8, 16, L), m[:, None, :], 1)[:, 0]; hm = np.take_along_axis(ho, m[:, None, :], 1)[:, 0]
                an = np.where(found[:, None, :], np.take_along_axis(X[q], em[:, None, :], 2), T)
                dau[r, :, t] = np.where(found, em, n); h[r] = np.where(found, hm, h[r]); p[r] = (pr + 1 + np.where(found, m, 0)) & 15
                err[r] = err[r] + np.where(found, 0, 1); now[q] = np.sum(np.where(found, 0, 1)); a[r] = an
                np.put_along_axis(X[q], (16 * lane + p[r])[:, None, :], an, 2)
            A = now
        order = np.argsort(err * L + lane, axis=2)
        best = np.take_along_axis(dau, order[:, :, None, :K], 3)
        come = np.where((np.arange(K) & 1) == 1, np.roll(best, 1, axis=0), best)
        worst = order[:, :, ::-1][:, :, :K]
        np.put_along_axis(G, (S * worst)[:, :, None, :], come, 3)
    return {"yg": G[..., ::S].reshape(N, 128, L).astype(np.float32), "ya": a.reshape(N, 128, L).astype(np.float32), "ys": np.add.reduce(X.reshape(N, 8, 16, L, 16), axis=4).reshape(N, 128, L).astype(np.float32)}

@@ -1,0 +1,523 @@
+from concourse.mybir import AluOpType, AxisListType, ActivationFunctionType
+OP = AluOpType
+AF = ActivationFunctionType
+N, GENS, ST, K = 4, 2, 5, 64
+L, GW, XW = 256, 2048, 4096
+ZC = 2048
+XB = XW + 16
+MAGIC = 12582913.0
+TAU = GENS * ST
+CUT = [(0, 128, (64, 64)), (128, 256, (64, 64))]
+NCH = len(CUT)
+DMAS = 26
+ORDER = """D0 NG1 DA0 WW1 OF1 TR0 E1.0 NL1 D1 X0.0 DA1 E1.1 X0.1 TR1 AB0.0 AB0.1 WW0 X1.0 GO0 GV0 PK0 YY0 X1.1 PC0 AB1.0 M10 ML0
+ AB1.1 GO1 EE GV1 MC0 PK1 M30 M20 YY1 RR0' PC1 SB0' M11 OF0' ML1 NG0' M21 MC1 M31 ST CO E0.1' E0.0' HI NL0' RR1' SB1'""".split()
+FIRST = """LC WW1 RR0 SB0 NG0 OF0 RR1 RT SB1 GC E0.0 E0.1 Q1 Q0 Q3 Q8 Q5 Q2 Q7 WW0 Q10 NL0 OF1 Q11 NG1 D0 DA0 TR0 Q9 E1.0 NL1 D1
+ X0.0 X0.1 DA1 TR1 Q6 E1.1 AB0.0 AB0.1 X1.0 GO0 GV0 PK0 X1.1 Q4 PC0 AB1.0 EE M10 AB1.1 GO1 ML0 M30 MC0 YY0 GV1 M20 PK1 YY1
+ RR0' PC1 M11 SB0' OF0' ML1 MC1 CO NG0' M31 M21 ST E0.0' E0.1' RR1' SB1' HI NL0'""".split()
+ROTA = (0, 2, 3, 4, 8, 10, 11)
+TRQ = ["aaggggvvvvvvvvvv", "aagggggggvvvvvvv"]
+HFA, YYA = (1, 0), (1, 0)
+
+SCRATCH = {}
+for _n, _w, _d in (
+        ("gi", GW, "int32"), ("g4", 4 * GW, "float32"), ("n4", 4 * GW, "int32"), ("g16", GW, "float16"), ("xr", XB, "bfloat16"), ("w1", GW, "bfloat16"),
+        ("eg", 16 * L, "float16"), ("uu", 16 * L, "float16"), ("ab", 16 * L, "float16"), ("tr", 16 * L, "bfloat16"),
+        ("rr", L, "float16"), ("sb", L, "float16"), ("ww", L, "bfloat16"), ("m0", L, "bfloat16"), ("of", L, "uint16"), ("ng", L, "float16"),
+        ("nl", 16, "uint16"), ("nf", 16, "float32"), ("dd", L, "bfloat16"), ("tt", L, "bfloat16"), ("xl", L, "uint16"),
+        ("ok", L, "bfloat16"), ("ff", L, "float16"), ("qq", 3 * L, "float16"), ("yy", L, "bfloat16"), ("xo", 16, "uint16"), ("ti", 64, "float32"),
+        ("yi", 16, "int32"), ("li", 64, "int32"), ("zs", 16, "float32"), ("zr", 16, "float32"), ("zf", 16, "float32"),
+        ("lo", 64 * TAU, "uint16"), ("ln", 64 * TAU, "uint16"), ("lc", 64, "uint16"), ("ci", 16, "int32"), ("cs", 16, "uint16"), ("cb", 16, "float32"),
+        ("ao", L * TAU, "bfloat16"), ("an", L * TAU, "bfloat16"), ("ho", 32 * TAU, "float16"), ("hn", 32 * TAU, "float16"), ("hl", 80, "float16"), ("er", 16, "float32"),
+        ("ed", 5 * L, "float16"), ("eb", L, "float16"), ("nb2", L, "float16"), ("et", L, "float16"),
+        ("og", L, "float32"), ("gm", L, "float32"), ("da", L, "float32"), ("sr", L, "float32"), ("rv", L, "float32"),
+        ("bi", 2 * K, "float32"), ("o16", L, "float16"), ("ind", L, "float16"), ("pre", L, "float16"), ("on", L, "float16"), ("x1", L, "float16"), ("x2", L, "float16"),
+        ("pl", 16, "uint16"), ("pr", 16, "uint16"), ("af", 1, "float32"), ("ai", 2, "int32"), ("lim", 1, "float32"), ("thi", 1, "int32"), ("thf", 1, "float32"),
+        ("jj", L, "int32"), ("jf", L, "float32"), ("jt", 128, "int32"), ("kk", 16, "int32"), ("kb", 16, "int32"), ("kf", 16, "float32"), ("wf", 16, "float32"),
+        ("pi", 4, "int32"), ("pf", 8, "float32"), ("u16", 16, "float32"), ("tw", 16, "bfloat16"), ("ts", 16, "bfloat16"), ("tm", 16, "bfloat16"),
+        ("se", 2048, "float16"), ("ss", 2048, "float16"), ("idn", 128, "float16"), ("ib", 128, "bfloat16"), ("bo", 128, "float16"), ("bh", 128, "bfloat16"), ("bn", 128, "bfloat16"),
+        ("lt", 128, "float16"), ("l2", 128, "float16"), ("one", 128, "float16"), ("rt", 384, "float16"), ("r2", 384, "float16"), ("jr", 384, "int32"),
+        ("fo", 3 * L, "float32")):
+    SCRATCH[_n] = ("sbuf", [128, _w], _d)
+PSUM = ["pe0", "pe1", "pd0", "pd1", "pl0", "pl1", "pa", "pb"]
+for _n in PSUM:
+    SCRATCH[_n] = ("psum", [128, 512], "float32")
+SEMAPHORES = ["v", "a", "p", "gc", "loc", "b0", "b1"] + ["d%d" % i for i in range(DMAS)] + ["h%d" % i for i in range(TAU)]
+for _b in range(NCH):
+    SEMAPHORES += ["li%d_%d" % (_t, _b) for _t in range(TAU)] + ["ar%d_%d" % (_t, _b) for _t in range(TAU)]
+
+
+def rank_program(g, core, T, topo):
+    rank = T.rank_of(core)
+    if rank is None:
+        return
+    queues = {"v": g.vector, "a": g.scalar, "p": g.tensor, "g": g, "s": g.sync}
+    own = {"v": "v", "a": "a", "p": "p", "g": "gc"}
+    cnt = {"v": 0, "a": 0, "p": 0, "gc": 0}
+    known = {q: {} for q in queues}
+    clock = {}
+    wr, rd = {}, {}
+    nd = [0]
+    locs = [0]
+
+    def R(name, lo=0, hi=None):
+        return (name, lo, SCRATCH[name][1][-1] if hi is None else hi)
+
+    def need(q, reads, writes):
+        best = {}
+
+        def look(lists, rs):
+            for name, lo, hi in rs:
+                ps = name in PSUM
+                for l, h, q2, (s, n) in lists.get(name, ()):
+                    if (q2 != q if ps else (l < hi and lo < h)) and n > known[q].get(s, 0) and n > best.get(s, 0):
+                        best[s] = n
+        look(wr, reads + writes)
+        look(rd, writes + [r for r in reads if r[0] in PSUM])
+        for s in sorted(best):
+            n = best[s]
+            if n > known[q].get(s, 0):
+                queues[q].wait_ge(T.sem[s], n)
+                known[q][s] = n
+                for s2, n2 in clock.get((s, n), {}).items():
+                    if n2 > known[q].get(s2, 0):
+                        known[q][s2] = n2
+
+    def note(q, reads, writes, tok):
+        for name, lo, hi in writes:
+            for d in (wr, rd):
+                d[name] = [e for e in d.get(name, ()) if not (lo <= e[0] and e[1] <= hi)]
+            wr[name].append((lo, hi, q, tok))
+        for name, lo, hi in reads:
+            rd[name] = [e for e in rd.get(name, ()) if not (lo <= e[0] and e[1] <= hi and e[2] == q)] + [(lo, hi, q, tok)]
+
+    def op(q, fn, reads, writes):
+        need(q, reads, writes)
+        s = own[q]
+        fn(queues[q]).then_inc(T.sem[s], 1)
+        cnt[s] += 1
+        clock[(s, cnt[s])] = dict(known[q])
+        note(q, reads, writes, (s, cnt[s]))
+
+    def dma(pairs, reads, reg, out=False):
+        need("s", reads, [] if out else [reg])
+        toks = []
+        for o, src in pairs:
+            s = "d%d" % nd[0]
+            nd[0] += 1
+            g.sync.dma_start(o, src).then_inc(T.sem[s], 16)
+            clock[(s, 16)] = dict(known["s"])
+            toks.append((s, (s, 16)))
+        for s, tok in toks:
+            if len(pairs) > 1:
+                wr[reg[0]] = list(wr.get(reg[0], ())) + [reg[1:3] + (s, tok)]
+            else:
+                note(s, reads, [] if out else [reg], tok)
+
+    def send(dst, name, lo, hi, to, lo2, sem):
+        need("g", [(name, lo, hi)], [])
+        rid, pid, _ = topo.addr(dst)
+        ne = len(topo.engines(core, dst))
+        g.remote_dma(T[to][:, lo2:lo2 + hi - lo], T[name][:, lo:hi], T.sem[sem], T.sem.loc, pid, rid, topo.mask(core, dst))
+        locs[0] += ne
+        note(sem, [], [(to, lo2, lo2 + hi - lo)], (sem, ne))
+
+    def X(r):
+        if len(r) == 1:
+            return T[r[0]][:], R(r[0])
+        if len(r) == 4:
+            return T[r[0]][:, r[1]:r[2]:r[3]], r[0:3]
+        return T[r[0]][:, r[1]:r[2]], r
+
+    def side(r):
+        if len(r) == 2 and isinstance(r[0], tuple):
+            return X(r[0])[0].indirect(X(r[1])[0]), [X(r[0])[1], X(r[1])[1]]
+        a, i = X(r)
+        return a, [i]
+
+    def sc(s):
+        return (X(s)[0], [X(s)[1]]) if isinstance(s, tuple) else (s, [])
+
+    def ts(out, src, s1, op0, s2=None, op1=None, tag=None):
+        o, io = side(out)
+        a, ia = side(src)
+        c1, i1 = sc(s1)
+        c2, i2 = sc(s2)
+        w = [tag] if tag else io
+        if op1 is None:
+            op("v", lambda v: v.tensor_scalar(o, a, c1, None, op0), ia + i1, w)
+        else:
+            op("v", lambda v: v.tensor_scalar(o, a, c1, c2, op0, op1), ia + i1 + i2, w)
+
+    def tt(out, a, b, op0, more=()):
+        o, io = side(out)
+        x, ix = side(a)
+        y, iy = side(b)
+        op("v", lambda v: v.tensor_tensor(o, x, y, op0), ix + iy + list(more), io)
+
+    def cp(out, src, tag=None):
+        o, io = side(out)
+        a, ia = side(src)
+        op("v", lambda v: v.tensor_copy(o, a), ia + (io[1:] if len(io) > 1 else []), [tag] if tag else io[:1])
+
+    def act(out, src, f, bias=0.0, scale=1.0, tag=None):
+        o, io = side(out)
+        a, ia = side(src)
+        b, ib = sc(bias)
+        c, ic = sc(scale)
+        op("a", lambda s: s.activation(o, a, f, bias=b, scale=c), ia + ib + ic, [tag] if tag else io)
+
+    def sel(out, src, pattern, cmp, base, ch, tag=None):
+        o, io = side(out)
+        a, ia = side(src)
+        op("g", lambda q: q.affine_select(o, a, pattern, cmp, 0.0, base, ch), ia, [tag] if tag else io)
+
+    def iota(out, pattern, base, ch):
+        o, io = side(out)
+        op("g", lambda q: q.iota(o, pattern, base, ch), [], io)
+
+    def fill(out, c):
+        o, io = side(out)
+        op("v", lambda v: v.memset(o, c), [], io)
+
+    def mm(out, lhsT, rhs, start=True, stop=True):
+        o, io = side(out)
+        a, ia = side(lhsT)
+        b, ib = side(rhs)
+        op("p", lambda t: t.matmul(o, a, b, start, stop), ia + ib, io)
+
+    nxt = T.cores[(rank + 1) % N]
+
+    H = GW // 2
+    for lo in (0, H):
+        dma([(T.gi[:, lo:lo + H], T.gn[:, lo:lo + H])], [], R("gi", lo, lo + H))
+    dma([(T.n4[:, 0:GW], T.nb[:])], [], R("n4", 0, GW))
+    dma([(T.thi[:], T.th[:])], [], R("thi"))
+    dma([(T.an[:, 0:L], T.a0[:])], [], R("an", 0, L))
+    dma([(T.xr[:, 0:ZC], T.x[:, 0:ZC])], [], R("xr", 0, ZC))
+    iota(("pi", 0, 1), [[0, 1]], 0, 1)
+    iota(("jj",), [[1, L]], 0, 0)
+    iota(("kk",), [[0, 4], [-1, 4]], 16, 1)
+    fill(("w1",), 1.0)
+    fill(("xr", ZC, XB), 0.0)
+    dma([(T.xr[:, ZC + 1:XW + 1], T.x[:, ZC:XW])], [], R("xr", ZC, XB))
+    for k in range(1, 4):
+        reg = R("n4", k * GW, (k + 1) * GW)
+        dma([(T.n4[k:128, reg[1]:reg[2]], T.nb[0:128 - k, :])], [], reg)
+        rows = [(T.n4[u::16, reg[1]:reg[2]], T.nb[16 - k + u::16, :]) for u in range(k)]
+        dma(rows, [], reg)
+    sel(("ss",), ("w1",), [[16384, 16], [-16, 8], [-16384, 16]], OP.is_ge, 0, 1)
+    sel(("ss",), ("ss",), [[-16384, 16], [16, 8], [16384, 16]], OP.is_ge, 15, -1)
+    sel(("se",), ("w1",), [[-1024, 16], [16, 8], [1025, 16]], OP.is_equal, 0, -1)
+    iota(("jr",), [[4, 3], [32, 8], [1, 16]], 4, 0)
+    ts(("pi", 1, 2), ("pi", 0, 1), 15, OP.bitwise_and)
+    ts(("pi", 2, 3), ("pi", 0, 1), 4, OP.arith_shift_right)
+    cp(("pf", 0, 3), ("pi", 0, 3))
+    ROW, GRP = ("pf", 1, 2), ("pf", 2, 3)
+    cp(("jf",), ("jj",))
+    ts(("idn",), ("jf", 0, 128), ("pf", 0, 1), OP.is_equal)
+    ts(("jt",), ("jj", 0, 128), 4, OP.arith_shift_right)
+    ts(("bo",), ("jt",), GRP, OP.is_equal)
+    ts(("u16",), ("jf", 0, 16), ROW, OP.is_equal)
+    ts(("pf", 3, 4), ROW, 8.0, OP.mult)
+    ts(("pf", 4, 5), ROW, 16.0, OP.mult)
+    ts(("pf", 5, 6), ROW, 1.0, OP.add, 2048.0, OP.mult)
+    ts(("pf", 6, 7), ROW, 5.0, OP.is_ge)
+    ts(("pf", 7, 8), GRP, 16.0, OP.mult, ("pf", 0, 1), OP.add)
+    ts(("zf",), ("jf", 0, 16), 128.0, OP.mult, ("pf", 3, 4), OP.add)
+    cp(("lc", 0, 16), ("zf",))
+    ts(("lc", 16, 32), ("zf",), 0.0, OP.mult)
+    ts(("kb",), ("jj", 0, 16), 2, OP.arith_shift_right)
+    ts(("ts",), ("kb",), 2048.0, OP.mult)
+    cp(("tm",), ("u16",))
+    for lo in (0, H):
+        ts(("g4", lo, lo + H), ("gi", lo, lo + H), 1.0 + 2.0 ** -12, OP.mult, MAGIC, OP.add)
+        act(("g4", lo, lo + H), ("g4", lo, lo + H), AF.Copy, bias=-(MAGIC + 2048.0))
+
+    def constants():
+        ts(("kk",), ("kk",), 15, OP.bitwise_and)
+        fill(("wf",), 16777216.0)
+        for j in range(4):
+            ts(("kb",), ("kk",), j, OP.arith_shift_right, 1, OP.bitwise_and)
+            ts(("kf",), ("kb",), 2.0 ** -(1 << j) - 1.0, OP.mult, 1.0, OP.add)
+            tt(("wf",), ("wf",), ("kf",), OP.mult)
+        cp(("tw",), ("wf",))
+        ts(("bh",), ("bo",), 0.5, OP.mult)
+        ts(("bn",), ("bo",), -0.5, OP.mult)
+        cp(("ib",), ("idn",))
+        ts(("cb",), ("jf", 0, 16), 256.0, OP.mult, ("pf", 4, 5), OP.add)
+        ts(("cb", 8, 16), ("cb", 8, 16), 1.0, OP.add)
+        cp(("one",), ("w1", 0, 128))
+        cp(("on",), ("w1", 0, L))
+        ts(("jt",), ("jj", 0, 128), 15, OP.bitwise_and)
+        ts(("l2",), ("jt",), ROW, OP.is_gt)
+        tt(("lt",), ("l2",), ("bo",), OP.mult)
+        ts(("thf",), ("thi",), 1.0, OP.add)
+        ts(("lim",), ("thf",), 16777216.0, OP.mult)
+        cp(("og",), ("g4", 0, GW, 8))
+
+    def turns():
+        ts(("rt",), ("jr",), ("pf", 7, 8), OP.is_equal)
+        ts(("r2",), ("jr",), -16.0, OP.add, ("pf", 7, 8), OP.is_equal)
+        tt(("rt",), ("rt",), ("r2",), OP.add)
+
+    def turn(n):
+        s, lo = 1 + n // 4, 512 * (n % 4)
+        bank = ("pa", "pd1")[n % 2]
+        mm((bank,), ("rt", (s - 1) * 128, s * 128), ("g16", lo, lo + 512))
+        out = ("g4", s * GW + lo, s * GW + lo + 512)
+        if n in ROTA:
+            act(out, (bank,), AF.Copy)
+        else:
+            cp(out, (bank,))
+
+    def turn_own():
+        cp(("o16",), ("og",))
+        for s in range(1, 4):
+            bank = ("pa", "pd1")[s % 2]
+            mm((bank, 0, L), ("rt", (s - 1) * 128, s * 128), ("o16",))
+            if s == 2:
+                act(("g4", s * GW, (s + 1) * GW, 8), (bank, 0, L), AF.Copy)
+            else:
+                cp(("g4", s * GW, (s + 1) * GW, 8), (bank, 0, L))
+
+    def lst(tau, b, kind):
+        c0, c1 = CUT[b][0:2]
+        n = (c1 - c0) // 16
+        if tau % ST == 0:
+            lo = (0 if kind in (1, 3) else 16) + c0 // 16
+            return ("lc", lo, lo + n)
+        lo = 64 * tau + c0 // 4 + kind * n
+        return ("ln", lo, lo + n)
+
+    def run(tok, tau):
+        gen, t = divmod(tau, ST)
+        tok, _, js = tok.partition(".")
+        kind = tok.rstrip("0123456789") if tok[0] != "M" else tok[0:2]
+        b = int(tok[len(kind):]) if tok[len(kind):] else 0
+        c0, c1, subs = CUT[b]
+        n = c1 - c0
+        l0, l1 = c0 // 16, c1 // 16
+        lc = l1 - l0
+        pe, pd, pn = "pe%d" % (b % 2), "pd%d" % (b % 2), "pl%d" % (b % 2)
+        gw = GW if t == 0 else 4 * GW
+        e0 = c0 + sum(subs[0:int(js)]) if js else 0
+        e1 = e0 + subs[int(js)] if js else 0
+        q = 3 * c0
+        sco = (pd, 256 + c0, 256 + c1)
+        le, lr, ls = [(pn, 64 + k * lc, 64 + (k + 1) * lc) for k in range(3)]
+        hv = ("ho", 32 * tau + l0, 32 * tau + l1)
+        hf = ("ho", 32 * tau + 16 + l0, 32 * tau + 16 + l1)
+        li = [("li", c0 // 4 + k * lc, c0 // 4 + (k + 1) * lc) for k in range(4)]
+        yi = ("yi", l0, l1)
+        ti = [("ti", 16 * k + l0, 16 * k + l1) for k in range(4)]
+        if kind == "RR":
+            cp(("rr", c0, c1), (("n4", 0, gw), lst(tau, b, 1)))
+        elif kind == "SB":
+            act(("sb", c0, c1), (("ts", 0, 16), lst(tau, b, 2)), AF.Copy)
+            mm(("pb", c0, c1), ("idn",), ("rr", c0, c1), True, False)
+            mm(("pb", c0, c1), ("idn",), ("sb", c0, c1), False, True)
+            mm(("pb", 256 + c0, 256 + c1), ("idn",), ("rr", c0, c1))
+            act(("m0", c0, c1), (("tm", 0, 16), lst(tau, b, 2)), AF.Copy)
+        elif kind == "OF":
+            cp(("of", c0, c1), ("pb", c0, c1))
+        elif kind == "NG":
+            tt(("ng", c0, c1), (("g4", 0, GW), lst(tau, b, 3)), ("m0", c0, c1), OP.mult)
+            for a in range(16):
+                mm((pn, 0, lc), ("ss", a * 128, a * 128 + 128), ("ng", c0 + a, c1, 16), a == 0, a == 15)
+        elif kind == "NL":
+            ts(("nl", l0, l1), (pn, 0, lc), 2048.0, OP.add)
+            act(("nf", l0, l1), (pn, 0, lc), AF.Copy)
+        elif kind == "WW":
+            act(("ww", c0, c1), (("tw", 0, 16), lst(tau, b, 2)), AF.Copy)
+            ts(("zr", l0, l1), lst(tau, b, 1), 2048.0, OP.add)
+            cp(("zs", l0, l1), lst(tau, b, 0))
+        elif kind == "E":
+            act(("eg", 16 * e0, 16 * e1), (("g4", 0, gw), ("of", e0, e1)), AF.Copy)
+            for s in range(16):
+                mm((pe, e0, e1), ("se", s * 128, s * 128 + 128), ("eg", 16 * e0 + s, 16 * e1, 16), s == 0, s == 15)
+        elif kind == "D":
+            an, ao = ("an", L * tau) if t or tau == 0 else ("ao", L * (tau - 1))
+            tt(("dd", c0, c1), (("xr",), ("nl", l0, l1)), (an, ao + c0, ao + c1), OP.subtract)
+        elif kind == "DA":
+            act(("tt", c0, c1), ("dd", c0, c1), AF.Abs)
+        elif kind == "TR":
+            for s, w in enumerate(TRQ[b]):
+                o, tag = ("tr", 16 * c0 + s, 16 * c1, 16), ("tr%d" % s, c0, c1)
+                if w == "a":
+                    act(o, ("tt", c0, c1), AF.Copy, tag=tag)
+                elif w == "g":
+                    sel(o, ("tt", c0, c1), [[0, n]], OP.is_ge, 0, 0, tag=tag)
+                else:
+                    cp(o, ("tt", c0, c1), tag=tag)
+        elif kind == "X":
+            ts(("xl", e0, e1), (pe, e0, e1), 2048.0, OP.add)
+            tt(("uu", 16 * e0, 16 * e1), (("xr",), ("xl", e0, e1)), ("tr", 16 * e0, 16 * e1), OP.add, more=[("tr%d" % s, e0, e1) for s in range(16)])
+        elif kind == "AB":
+            act(("ab", 16 * e0, 16 * e1), ("uu", 16 * e0, 16 * e1), AF.Abs, bias=-255.0)
+            for s in range(16):
+                mm((pd, e0, e1), ("ss", s * 128, s * 128 + 128), ("ab", 16 * e0 + s, 16 * e1, 16), s == 0, s == 15)
+        elif kind == "GO":
+            act((pd, c0, c1), (pd, c0, c1), AF.Relu, bias=("lim",), scale=-16777216.0)
+        elif kind == "GV":
+            tt(("ok", c0, c1), (pd, c0, c1), ("ww", c0, c1), OP.min)
+            mm(sco, ("bh",), ("ok", c0, c1))
+        elif kind == "PK":
+            tt(("ff", c0, c1), ("ok", c0, c1), sco, OP.is_gt)
+            tt(("qq", q, q + n), ("ff", c0, c1), (pe, c0, c1), OP.mult)
+            tt(("qq", q + n, q + 2 * n), ("ff", c0, c1), ("pb", 256 + c0, 256 + c1), OP.mult)
+            act(("qq", q + 2 * n, q + 3 * n), ("ff", c0, c1), AF.Copy, scale=("pf", 5, 6))
+        elif kind == "PC":
+            for a in range(16):
+                mm((pn, 64, 64 + 3 * lc), ("ss", a * 128, a * 128 + 128), ("qq", q + a, q + 3 * n, 16), a == 0, a == 15)
+        elif kind == "YY":
+            if t == ST - 1:
+                act(("nb2", c0, c1), sco, AF.Relu, bias=1.0, scale=-1.0)
+            if YYA[b]:
+                mm((pn, 384, 384 + n), ("ib",), ("tt", c0, c1), True, False)
+                mm((pn, 384, 384 + n), ("bn",), ("ok", c0, c1), False, True)
+                act(("yy", c0, c1), (pn, 384, 384 + n), AF.Relu)
+            else:
+                tt(("yy", c0, c1), ("tt", c0, c1), sco, OP.subtract)
+        elif kind == "M1":
+            if HFA[b]:
+                act(hf, ls, AF.Relu, bias=1.0, scale=-1.0)
+            else:
+                ts(hf, ls, 0.0, OP.is_equal)
+            ts(("xo", l0, l1), le, 2048.0, OP.add)
+            tt(ti[0], ls, ("zs", l0, l1), OP.add)
+            tt(ti[1], hf, ("zr", l0, l1), OP.mult)
+            tt(ti[2], lr, ti[1], OP.add)
+            tt(yi, ti[0], ti[2], OP.add)
+            ts(li[2], yi, 11, OP.arith_shift_right, 15, OP.bitwise_and)
+        elif kind == "ML":
+            if t < ST - 1:
+                for k, m in ((1, 8191), (3, 2047), (0, 24576)):
+                    ts(li[k], yi, m, OP.bitwise_and)
+                o = 64 * tau + c0 // 4
+                cp(("lo", o, o + 4 * lc), ("li", c0 // 4, c0 // 4 + 4 * lc))
+                send(nxt, "lo", o, o + 4 * lc, "ln", o + 64, "li%d_%d" % (tau, b))
+        elif kind == "M2":
+            ao = L * tau
+            tt(("ao", ao + c0, ao + c1), (("xr",), ("xo", l0, l1)), ("yy", c0, c1), OP.max)
+            if t < ST - 1:
+                send(nxt, "ao", ao + c0, ao + c1, "an", ao + L + c0, "ar%d_%d" % (tau, b))
+        elif kind == "MC":
+            tt(("ci", l0, l1), li[2], ("cb", l0, l1), OP.add)
+            cp(("cs", l0, l1), ("ci", l0, l1))
+        elif kind == "M3":
+            tt(ti[3], hf, ("nf", l0, l1), OP.mult)
+            tt(hv, le, ti[3], OP.add)
+        elif kind == "ST":
+            cp((("xr",), ("cs",)), ("ao", L * tau, L * tau + L))
+        elif kind == "HI":
+            if t in (1, 2, 3):
+                send(T.cores[(rank - t) % N], "ho", 32 * tau, 32 * tau + 32, "hn", 32 * tau, "h%d" % tau)
+        elif kind == "CO":
+            if tau < TAU - 1:
+                mm(("pa", 256, 272), ("one",), ("ho", 32 * tau + 16, 32 * tau + 32))
+                op("v", lambda v: v.tensor_reduce(T.af[:], T.pa[:, 256:272], AxisListType.X, OP.add), [R("pa")], [R("af")])
+                cp(("ai", 0, 1), ("af",))
+                ts(("ai", 1, 2), ("ai", 0, 1), 63, OP.bitwise_and)
+                ts(("lim",), ("ai", 1, 2), ("thf",), OP.add, 16777216.0, OP.mult)
+        elif kind == "EE" and t == ST - 1:
+            early_end(gen)
+
+    def plane(gen, t):
+        return "hn" if t in (1, 2, 3) else "ho", 32 * (ST * gen + t)
+
+    def spread(p0, p1):
+        for a in range(16):
+            ts(("ed", p0 * L + a, p1 * L, 16), ("hl", p0 * 16, p1 * 16), ("u16", a, a + 1), OP.mult, tag=("ed%d" % a, p0 * L, p1 * L))
+        need("p", [("ed%d" % a, p0 * L, p1 * L) for a in range(16)], [])
+
+    def early_end(gen):
+        for t in range(4):
+            b, o = plane(gen, t)
+            cp(("hl", 16 * t, 16 * t + 16), (b, o, o + 16))
+            if t == 0:
+                cp(("er",), (b, o + 16, o + 32))
+            else:
+                tt(("er",), ("er",), (b, o + 16, o + 32), OP.add)
+        cp(("hl", 64, 80), ("er",))
+        spread(0, 5)
+        mm(("pa", 0, L), ("bo",), ("ed", 4 * L, 5 * L))
+        act(("eb",), ("pa", 0, L), AF.Copy)
+        ts(("gm",), ("og",), ("pf", 6, 7), OP.mult)
+
+    def registers_and_sums():
+        cp(("fo", L, 2 * L), ("ao", L * (TAU - 1), L * TAU))
+        dma([(T.ya[:], T.fo[:, L:2 * L])], [R("fo", L, 2 * L)], None, True)
+        for h in range(2):
+            o = h * (ZC + 1)
+            for s in range(16):
+                mm(("pe0", 128 * h, 128 * h + 128), ("ib",), ("xr", o + s, o + ZC, 16), s == 0, s == 15)
+        cp(("fo", 2 * L, 3 * L), ("pe0", 0, L))
+        dma([(T.ys[:], T.fo[:, 2 * L:3 * L])], [R("fo", 2 * L, 3 * L)], None, True)
+
+    def end(gen):
+        b, o = plane(gen, 4)
+        tt(("et",), ("eb",), ("nb2",), OP.add)
+        ts(("ind",), ("et",), ROW, OP.is_equal)
+        op("v", lambda v: v.tensor_tensor_scan(T.pre[:], T.on[:], T.ind[:], 0.0, OP.mult, OP.add), [R("on"), R("ind")], [R("pre")])
+        mm(("pa", 300, 301), ("lt",), ("pre", L - 1, L))
+        cp(("hl", 64, 80), (b, o, o + 16))
+        ts(("x1",), ("pre",), ("pa", 300, 301), OP.add, -1.0, OP.add)
+        tt(("x2",), ("x1",), ("ind",), OP.mult)
+        for a in range(16):
+            mm(("pa", 320, 336), ("ss", a * 128, a * 128 + 128), ("x2", a, L, 16), a == 0, a == 15)
+        spread(4, 5)
+        for t in range(5):
+            mm(("pb", 0, L), ("ss", t * 128, t * 128 + 128), ("ed", t * L, (t + 1) * L), t == 0, t == 4)
+        tt(("da",), ("pb", 0, L), ("gm",), OP.add)
+        cp(("pl",), ("pa", 320, 336))
+        cp((("sr",), ("pl",)), ("da",))
+        ob = K * gen
+        send(nxt, "sr", 0, K, "bi", ob, "b%d" % gen)
+        ts(("pr",), ("pa", 320, 336), -1.0, OP.mult, 255.0, OP.add)
+        cp((("rv",), ("pr",)), ("og",))
+        cp(("rv", 0, K, 2), ("sr", 0, K, 2))
+        if gen == GENS - 1:
+            registers_and_sums()
+        cp(("rv", 1, K, 2), ("bi", ob + 1, ob + K, 2))
+        cp(("og",), (("rv",), ("pr",)))
+
+    for tau in range(TAU):
+        gen, t = divmod(tau, ST)
+        if tau == 0:
+            for tok in FIRST:
+                if tok[0] == "Q":
+                    turn(int(tok[1:]))
+                elif tok == "RT":
+                    turns()
+                elif tok == "LC":
+                    constants()
+                elif tok == "GC":
+                    act(("g16",), ("g4", 0, GW), AF.Copy)
+                else:
+                    run(tok.rstrip("'"), 1 if tok[-1] == "'" else 0)
+            continue
+        if t == 0:
+            for tok in ORDER:
+                if tok[-1] == "'":
+                    run(tok[0:-1], tau)
+            turn_own()
+        for tok in ORDER:
+            if tok[-1] != "'":
+                run(tok, tau)
+            elif t < ST - 1:
+                run(tok[0:-1], tau + 1)
+        if t == ST - 1:
+            end(gen)
+            if gen < GENS - 1:
+                cp(("g4", 0, GW, 8), ("og",))
+
+    ts(("fo", 0, L), ("og",), 0.0, OP.is_le, 2047.0, OP.add)
+    tt(("fo", 0, L), ("fo", 0, L), ("og",), OP.add)
+    dma([(T.yg[:], T.fo[:, 0:L])], [R("fo", 0, L)], None, True)
+    for i in range(nd[0]):
+        if known["s"].get("d%d" % i, 0) < 16:
+            g.sync.wait_ge(T.sem["d%d" % i], 16)
+    g.wait_ge(T.sem.loc, locs[0])
+    for s in ("v", "a", "p", "gc"):
+        g.sync.wait_ge(T.sem[s], cnt[s])

@@ -4,38 +4,47 @@ AF = ActivationFunctionType
 N, GENS, ST, K = 4, 2, 5, 64
 L, GW, XW = 256, 2048, 4096
 ZC = 2048
-XB = XW + 16
 MAGIC = 12582913.0
+BIG = 2.0 ** 40
 TAU = GENS * ST
 CUT = [(0, 128, (64, 64)), (128, 256, (64, 64))]
+PLAIN = ((0, 0),)
 NCH = len(CUT)
 DMAS = 26
-ORDER = """D0 NG1 DA0 WW1 OF1 TR0 E1.0 NL1 D1 X0.0 DA1 E1.1 X0.1 TR1 AB0.0 AB0.1 WW0 X1.0 GO0 GV0 PK0 YY0 X1.1 PC0 AB1.0 M10 ML0
- AB1.1 GO1 EE GV1 MC0 PK1 M30 M20 YY1 RR0' PC1 SB0' M11 OF0' ML1 NG0' M21 MC1 M31 ST CO E0.1' E0.0' HI NL0' RR1' SB1'""".split()
-FIRST = """LC WW1 RR0 SB0 NG0 OF0 RR1 RT SB1 GC E0.0 E0.1 Q1 Q0 Q3 Q8 Q5 Q2 Q7 WW0 Q10 NL0 OF1 Q11 NG1 D0 DA0 TR0 Q9 E1.0 NL1 D1
- X0.0 X0.1 DA1 TR1 Q6 E1.1 AB0.0 AB0.1 X1.0 GO0 GV0 PK0 X1.1 Q4 PC0 AB1.0 EE M10 AB1.1 GO1 ML0 M30 MC0 YY0 GV1 M20 PK1 YY1
- RR0' PC1 M11 SB0' OF0' ML1 MC1 CO NG0' M31 M21 ST E0.0' E0.1' RR1' SB1' HI NL0'""".split()
+LW = 80
+SR, BI, OG = 64, (320, 0), 384
+ORDER = """D0 DA0 RR1 WW1 TA0 OF1 TB0.0 MK1 NG1 TB0.1 X0.0 E1.0 NL1 D1 DA1 X0.1 E1.1 TA1 TB1.0 TB1.1 AB0.0 AB0.1 PZ0 PZ1 X1.0 GO0 GV0 PK0 YY0 PC0 X1.1
+ AB1.0 M10 ML0 FL0 XO0 M20 AB1.1 EE RR0' WW0' OF0' MK0' GO1 GV1 PK1 E0.0' FL1 YY1 PC1 NG0' SA M11 ML1 XO1 SB M21 ST E0.1' SC CO HI NL0'""".split()
+FIRST = """LC OF0 NG0 NL0 E0.0 E1.0v E0.1 RT GC OF1 NG1 NL1 D0 DA0 TA0 TB0.0 TB0.1 D1 DA1 E1.1 X0.0 TA1 TB1.0 TB1.1 X0.1 AB0.0 Q0 Q1 AB0.1 X1.0 GO0 GV0 PK0 YY0 PC0
+ M10 ML0 X1.1 AB1.0 Q2 Q3 XO0 M20 Q4 Q5 AB1.1 Q6 Q7 GO1 GV1 PK1 YY1 PC1 Q8 Q9 M11 ML1 Q10 Q11 XO1 M21 RR0' WW0' OF0' MK0' E0.0' NG0' ST E0.1' CO NL0'""".split()
+AGAIN = """OW E0.0 E1.0v OF0 NG0 NL0 E0.1 OF1 NG1 NL1 D0 DA0 TA0 TB0.0 TB0.1 D1 DA1 E1.1 X0.0 TA1 TB1.0 TB1.1 X0.1 AB0.0 AB0.1 OT X1.0 GO0 GV0 PK0 YY0 PC0
+ X1.1 AB1.0 M10 ML0 XO0 M20 AB1.1 GO1 GV1 PK1 YY1 PC1 RR0' WW0' OF0' MK0' M11 ML1 XO1 E0.0' M21 NG0' ST E0.1' CO NL0'""".split()
 ROTA = (0, 2, 3, 4, 8, 10, 11)
-TRQ = ["aaggggvvvvvvvvvv", "aagggggggvvvvvvv"]
-HFA, YYA = (1, 0), (1, 0)
+TBQ = ("gvg", "vgv", "gvg", "vgv")
+ORDER = """D0 MK1 RR1 NG1 WW1 PZ1 XL0.1 OF1 DA0 TA0 E1.1v NM1 NL1 TB0.1 X0.0 PA0.0 D1 E1.0 X0.1 DA1 PB0.0 F1.0 F1.1 AB0.0 TA1 AB0.1 PZ0 AM0.0 AM0.1 EE TB1.0 XL1.0 TB1.1 XL1.1 X1.0 GO0 GV0 X1.1 AB1.0 PK0 AM1.0 PC0 AB1.1 M10 ML0 AM1.1 GO1 GV1 PK1 YY0 FL0 XO0 WW0' YY1 FL1 PC1 M20 MK0' RR0' M11 SA OF0' E0.0' NG0' ML1 NM0' XO1 E0.1' HI M21 NL0' SB F0.0' ST SC CO XL0.0' F0.1'""".split()
+AGAIN = """E1.0v OW E0.0 NM0 NL0 NM1 D0 DA0 F0.0 F1.0 NL1 D1 E0.1 TA0 OF0 XL0.0 F0.1 X0.0v PA0.0 DA1 TB0.1 PB0.0 OF1 XL0.1 TA1 E1.1 X0.1 TB1.0 F1.1 AB0.0 AB0.1 AM0.0 XL1.0 TB1.1 AM0.1 XL1.1 GO0 X1.0 GV0 PK0 AB1.0 X1.1 PC0 AM1.0 M10 ML0 AB1.1 OT AM1.1 GO1 GV1 YY0 XO0 PK1 WW0' MK0' RR0' M20 YY1 PC1 M11 OF0' XO1 E0.0' NG0' E0.1' NM0' ML1 CO M21 ST F0.0' XL0.0' NL0' F0.1'""".split()
+FIRST = """LC NM1 E0.0v NL1 F0.0 GC E1.1 NM0 NL0 E1.0v D0 OF0 F1.1 E0.1 DA0 XL0.0 TA0 TB0.1 X0.0 OF1 F0.1 D1 RT PA0.0 PB0.0 F1.0 AB0.0 DA1 AM0.0 TA1 XL0.1 X0.1 TB1.1 AB0.1 TB1.0 XL1.1 AM0.1 GO0 X1.1 Q0 XL1.0 X1.0 Q1 Q3 Q2 GV0 PK0 PC0 Q5 M10 AB1.1 AM1.1 Q7 Q9 Q4 AB1.0 Q11 AM1.0 ML0 GO1 Q6 GV1 PK1 MK0' WW0' XO0 NG0' YY0 PC1 YY1 Q8 M11 M20 XO1 NM0' Q10 ML1 CO M21 NL0' ST RR0' OF0' E0.0v' F0.0' E0.1' XL0.0' F0.1'""".split()
+ROTA = (1, 2, 4, 7, 8, 10, 11)
+TBQ = ('gga', 'ggv', 'gvv', 'gvg')
 
 SCRATCH = {}
 for _n, _w, _d in (
-        ("gi", GW, "int32"), ("g4", 4 * GW, "float32"), ("n4", 4 * GW, "int32"), ("g16", GW, "float16"), ("xr", XB, "bfloat16"), ("w1", GW, "bfloat16"),
+        ("gi", GW, "int32"), ("g4", 4 * GW, "float32"), ("n4", 4 * GW, "int32"), ("g16", GW, "float16"), ("xr", XW + 16, "bfloat16"), ("w1", GW, "bfloat16"),
         ("eg", 16 * L, "float16"), ("uu", 16 * L, "float16"), ("ab", 16 * L, "float16"), ("tr", 16 * L, "bfloat16"),
-        ("rr", L, "float16"), ("sb", L, "float16"), ("ww", L, "bfloat16"), ("m0", L, "bfloat16"), ("of", L, "uint16"), ("ng", L, "float16"),
-        ("nl", 16, "uint16"), ("nf", 16, "float32"), ("dd", L, "bfloat16"), ("tt", L, "bfloat16"), ("xl", L, "uint16"),
-        ("ok", L, "bfloat16"), ("ff", L, "float16"), ("qq", 3 * L, "float16"), ("yy", L, "bfloat16"), ("xo", 16, "uint16"), ("ti", 64, "float32"),
-        ("yi", 16, "int32"), ("li", 64, "int32"), ("zs", 16, "float32"), ("zr", 16, "float32"), ("zf", 16, "float32"),
-        ("lo", 64 * TAU, "uint16"), ("ln", 64 * TAU, "uint16"), ("lc", 64, "uint16"), ("ci", 16, "int32"), ("cs", 16, "uint16"), ("cb", 16, "float32"),
-        ("ao", L * TAU, "bfloat16"), ("an", L * TAU, "bfloat16"), ("ho", 32 * TAU, "float16"), ("hn", 32 * TAU, "float16"), ("hl", 80, "float16"), ("er", 16, "float32"),
-        ("ed", 5 * L, "float16"), ("eb", L, "float16"), ("nb2", L, "float16"), ("et", L, "float16"),
-        ("og", L, "float32"), ("gm", L, "float32"), ("da", L, "float32"), ("sr", L, "float32"), ("rv", L, "float32"),
-        ("bi", 2 * K, "float32"), ("o16", L, "float16"), ("ind", L, "float16"), ("pre", L, "float16"), ("on", L, "float16"), ("x1", L, "float16"), ("x2", L, "float16"),
-        ("pl", 16, "uint16"), ("pr", 16, "uint16"), ("af", 1, "float32"), ("ai", 2, "int32"), ("lim", 1, "float32"), ("thi", 1, "int32"), ("thf", 1, "float32"),
-        ("jj", L, "int32"), ("jf", L, "float32"), ("jt", 128, "int32"), ("kk", 16, "int32"), ("kb", 16, "int32"), ("kf", 16, "float32"), ("wf", 16, "float32"),
-        ("pi", 4, "int32"), ("pf", 8, "float32"), ("u16", 16, "float32"), ("tw", 16, "bfloat16"), ("ts", 16, "bfloat16"), ("tm", 16, "bfloat16"),
-        ("se", 2048, "float16"), ("ss", 2048, "float16"), ("idn", 128, "float16"), ("ib", 128, "bfloat16"), ("bo", 128, "float16"), ("bh", 128, "bfloat16"), ("bn", 128, "bfloat16"),
+        ("rr", L, "float16"), ("ww", L, "bfloat16"), ("m0", L, "bfloat16"), ("of", L, "uint16"), ("ng", L, "float16"), ("nf", L, "float16"),
+        ("r0", L, "float16"), ("o0", L, "uint16"), ("w0", L, "bfloat16"), ("dd", L, "bfloat16"), ("xl", L, "uint16"),
+        ("ok", L, "bfloat16"), ("ff", L, "float16"), ("qq", 3 * L, "float16"), ("yy", L, "bfloat16"), ("ti", 32, "float32"),
+        ("yi", 16, "int32"), ("li", LW, "int32"), ("zz", 32, "float32"), ("z0", 32, "float32"), ("cb", 16, "float32"),
+        ("lo", LW * TAU, "uint16"), ("ln", LW * TAU, "uint16"), ("ao", L * TAU, "bfloat16"), ("an", L * TAU, "bfloat16"),
+        ("ho", 32 * TAU, "uint16"), ("hn", 32 * TAU, "uint16"), ("hv", 128, "float16"), ("hf", 128, "float16"), ("hm", 128, "float16"), ("hw", 128, "float16"),
+        ("hc", 16, "float16"), ("e1", 48, "float16"), ("er", 16, "float16"), ("eb", L, "float16"),
+        ("wn", OG + L, "float32"), ("da", L, "float32"), ("o16", L, "float16"), ("ind", L, "float16"), ("pre", L, "float16"), ("on", L, "float16"),
+        ("x1", L, "float16"), ("x2", L, "float16"), ("pl", 16, "uint16"), ("pr", 16, "uint16"), ("kr", 32, "int32"), ("kf", 64, "float32"), ("ob", 16, "float32"),
+        ("af", 1, "float32"), ("ai", 2, "int32"), ("lim", 1, "float32"), ("thi", 1, "int32"), ("thf", 1, "float32"),
+        ("jj", L, "int32"), ("jf", L, "float32"), ("jt", 128, "int32"), ("kb", 32, "int32"), ("wf", 64, "float32"),
+        ("pi", 4, "int32"), ("pf", 16, "float32"), ("u16", 16, "float32"), ("tw", 16, "bfloat16"), ("tm", 16, "bfloat16"),
+        ("se", 2048 + 32, "float16"), ("sz", 144, "float16"), ("idn", 128, "float16"), ("ib", 128, "bfloat16"), ("bo", 128, "float16"), ("bm", 128, "float16"),
+        ("bh", 128, "bfloat16"), ("bn", 128, "bfloat16"), ("b15", 128, "bfloat16"), ("b0", 128, "float16"), ("d5", 128, "float16"),
         ("lt", 128, "float16"), ("l2", 128, "float16"), ("one", 128, "float16"), ("rt", 384, "float16"), ("r2", 384, "float16"), ("jr", 384, "int32"),
         ("fo", 3 * L, "float32")):
     SCRATCH[_n] = ("sbuf", [128, _w], _d)
@@ -138,16 +147,15 @@ def rank_program(g, core, T, topo):
     def sc(s):
         return (X(s)[0], [X(s)[1]]) if isinstance(s, tuple) else (s, [])
 
-    def ts(out, src, s1, op0, s2=None, op1=None, tag=None):
+    def ts(out, src, s1, op0, s2=None, op1=None):
         o, io = side(out)
         a, ia = side(src)
         c1, i1 = sc(s1)
         c2, i2 = sc(s2)
-        w = [tag] if tag else io
         if op1 is None:
-            op("v", lambda v: v.tensor_scalar(o, a, c1, None, op0), ia + i1, w)
+            op("v", lambda v: v.tensor_scalar(o, a, c1, None, op0), ia + i1, io)
         else:
-            op("v", lambda v: v.tensor_scalar(o, a, c1, c2, op0, op1), ia + i1 + i2, w)
+            op("v", lambda v: v.tensor_scalar(o, a, c1, c2, op0, op1), ia + i1 + i2, io)
 
     def tt(out, a, b, op0, more=()):
         o, io = side(out)
@@ -155,10 +163,17 @@ def rank_program(g, core, T, topo):
         y, iy = side(b)
         op("v", lambda v: v.tensor_tensor(o, x, y, op0), ix + iy + list(more), io)
 
-    def cp(out, src, tag=None):
+    def cp(out, src, q="v", tag=None, more=()):
         o, io = side(out)
         a, ia = side(src)
-        op("v", lambda v: v.tensor_copy(o, a), ia + (io[1:] if len(io) > 1 else []), [tag] if tag else io[:1])
+        reads = ia + list(more) + (io[1:] if len(io) > 1 else [])
+        writes = [tag] if tag else io[:1]
+        if q == "v":
+            op("v", lambda v: v.tensor_copy(o, a), reads, writes)
+        elif q == "a":
+            op("a", lambda s: s.activation(o, a, AF.Copy, bias=0.0, scale=1.0), reads, writes)
+        else:
+            op("g", lambda s: s.affine_select(o, a, [[0, len(range(*out[1:]))]], OP.is_ge, 0.0, 0, 0), reads, writes)
 
     def act(out, src, f, bias=0.0, scale=1.0, tag=None):
         o, io = side(out)
@@ -166,11 +181,6 @@ def rank_program(g, core, T, topo):
         b, ib = sc(bias)
         c, ic = sc(scale)
         op("a", lambda s: s.activation(o, a, f, bias=b, scale=c), ia + ib + ic, [tag] if tag else io)
-
-    def sel(out, src, pattern, cmp, base, ch, tag=None):
-        o, io = side(out)
-        a, ia = side(src)
-        op("g", lambda q: q.affine_select(o, a, pattern, cmp, 0.0, base, ch), ia, [tag] if tag else io)
 
     def iota(out, pattern, base, ch):
         o, io = side(out)
@@ -180,13 +190,26 @@ def rank_program(g, core, T, topo):
         o, io = side(out)
         op("v", lambda v: v.memset(o, c), [], io)
 
-    def mm(out, lhsT, rhs, start=True, stop=True):
+    def scan(out, d0, d1, first):
+        op("v", lambda v: v.tensor_tensor_scan(X(out)[0], X(d0)[0], X(d1)[0], first, OP.mult, OP.add), [X(d0)[1], X(d1)[1]], [X(out)[1]])
+
+    def total(out, src):
+        op("v", lambda v: v.tensor_reduce(X(out)[0], X(src)[0], AxisListType.X, OP.add), [X(src)[1]], [X(out)[1]])
+
+    def mm(out, lhsT, rhs, start=True, stop=True, more=()):
         o, io = side(out)
         a, ia = side(lhsT)
         b, ib = side(rhs)
-        op("p", lambda t: t.matmul(o, a, b, start, stop), ia + ib, io)
+        op("p", lambda t: t.matmul(o, a, b, start, stop), ia + ib + list(more), io)
+
+    def onto(a):
+        return ("sz", 15 - a, 143 - a)
+
+    def move(a, b):
+        return ("se", 16 + 129 * a - b, 144 + 129 * a - b)
 
     nxt = T.cores[(rank + 1) % N]
+    XR = ("xr", 0, XW + 1)
 
     H = GW // 2
     for lo in (0, H):
@@ -197,18 +220,15 @@ def rank_program(g, core, T, topo):
     dma([(T.xr[:, 0:ZC], T.x[:, 0:ZC])], [], R("xr", 0, ZC))
     iota(("pi", 0, 1), [[0, 1]], 0, 1)
     iota(("jj",), [[1, L]], 0, 0)
-    iota(("kk",), [[0, 4], [-1, 4]], 16, 1)
+    fill(("xr", ZC, ZC + 8), 0.0)
     fill(("w1",), 1.0)
-    fill(("xr", ZC, XB), 0.0)
-    dma([(T.xr[:, ZC + 1:XW + 1], T.x[:, ZC:XW])], [], R("xr", ZC, XB))
+    dma([(T.xr[:, ZC + 1:XW + 1], T.x[:, ZC:XW])], [], R("xr", ZC, XW + 1))
     for k in range(1, 4):
         reg = R("n4", k * GW, (k + 1) * GW)
         dma([(T.n4[k:128, reg[1]:reg[2]], T.nb[0:128 - k, :])], [], reg)
         rows = [(T.n4[u::16, reg[1]:reg[2]], T.nb[16 - k + u::16, :]) for u in range(k)]
         dma(rows, [], reg)
-    sel(("ss",), ("w1",), [[16384, 16], [-16, 8], [-16384, 16]], OP.is_ge, 0, 1)
-    sel(("ss",), ("ss",), [[-16384, 16], [16, 8], [16384, 16]], OP.is_ge, 15, -1)
-    sel(("se",), ("w1",), [[-1024, 16], [16, 8], [1025, 16]], OP.is_equal, 0, -1)
+    op("g", lambda q: q.affine_select(T.se[:, 16:2064], T.w1[:], [[-1024, 16], [16, 8], [1025, 16]], OP.is_equal, 0.0, 0, -1), [R("w1")], [R("se", 16, 2064)])
     iota(("jr",), [[4, 3], [32, 8], [1, 16]], 4, 0)
     ts(("pi", 1, 2), ("pi", 0, 1), 15, OP.bitwise_and)
     ts(("pi", 2, 3), ("pi", 0, 1), 4, OP.arith_shift_right)
@@ -218,43 +238,65 @@ def rank_program(g, core, T, topo):
     ts(("idn",), ("jf", 0, 128), ("pf", 0, 1), OP.is_equal)
     ts(("jt",), ("jj", 0, 128), 4, OP.arith_shift_right)
     ts(("bo",), ("jt",), GRP, OP.is_equal)
-    ts(("u16",), ("jf", 0, 16), ROW, OP.is_equal)
-    ts(("pf", 3, 4), ROW, 8.0, OP.mult)
-    ts(("pf", 4, 5), ROW, 16.0, OP.mult)
-    ts(("pf", 5, 6), ROW, 1.0, OP.add, 2048.0, OP.mult)
-    ts(("pf", 6, 7), ROW, 5.0, OP.is_ge)
-    ts(("pf", 7, 8), GRP, 16.0, OP.mult, ("pf", 0, 1), OP.add)
-    ts(("zf",), ("jf", 0, 16), 128.0, OP.mult, ("pf", 3, 4), OP.add)
-    cp(("lc", 0, 16), ("zf",))
-    ts(("lc", 16, 32), ("zf",), 0.0, OP.mult)
-    ts(("kb",), ("jj", 0, 16), 2, OP.arith_shift_right)
-    ts(("ts",), ("kb",), 2048.0, OP.mult)
-    cp(("tm",), ("u16",))
+    ts(("sz",), ("w1", 0, 144), 0.0, OP.mult)
+    cp(("sz", 15, 128, 16), ("bo", 0, 128, 16))
+    for lo in (0, 2064):
+        ts(("se", lo, lo + 16), ("w1", 0, 16), 0.0, OP.mult)
     for lo in (0, H):
         ts(("g4", lo, lo + H), ("gi", lo, lo + H), 1.0 + 2.0 ** -12, OP.mult, MAGIC, OP.add)
         act(("g4", lo, lo + H), ("g4", lo, lo + H), AF.Copy, bias=-(MAGIC + 2048.0))
+        if lo == 0:
+            ts(("u16",), ("jf", 0, 16), ROW, OP.is_equal)
+            cp(("tm",), ("u16",))
+            ts(("pf", 3, 4), ROW, 8.0, OP.mult, 1024.0, OP.add)
+            ts(("pf", 4, 5), ROW, 16.0, OP.mult)
+            ts(("pf", 5, 6), ROW, 2048.0, OP.mult, 33.0 * 1024.0, OP.add)
+            ts(("pf", 6, 7), ROW, 5.0, OP.is_ge)
+            ts(("pf", 7, 8), GRP, 16.0, OP.mult, ("pf", 0, 1), OP.add)
+            ts(("pf", 8, 9), ROW, 15.0, OP.is_equal, 0.25, OP.mult)
+            ts(("pf", 9, 10), ROW, 0.0, OP.is_equal)
+            ts(("pf", 10, 11), ROW, -1.0, OP.add)
 
     def constants():
-        ts(("kk",), ("kk",), 15, OP.bitwise_and)
-        fill(("wf",), 16777216.0)
-        for j in range(4):
-            ts(("kb",), ("kk",), j, OP.arith_shift_right, 1, OP.bitwise_and)
-            ts(("kf",), ("kb",), 2.0 ** -(1 << j) - 1.0, OP.mult, 1.0, OP.add)
-            tt(("wf",), ("wf",), ("kf",), OP.mult)
-        cp(("tw",), ("wf",))
+        fill(("wf", 0, 16), 0.5)
+        fill(("wf", 16, 32), 0.0)
+        scan(("wf", 32, 48), ("wf", 0, 16), ("wf", 16, 32), 2.0 * BIG)
+        tt(("wf", 48, 64), ("wf", 32, 48), ("u16",), OP.mult)
+        total(("pf", 11, 12), ("wf", 48, 64))
+        ts(("kb", 0, 16), ("jj", 0, 16), 3, OP.bitwise_and)
+        ts(("kb", 16, 32), ("jj", 0, 16), 2, OP.arith_shift_right)
+        ts(("wf", 0, 16), ("kb", 0, 16), ROW, OP.is_gt, 2.0 ** -20 - 1.0, OP.mult)
+        ts(("wf", 16, 32), ("kb", 16, 32), ("pf", 8, 9), OP.mult, 1.0, OP.add)
+        ts(("wf", 0, 16), ("wf", 0, 16), 1.0, OP.add, ("pf", 11, 12), OP.mult)
+        tt(("tw",), ("wf", 0, 16), ("wf", 16, 32), OP.mult)
+        ts(("w0",), ("w1", 0, L), ("pf", 11, 12), OP.mult)
         ts(("bh",), ("bo",), 0.5, OP.mult)
         ts(("bn",), ("bo",), -0.5, OP.mult)
+        ts(("bm",), ("bo",), -1.0, OP.mult)
+        ts(("b15",), ("bo",), ("pf", 8, 9), OP.mult, 2.0 ** -10, OP.mult)
+        ts(("b0",), ("bo",), ("pf", 9, 10), OP.mult)
+        ts(("d5",), ("idn",), ("pf", 6, 7), OP.mult)
         cp(("ib",), ("idn",))
         ts(("cb",), ("jf", 0, 16), 256.0, OP.mult, ("pf", 4, 5), OP.add)
         ts(("cb", 8, 16), ("cb", 8, 16), 1.0, OP.add)
+        ts(("ob",), ("jf", 0, 16), 16.0, OP.mult, ROW, OP.add)
+        fill(("z0",), 1024.0)
+        for c0, c1, _ in CUT:
+            ts(("z0", c0 // 8, c0 // 16 + c1 // 16), ("jf", c0 // 16, c1 // 16), 128.0, OP.mult, ("pf", 3, 4), OP.add)
         cp(("one",), ("w1", 0, 128))
         cp(("on",), ("w1", 0, L))
         ts(("jt",), ("jj", 0, 128), 15, OP.bitwise_and)
         ts(("l2",), ("jt",), ROW, OP.is_gt)
         tt(("lt",), ("l2",), ("bo",), OP.mult)
         ts(("thf",), ("thi",), 1.0, OP.add)
-        ts(("lim",), ("thf",), 16777216.0, OP.mult)
-        cp(("og",), ("g4", 0, GW, 8))
+        ts(("lim",), ("thf",), BIG, OP.mult)
+        own_columns()
+        cp(("wn", OG, OG + L), ("g4", 0, GW, 8), "a")
+        cp(("o0",), ("n4", 0, GW, 8))
+        cp(("r0",), ("n4", 0, GW, 8))
+
+    def own_columns():
+        cp(("o16",), ("g4", 0, GW, 8), "a")
 
     def turns():
         ts(("rt",), ("jr",), ("pf", 7, 8), OP.is_equal)
@@ -263,257 +305,253 @@ def rank_program(g, core, T, topo):
 
     def turn(n):
         s, lo = 1 + n // 4, 512 * (n % 4)
-        bank = ("pa", "pd1")[n % 2]
+        bank = ("pa", "pb")[n % 2]
         mm((bank,), ("rt", (s - 1) * 128, s * 128), ("g16", lo, lo + 512))
-        out = ("g4", s * GW + lo, s * GW + lo + 512)
-        if n in ROTA:
-            act(out, (bank,), AF.Copy)
-        else:
-            cp(out, (bank,))
+        cp(("g4", s * GW + lo, s * GW + lo + 512), (bank,), "a" if n in ROTA else "v")
 
     def turn_own():
-        cp(("o16",), ("og",))
         for s in range(1, 4):
-            bank = ("pa", "pd1")[s % 2]
+            bank = ("pa", "pb")[s % 2]
             mm((bank, 0, L), ("rt", (s - 1) * 128, s * 128), ("o16",))
-            if s == 2:
-                act(("g4", s * GW, (s + 1) * GW, 8), (bank, 0, L), AF.Copy)
-            else:
-                cp(("g4", s * GW, (s + 1) * GW, 8), (bank, 0, L))
-
-    def lst(tau, b, kind):
-        c0, c1 = CUT[b][0:2]
-        n = (c1 - c0) // 16
-        if tau % ST == 0:
-            lo = (0 if kind in (1, 3) else 16) + c0 // 16
-            return ("lc", lo, lo + n)
-        lo = 64 * tau + c0 // 4 + kind * n
-        return ("ln", lo, lo + n)
+            cp(("g4", s * GW, (s + 1) * GW, 8), (bank, 0, L), "av"[s % 2])
+        cp(("wn", OG, OG + L), ("o16",), "a")
 
     def run(tok, tau):
         gen, t = divmod(tau, ST)
         tok, _, js = tok.partition(".")
-        kind = tok.rstrip("0123456789") if tok[0] != "M" else tok[0:2]
+        eng = js[1:] or "a"
+        js = js[0:1]
+        kind = tok.rstrip("0123456789") if tok[0:2] not in ("M1", "M2") else tok[0:2]
         b = int(tok[len(kind):]) if tok[len(kind):] else 0
         c0, c1, subs = CUT[b]
         n = c1 - c0
         l0, l1 = c0 // 16, c1 // 16
         lc = l1 - l0
-        pe, pd, pn = "pe%d" % (b % 2), "pd%d" % (b % 2), "pl%d" % (b % 2)
-        gw = GW if t == 0 else 4 * GW
+        pe, pd, pn = "pe%d" % b, "pd%d" % b, "pl%d" % b
         e0 = c0 + sum(subs[0:int(js)]) if js else 0
         e1 = e0 + subs[int(js)] if js else 0
+        plain = js and (b, int(js)) in PLAIN
         q = 3 * c0
-        sco = (pd, 256 + c0, 256 + c1)
-        le, lr, ls = [(pn, 64 + k * lc, 64 + (k + 1) * lc) for k in range(3)]
-        hv = ("ho", 32 * tau + l0, 32 * tau + l1)
-        hf = ("ho", 32 * tau + 16 + l0, 32 * tau + 16 + l1)
-        li = [("li", c0 // 4 + k * lc, c0 // 4 + (k + 1) * lc) for k in range(4)]
+        sco = (pd, 256, 256 + n)
+        rp = (pn, 192, 192 + n)
+        le, lr, ls = [(pn, 400 + k * lc, 400 + (k + 1) * lc) for k in range(3)]
+        hist = "ho" if t in (1, 2, 3) else "hn"
+        xo = (hist, 32 * tau + l0, 32 * tau + l1)
+        nl = (hist, 32 * tau + 16 + l0, 32 * tau + 16 + l1)
+        lb = 5 * l0 + b * lc
+        li = [("li", lb + k * lc, lb + (k + 1) * lc) for k in range(4)]
+        ln = [("ln", LW * tau + r[1], LW * tau + r[2]) for r in li]
+        cs = 5 * l0 + (4 * lc if b == 0 else 0)
+        ww = ("ww" if t else "w0", c0, c1)
+        zz = "zz" if t else "z0"
         yi = ("yi", l0, l1)
-        ti = [("ti", 16 * k + l0, 16 * k + l1) for k in range(4)]
+        last = t == ST - 1
+        if kind in ("RR", "WW", "MK", "PZ") and t == 0:
+            return
         if kind == "RR":
-            cp(("rr", c0, c1), (("n4", 0, gw), lst(tau, b, 1)))
-        elif kind == "SB":
-            act(("sb", c0, c1), (("ts", 0, 16), lst(tau, b, 2)), AF.Copy)
-            mm(("pb", c0, c1), ("idn",), ("rr", c0, c1), True, False)
-            mm(("pb", c0, c1), ("idn",), ("sb", c0, c1), False, True)
-            mm(("pb", 256 + c0, 256 + c1), ("idn",), ("rr", c0, c1))
-            act(("m0", c0, c1), (("tm", 0, 16), lst(tau, b, 2)), AF.Copy)
-        elif kind == "OF":
-            cp(("of", c0, c1), ("pb", c0, c1))
-        elif kind == "NG":
-            tt(("ng", c0, c1), (("g4", 0, GW), lst(tau, b, 3)), ("m0", c0, c1), OP.mult)
-            for a in range(16):
-                mm((pn, 0, lc), ("ss", a * 128, a * 128 + 128), ("ng", c0 + a, c1, 16), a == 0, a == 15)
-        elif kind == "NL":
-            ts(("nl", l0, l1), (pn, 0, lc), 2048.0, OP.add)
-            act(("nf", l0, l1), (pn, 0, lc), AF.Copy)
+            cp(("rr", c0, c1), (("n4",), ln[0]))
         elif kind == "WW":
-            act(("ww", c0, c1), (("tw", 0, 16), lst(tau, b, 2)), AF.Copy)
-            ts(("zr", l0, l1), lst(tau, b, 1), 2048.0, OP.add)
-            cp(("zs", l0, l1), lst(tau, b, 0))
+            cp(ww, (("tw",), ln[2]), "a")
+        elif kind == "OF":
+            if t:
+                mm((pn, 0, n), ("idn",), ("rr", c0, c1), True, False)
+                mm((pn, 0, n), ("b15",), ww, False, True)
+                ts(("of", c0, c1), (pn, 0, n), -8192.0, OP.add)
+            mm(rp, ("idn",), ("rr" if t else "r0", c0, c1))
+        elif kind == "MK":
+            cp(("m0", c0, c1), (("tm",), ln[2]), "a")
+        elif kind == "NG":
+            if t:
+                tt(("ng", c0, c1), (("g4", 0, GW), ln[3]), ("m0", c0, c1), OP.mult)
+        elif kind == "NM":
+            for a in range(16):
+                mm((pn, 384, 384 + lc), onto(a) if t else move(0, a), ("ng" if t else "o16", c0 + a, c1, 16), a == 0, a == 15)
+        elif kind == "NL":
+            ts(nl, (pn, 384, 384 + lc), 2048.0, OP.add)
+        elif kind == "PZ":
+            ts(("zz", 2 * l0, 2 * l1), ("ln", ln[0][1], ln[1][2]), 1024.0, OP.add)
         elif kind == "E":
-            act(("eg", 16 * e0, 16 * e1), (("g4", 0, gw), ("of", e0, e1)), AF.Copy)
+            cp(("eg", 16 * e0, 16 * e1), (("g4", 0, 4 * GW if t else GW), ("of" if t else "o0", e0, e1)), eng)
+        elif kind == "F":
             for s in range(16):
-                mm((pe, e0, e1), ("se", s * 128, s * 128 + 128), ("eg", 16 * e0 + s, 16 * e1, 16), s == 0, s == 15)
+                mm((pe, e0 - c0, e1 - c0), move(s, s), ("eg", 16 * e0 + s, 16 * e1, 16), s == 0, s == 15)
         elif kind == "D":
             an, ao = ("an", L * tau) if t or tau == 0 else ("ao", L * (tau - 1))
-            tt(("dd", c0, c1), (("xr",), ("nl", l0, l1)), (an, ao + c0, ao + c1), OP.subtract)
+            tt(("dd", c0, c1), (XR, nl), (an, ao + c0, ao + c1), OP.subtract)
         elif kind == "DA":
-            act(("tt", c0, c1), ("dd", c0, c1), AF.Abs)
-        elif kind == "TR":
-            for s, w in enumerate(TRQ[b]):
-                o, tag = ("tr", 16 * c0 + s, 16 * c1, 16), ("tr%d" % s, c0, c1)
-                if w == "a":
-                    act(o, ("tt", c0, c1), AF.Copy, tag=tag)
-                elif w == "g":
-                    sel(o, ("tt", c0, c1), [[0, n]], OP.is_ge, 0, 0, tag=tag)
-                else:
-                    cp(o, ("tt", c0, c1), tag=tag)
+            act(("tr", 16 * c0, 16 * c1, 16), ("dd", c0, c1), AF.Abs, tag=("t0", c0, c1))
+        elif kind == "TA":
+            f0 = c0 + sum(m for j, m in enumerate(subs) if (b, j) in PLAIN)
+            cp(("tr", 16 * f0 + 8, 16 * c1, 16), ("tr", 16 * f0, 16 * c1, 16), tag=("t8", f0, c1), more=[("t0", f0, c1)])
+            cp(("tr", 16 * f0 + 4, 16 * c1, 8), ("tr", 16 * f0, 16 * c1, 8), tag=("t4", f0, c1), more=[("t0", f0, c1), ("t8", f0, c1)])
+        elif kind == "TB":
+            for s, w in enumerate(TBQ[e0 // 64]):
+                cp(("tr", 16 * e0 + s + 1, 16 * e1, 4), ("tr", 16 * e0, 16 * e1, 4), w, ("t%d" % (s + 1), e0, e1), [("t%d" % k, e0, e1) for k in (0, 4, 8)])
+        elif kind == "XL":
+            ts(("xl", e0, e1), (pe, e0 - c0, e1 - c0), 2048.0, OP.add)
         elif kind == "X":
-            ts(("xl", e0, e1), (pe, e0, e1), 2048.0, OP.add)
-            tt(("uu", 16 * e0, 16 * e1), (("xr",), ("xl", e0, e1)), ("tr", 16 * e0, 16 * e1), OP.add, more=[("tr%d" % s, e0, e1) for s in range(16)])
+            if plain:
+                cp(("uu", 16 * e0, 16 * e1), (XR, ("xl", e0, e1)), eng)
+            else:
+                tt(("uu", 16 * e0, 16 * e1), (XR, ("xl", e0, e1)), ("tr", 16 * e0, 16 * e1), OP.add, more=[("t%d" % k, e0, e1) for k in (0, 1, 2, 3, 4, 8)])
+        elif kind in ("PA", "PB"):
+            for s in range(8):
+                o = (kind.lower(), 64 * s, 64 * s + 64)
+                mm(o, ("idn",), ("uu", 16 * e0 + s + 8 * (kind == "PB"), 16 * e1, 16), True, False)
+                mm(o, ("ib",), ("tr", 16 * e0, 16 * e1, 16), False, True, [("t0", e0, e1)])
         elif kind == "AB":
-            act(("ab", 16 * e0, 16 * e1), ("uu", 16 * e0, 16 * e1), AF.Abs, bias=-255.0)
+            if plain:
+                for h in range(2):
+                    act(("ab", 16 * e0 + 512 * h, 16 * e0 + 512 * h + 512), (("pa", "pb")[h],), AF.Abs, bias=-255.0)
+            else:
+                act(("ab", 16 * e0, 16 * e1), ("uu", 16 * e0, 16 * e1), AF.Abs, bias=-255.0)
+        elif kind == "AM":
             for s in range(16):
-                mm((pd, e0, e1), ("ss", s * 128, s * 128 + 128), ("ab", 16 * e0 + s, 16 * e1, 16), s == 0, s == 15)
+                rhs = ("ab", 16 * e0 + 64 * s, 16 * e0 + 64 * s + 64) if plain else ("ab", 16 * e0 + s, 16 * e1, 16)
+                mm((pd, e0 - c0, e1 - c0), onto(s), rhs, s == 0, s == 15)
         elif kind == "GO":
-            act((pd, c0, c1), (pd, c0, c1), AF.Relu, bias=("lim",), scale=-16777216.0)
+            act((pd, 0, n), (pd, 0, n), AF.Relu, bias=("lim",), scale=-BIG)
         elif kind == "GV":
-            tt(("ok", c0, c1), (pd, c0, c1), ("ww", c0, c1), OP.min)
+            tt(("ok", c0, c1), (pd, 0, n), ww, OP.min)
             mm(sco, ("bh",), ("ok", c0, c1))
         elif kind == "PK":
             tt(("ff", c0, c1), ("ok", c0, c1), sco, OP.is_gt)
-            tt(("qq", q, q + n), ("ff", c0, c1), (pe, c0, c1), OP.mult)
-            tt(("qq", q + n, q + 2 * n), ("ff", c0, c1), ("pb", 256 + c0, 256 + c1), OP.mult)
             act(("qq", q + 2 * n, q + 3 * n), ("ff", c0, c1), AF.Copy, scale=("pf", 5, 6))
+            tt(("qq", q, q + n), ("ff", c0, c1), (pe, 0, n), OP.mult)
+            tt(("qq", q + n, q + 2 * n), ("ff", c0, c1), rp, OP.mult)
         elif kind == "PC":
             for a in range(16):
-                mm((pn, 64, 64 + 3 * lc), ("ss", a * 128, a * 128 + 128), ("qq", q + a, q + 3 * n, 16), a == 0, a == 15)
+                mm((pn, 400, 400 + 3 * lc), onto(a), ("qq", q + a, q + 3 * n, 16), a == 0, a == 15)
         elif kind == "YY":
-            if t == ST - 1:
-                act(("nb2", c0, c1), sco, AF.Relu, bias=1.0, scale=-1.0)
-            if YYA[b]:
-                mm((pn, 384, 384 + n), ("ib",), ("tt", c0, c1), True, False)
-                mm((pn, 384, 384 + n), ("bn",), ("ok", c0, c1), False, True)
-                act(("yy", c0, c1), (pn, 384, 384 + n), AF.Relu)
-            else:
-                tt(("yy", c0, c1), ("tt", c0, c1), sco, OP.subtract)
+            mm((pd, 0, n), ("ib",), ("tr", 16 * c0, 16 * c1, 16), True, False, [("t0", c0, c1)])
+            mm((pd, 0, n), ("bn",), ("ok", c0, c1), False, True)
+            act(("yy", c0, c1), (pd, 0, n), AF.Relu)
         elif kind == "M1":
-            if HFA[b]:
-                act(hf, ls, AF.Relu, bias=1.0, scale=-1.0)
-            else:
-                ts(hf, ls, 0.0, OP.is_equal)
-            ts(("xo", l0, l1), le, 2048.0, OP.add)
-            tt(ti[0], ls, ("zs", l0, l1), OP.add)
-            tt(ti[1], hf, ("zr", l0, l1), OP.mult)
-            tt(ti[2], lr, ti[1], OP.add)
-            tt(yi, ti[0], ti[2], OP.add)
-            ts(li[2], yi, 11, OP.arith_shift_right, 15, OP.bitwise_and)
+            tt(("ti", l0, l1), ls, (zz, 2 * l0, 2 * l0 + lc), OP.max)
+            tt(("ti", 16 + l0, 16 + l1), lr, (zz, 2 * l0 + lc, 2 * l1), OP.add)
+            tt(yi, ("ti", l0, l1), ("ti", 16 + l0, 16 + l1), OP.add)
         elif kind == "ML":
-            if t < ST - 1:
-                for k, m in ((1, 8191), (3, 2047), (0, 24576)):
+            o = LW * tau
+            ts(li[2], yi, 11, OP.arith_shift_right, 15, OP.bitwise_and)
+            if not last:
+                for k, m in ((0, 8191), (3, 2047), (1, 24576)):
                     ts(li[k], yi, m, OP.bitwise_and)
-                o = 64 * tau + c0 // 4
-                cp(("lo", o, o + 4 * lc), ("li", c0 // 4, c0 // 4 + 4 * lc))
-                send(nxt, "lo", o, o + 4 * lc, "ln", o + 64, "li%d_%d" % (tau, b))
+            tt(("li", cs, cs + lc), li[2], ("cb", l0, l1), OP.add)
+            if last:
+                cp(("lo", o + cs, o + cs + lc), ("li", cs, cs + lc))
+            else:
+                cp(("lo", o + 5 * l0, o + 5 * l1), ("li", 5 * l0, 5 * l1))
+                send(nxt, "lo", o + lb, o + lb + 4 * lc, "ln", o + LW + lb, "li%d_%d" % (tau, b))
+        elif kind == "XO":
+            ts(xo, le, 2048.0, OP.add)
         elif kind == "M2":
             ao = L * tau
-            tt(("ao", ao + c0, ao + c1), (("xr",), ("xo", l0, l1)), ("yy", c0, c1), OP.max)
-            if t < ST - 1:
+            tt(("ao", ao + c0, ao + c1), (XR, xo), ("yy", c0, c1), OP.max)
+            if not last:
                 send(nxt, "ao", ao + c0, ao + c1, "an", ao + L + c0, "ar%d_%d" % (tau, b))
-        elif kind == "MC":
-            tt(("ci", l0, l1), li[2], ("cb", l0, l1), OP.add)
-            cp(("cs", l0, l1), ("ci", l0, l1))
-        elif kind == "M3":
-            tt(ti[3], hf, ("nf", l0, l1), OP.mult)
-            tt(hv, le, ti[3], OP.add)
         elif kind == "ST":
-            cp((("xr",), ("cs",)), ("ao", L * tau, L * tau + L))
+            o = LW * tau + CUT[0][1] // 4
+            cp((XR, ("lo", o, o + 16)), ("ao", L * tau, L * tau + L))
+            if tau == TAU - 1:
+                registers_and_sums()
         elif kind == "HI":
             if t in (1, 2, 3):
                 send(T.cores[(rank - t) % N], "ho", 32 * tau, 32 * tau + 32, "hn", 32 * tau, "h%d" % tau)
         elif kind == "CO":
             if tau < TAU - 1:
-                mm(("pa", 256, 272), ("one",), ("ho", 32 * tau + 16, 32 * tau + 32))
-                op("v", lambda v: v.tensor_reduce(T.af[:], T.pa[:, 256:272], AxisListType.X, OP.add), [R("pa")], [R("af")])
+                ts(("hc",), (hist, 32 * tau, 32 * tau + 16), float(ZC), OP.is_equal)
+                mm(("pa", 256, 272), ("one",), ("hc",))
+                total(("af",), ("pa", 256, 272))
                 cp(("ai", 0, 1), ("af",))
                 ts(("ai", 1, 2), ("ai", 0, 1), 63, OP.bitwise_and)
-                ts(("lim",), ("ai", 1, 2), ("thf",), OP.add, 16777216.0, OP.mult)
-        elif kind == "EE" and t == ST - 1:
-            early_end(gen)
-
-    def plane(gen, t):
-        return "hn" if t in (1, 2, 3) else "ho", 32 * (ST * gen + t)
-
-    def spread(p0, p1):
-        for a in range(16):
-            ts(("ed", p0 * L + a, p1 * L, 16), ("hl", p0 * 16, p1 * 16), ("u16", a, a + 1), OP.mult, tag=("ed%d" % a, p0 * L, p1 * L))
-        need("p", [("ed%d" % a, p0 * L, p1 * L) for a in range(16)], [])
-
-    def early_end(gen):
-        for t in range(4):
-            b, o = plane(gen, t)
-            cp(("hl", 16 * t, 16 * t + 16), (b, o, o + 16))
-            if t == 0:
-                cp(("er",), (b, o + 16, o + 32))
-            else:
-                tt(("er",), ("er",), (b, o + 16, o + 32), OP.add)
-        cp(("hl", 64, 80), ("er",))
-        spread(0, 5)
-        mm(("pa", 0, L), ("bo",), ("ed", 4 * L, 5 * L))
-        act(("eb",), ("pa", 0, L), AF.Copy)
-        ts(("gm",), ("og",), ("pf", 6, 7), OP.mult)
+                ts(("lim",), ("ai", 1, 2), ("thf",), OP.add, BIG, OP.mult)
+        elif not last:
+            return
+        elif kind == "EE":
+            o = 32 * ST * gen
+            ts(("hv",), ("hn", o, o + 128), -2048.0, OP.add)
+            ts(("hf",), ("hv",), 0.0, OP.is_equal)
+            tt(("hm", 0, 112), ("hf", 0, 112), ("hv", 16, 128), OP.mult)
+            tt(("e1",), ("hf", 0, 48), ("hf", 64, 112), OP.add)
+            tt(("hw", 0, 112), ("hv", 0, 112), ("hm", 0, 112), OP.add)
+            tt(("er",), ("e1", 0, 16), ("e1", 32, 48), OP.add)
+            mm(("pa", 0, L), ("b0",), ("on",), True, False)
+            for a in range(16):
+                mm(("pa", a, L, 16), move(a, 0), ("er",), False, a == 15)
+            cp(("eb",), ("pa", 0, L), "a")
+            mm(("pb", 0, L), ("d5",), ("o16",), True, False)
+            for s in range(4):
+                for a in range(16):
+                    mm(("pb", a, L, 16), move(a, s), ("hw", 32 * s, 32 * s + 16), False, False)
+        elif kind == "FL":
+            fl = (pe, 256, 256 + n)
+            mm(fl, ("b0",), ("on", c0, c1), True, False)
+            mm(fl, ("bm",), ("ff", c0, c1), False, True)
+            tt(("nf", c0, c1), ("ng", c0, c1), fl, OP.mult)
+        elif kind == "SA":
+            mm(("pa", 0, L), ("b0",), ("eb",), True, False)
+            mm(("pa", 0, L), ("bm",), ("ff",), False, True)
+            for c0, c1, _ in CUT:
+                mm(("pb", c0, c1), onto(4), ("qq", 3 * c0, 2 * c0 + c1), False, False)
+            mm(("pb", 0, L), onto(4), ("nf",), False, True)
+            ts(("ind",), ("pa", 0, L), ROW, OP.is_equal)
+            cp(("da",), ("pb", 0, L), "a")
+            scan(("pre",), ("on",), ("ind",), 0.0)
+            mm(("pa", 300, 301), ("lt",), ("pre", L - 1, L))
+            ts(("x1",), ("pre",), ("pa", 300, 301), OP.add, -1.0, OP.add)
+            tt(("x2",), ("x1",), ("ind",), OP.mult)
+            for a in range(16):
+                mm(("pa", 320, 336), onto(a), ("x2", a, L, 16), a == 0, a == 15)
+        elif kind == "SB":
+            cp(("pl",), ("pa", 320, 336))
+            cp((("wn", SR, SR + L), ("pl",)), ("da",))
+            send(nxt, "wn", SR, SR + K, "wn", BI[gen], "b%d" % gen)
+        elif kind == "SC":
+            w = min(SR, BI[gen])
+            ts(("kr", 0, 16), ("pa", 320, 336), -1.0, OP.mult, 255.0, OP.add)
+            ts(("kr", 16, 32), ("kr", 0, 16), 1, OP.bitwise_and)
+            ts(("kf", 0, 16), ("kr", 0, 16), float(K), OP.is_ge, 4096.0, OP.mult)
+            ts(("kf", 16, 32), ("kr", 16, 32), float(BI[gen] - SR), OP.mult, float(SR - OG), OP.add)
+            tt(("kf", 32, 48), ("kf", 0, 16), ("kr", 0, 16), OP.add)
+            tt(("kf", 48, 64), ("kf", 32, 48), ("kf", 16, 32), OP.add)
+            tt(("kf", 0, 16), ("kf", 48, 64), ("ob",), OP.min)
+            ts(("pr",), ("kf", 0, 16), float(OG - w), OP.add)
 
     def registers_and_sums():
-        cp(("fo", L, 2 * L), ("ao", L * (TAU - 1), L * TAU))
+        cp(("fo", L, 2 * L), ("ao", L * (TAU - 1), L * TAU), "a")
         dma([(T.ya[:], T.fo[:, L:2 * L])], [R("fo", L, 2 * L)], None, True)
         for h in range(2):
             o = h * (ZC + 1)
             for s in range(16):
                 mm(("pe0", 128 * h, 128 * h + 128), ("ib",), ("xr", o + s, o + ZC, 16), s == 0, s == 15)
-        cp(("fo", 2 * L, 3 * L), ("pe0", 0, L))
+        cp(("fo", 2 * L, 3 * L), ("pe0", 0, L), "a")
         dma([(T.ys[:], T.fo[:, 2 * L:3 * L])], [R("fo", 2 * L, 3 * L)], None, True)
-
-    def end(gen):
-        b, o = plane(gen, 4)
-        tt(("et",), ("eb",), ("nb2",), OP.add)
-        ts(("ind",), ("et",), ROW, OP.is_equal)
-        op("v", lambda v: v.tensor_tensor_scan(T.pre[:], T.on[:], T.ind[:], 0.0, OP.mult, OP.add), [R("on"), R("ind")], [R("pre")])
-        mm(("pa", 300, 301), ("lt",), ("pre", L - 1, L))
-        cp(("hl", 64, 80), (b, o, o + 16))
-        ts(("x1",), ("pre",), ("pa", 300, 301), OP.add, -1.0, OP.add)
-        tt(("x2",), ("x1",), ("ind",), OP.mult)
-        for a in range(16):
-            mm(("pa", 320, 336), ("ss", a * 128, a * 128 + 128), ("x2", a, L, 16), a == 0, a == 15)
-        spread(4, 5)
-        for t in range(5):
-            mm(("pb", 0, L), ("ss", t * 128, t * 128 + 128), ("ed", t * L, (t + 1) * L), t == 0, t == 4)
-        tt(("da",), ("pb", 0, L), ("gm",), OP.add)
-        cp(("pl",), ("pa", 320, 336))
-        cp((("sr",), ("pl",)), ("da",))
-        ob = K * gen
-        send(nxt, "sr", 0, K, "bi", ob, "b%d" % gen)
-        ts(("pr",), ("pa", 320, 336), -1.0, OP.mult, 255.0, OP.add)
-        cp((("rv",), ("pr",)), ("og",))
-        cp(("rv", 0, K, 2), ("sr", 0, K, 2))
-        if gen == GENS - 1:
-            registers_and_sums()
-        cp(("rv", 1, K, 2), ("bi", ob + 1, ob + K, 2))
-        cp(("og",), (("rv",), ("pr",)))
 
     for tau in range(TAU):
         gen, t = divmod(tau, ST)
-        if tau == 0:
-            for tok in FIRST:
-                if tok[0] == "Q":
-                    turn(int(tok[1:]))
-                elif tok == "RT":
-                    turns()
-                elif tok == "LC":
-                    constants()
-                elif tok == "GC":
-                    act(("g16",), ("g4", 0, GW), AF.Copy)
-                else:
-                    run(tok.rstrip("'"), 1 if tok[-1] == "'" else 0)
-            continue
-        if t == 0:
-            for tok in ORDER:
-                if tok[-1] == "'":
-                    run(tok[0:-1], tau)
-            turn_own()
-        for tok in ORDER:
-            if tok[-1] != "'":
+        for tok in (ORDER if t else AGAIN if tau else FIRST):
+            if tok[0] == "Q":
+                turn(int(tok[1:]))
+            elif tok == "RT":
+                turns()
+            elif tok == "LC":
+                constants()
+            elif tok == "GC":
+                cp(("g16",), ("g4", 0, GW), "a")
+            elif tok == "OW":
+                own_columns()
+            elif tok == "OT":
+                turn_own()
+            elif tok[-1] != "'":
                 run(tok, tau)
             elif t < ST - 1:
                 run(tok[0:-1], tau + 1)
         if t == ST - 1:
-            end(gen)
-            if gen < GENS - 1:
-                cp(("g4", 0, GW, 8), ("og",))
+            new = (("wn", min(SR, BI[gen]), OG + L), ("pr",))
+            cp(("g4", 0, GW, 8) if gen < GENS - 1 else ("da",), new)
 
-    ts(("fo", 0, L), ("og",), 0.0, OP.is_le, 2047.0, OP.add)
-    tt(("fo", 0, L), ("fo", 0, L), ("og",), OP.add)
+    ts(("fo", 0, L), ("da",), 0.0, OP.is_le, 2047.0, OP.add)
+    tt(("fo", 0, L), ("fo", 0, L), ("da",), OP.add)
     dma([(T.yg[:], T.fo[:, 0:L])], [R("fo", 0, L)], None, True)
     for i in range(nd[0]):
         if known["s"].get("d%d" % i, 0) < 16:

@@ -9,8 +9,10 @@ BIG = 2.0 ** 40
 TAU = GENS * ST
 CUT = [(0, 128, (64, 64)), (128, 256, (64, 64))]
 PLAIN = ((0, 0),)
+MOST = ((1, 1),)
 NCH = len(CUT)
-DMAS = 26
+DMAS = 44
+DROT = (1, 3, 2)
 LW = 80
 SR, BI, OG = 64, (320, 0), 384
 ORDER = """D0 DA0 RR1 WW1 TA0 OF1 TB0.0 MK1 NG1 TB0.1 X0.0 E1.0 NL1 D1 DA1 X0.1 E1.1 TA1 TB1.0 TB1.1 AB0.0 AB0.1 PZ0 PZ1 X1.0 GO0 GV0 PK0 YY0 PC0 X1.1
@@ -26,6 +28,21 @@ AGAIN = """E1.0v OW E0.0 NM0 NL0 NM1 D0 DA0 F0.0 F1.0 NL1 D1 E0.1 TA0 OF0 XL0.0 
 FIRST = """LC NM1 E0.0v NL1 F0.0 GC E1.1 NM0 NL0 E1.0v D0 OF0 F1.1 E0.1 DA0 XL0.0 TA0 TB0.1 X0.0 OF1 F0.1 D1 RT PA0.0 PB0.0 F1.0 AB0.0 DA1 AM0.0 TA1 XL0.1 X0.1 TB1.1 AB0.1 TB1.0 XL1.1 AM0.1 GO0 X1.1 Q0 XL1.0 X1.0 Q1 Q3 Q2 GV0 PK0 PC0 Q5 M10 AB1.1 AM1.1 Q7 Q9 Q4 AB1.0 Q11 AM1.0 ML0 GO1 Q6 GV1 PK1 MK0' WW0' XO0 NG0' YY0 PC1 YY1 Q8 M11 M20 XO1 NM0' Q10 ML1 CO M21 NL0' ST RR0' OF0' E0.0v' F0.0' E0.1' XL0.0' F0.1'""".split()
 ROTA = (1, 2, 4, 7, 8, 10, 11)
 TBQ = ('gga', 'ggv', 'gvv', 'gvg')
+AGAIN = """OW NM0 E0.0 E1.0v NL0 NM1 D0 DA0 F0.0 NL1 E0.1 RP1 D1 DA1 TA0 XL0.0 F1.0 X0.0v F0.1 PA0.0 E1.1 TB0.1 PB0.0 XL0.1 TA1 XL1.0 X0.1 RP0 AB0.0 F1.1 AB0.1 TB1.0 AM0.0 X1.0 TB1.1 AB1.0 XL1.1 AM0.1 GO0v GV0 GM0 PF0 PW0 PQ0 YM0 X1.1 PC0 AM1.0 M10 XO0 ML0 AB1.1 OT YY0v AM1.1 GO1 GV1 GM1 PF1 PW1 PQ1 YM1 WW0' MK0' PC1 M20 RR0' YY1 OM0' XO1 OF0' M11 CA E0.0' NG0' NM0' CB ML1 E0.1' M21 ST CC CD F0.0' RP0' XL0.0' NL0' F0.1' CE""".split()
+FIRST = """LC E0.0v E1.1 NM0 F0.0 F1.1 NM1 E0.1 F0.1 NL0 XL0.0 E1.0 NL1 GC X0.0v D1 DA1 D0 DA0 TA1 TA0 RP0 XL1.1 F1.0 TB0.1 PB0.0 RT XL0.1 X0.1 PA0.0 TB1.0 AB0.0 XL1.0 TB1.1 Q0 AB0.1 X1.1 AM0.0 AM0.1 X1.0 GO0 GV0 Q2 RP1 Q1 Q3 GM0 AB1.1 PF0 PQ0 YM0 PW0v PC0 M10 ML0 YY0v AB1.0 Q5 AM1.1 AM1.0 GO1v Q4 GV1 GM1 PF1 Q7 YM1 PQ1 PW1v Q9 XO0 PC1 Q6 MK0v' M11 Q8 WW0v' NG0' Q10 ML1 M20 YY1 XO1 NM0' CA Q11 M21 CB NL0' CC CD ST RR0' OM0' OF0' RP0' E0.1' CE E0.0v' F0.0' XL0.0' F0.1'""".split()
+ORDER = """MK1 D0 RR1 NG1 PZ0 DA0 WW1 TA0 TB0.1 XL0.1 NM1 X0.0 NL1 OM1 D1 PA0.0 OF1 X0.1 DA1 TA1 E1.0 PB0.0 AB0.0 F1.0 AB0.1 E1.1v RP1 XL1.0 AM0.0 TB1.0 AM0.1 EE GO0 X1.0 F1.1 TB1.1 EF GV0 XL1.1 GM0 PF0 PW0 AB1.0 PQ0 EG X1.1 YM0 PC0 FL0 AB1.1 EH AM1.0 M10 AM1.1 ML0 GO1 YY0 GV1 XO0 EI GM1 PZ1 WW0' PF1 EJ PW1 RR0' PQ1 MK0' OM0' OF0' FL1 YM1 M20 NG0' SA SD PC1 SE SF YY1 NM0' M11 XO1 E0.0' ML1 HI CA M21 SB ST F0.0' CB E0.1' CC XL0.0' SC RP0' CD NL0' F0.1' CE""".split()
+TBQ = ('aaa', 'vvg', 'vgg', 'gaa')
+MOST = ()
+LAST = """MK1 D0 RR1 NG1 PZ0 DA0 WW1 TA0 TB0.1 XL0.1 NM1 X0.0 NL1 OM1 D1 PA0.0 OF1 X0.1 DA1 TA1 E1.0 PB0.0 AB0.0 F1.0 AB0.1 E1.1v RP1 XL1.0 AM0.0 TB1.0 AM0.1 EE EK GO0 X1.0 F1.1 TB1.1 EF GV0 XL1.1 GM0 PF0 PW0 AB1.0 PQ0 EG X1.1 YM0 PC0 FL0 AB1.1 EH EI EJ AM1.0 M10 AM1.1 ML0 GO1 YY0 GV1 XO0 GM1 PZ1 PF1 PW1 PQ1 FL1 YM1 M20 SA SG SD PC1 SE SF YY1 M11 XO1 ML1 CA M21 SB ST RS CB CC SC CD CE""".split()
+ORDER = [_t for _t in ORDER if _t[0:2] not in ("EE", "EF", "EG", "EH", "EI", "EJ", "FL", "SA", "SB", "SC", "SD", "SE", "SF")]
+FIRST = """L0 G0 L1 G1 L2 G2 G3 RA OW O0 E0.0v E0.1 L4 L5 NM0 F0.0 O1 R0 R1 NM1 F0.1 NL0 XL0.0 E1.0 E1.1v NL1 RB X0.0 D0 D1 DA0 DA1 F1.0 F1.1 TA0 TA1 RP0 TB0.1 PA0.0 PB0.0 XL0.1 X0.1 TB1.0 AB0.0 XL1.0 XL1.1 TB1.1 AB0.1 X1.0 AM0.0 AM0.1 L3 GO0 GV0 RP1 GM0 PF0 PQ0 YM0 PW0 PC0 X1.1 M10 ML0 YY0 AB1.0 AM1.0 AB1.1 AM1.1 L6 L7 RT GO1 GV1 GM1 PF1 YM1 PQ1 PW1 XO0 PC1 MK0' M11 WW0' NG0' ML1 M20 YY1 XO1 NM0' CA M21 CB NL0' CC CD ST RR0' OM0' OF0' RP0' E0.1' CE E0.0v' F0.0' XL0.0' F0.1'""".split()
+FIRST = """G0 G1 G2 G3 RA RB L0 O0 L2 OW RT NM0 R0 NM1 NL1 E0.1 L1 NL0 O1 F0.1 E1.0v E0.0 D0 GC F0.0 D1 XL0.0 F1.0 E1.1 DA0 L3 DA1 F1.1 XL0.1 X0.0 TA0 PA0.0 PB0.0 RP0 TA1 TB0.1 XL1.0 TB1.1 XL1.1 AB0.0 X0.1 TB1.0 X1.1 X1.0 AM0.0 AB0.1 AM0.1 AB1.1 GO0 GV0 Q5 GM0 PF0 PW0 PQ0 AB1.0 AM1.1 R1 L7 PC0 Q4 RP1 AM1.0 GO1 YM0 Q7 Q6 M10 ML0 GV1 XO0 GM1 Q9 PF1 PQ1 PW1v YY0v PC1 Q8 Q11 YM1 XO1 Q10 M11 L6 L4 CA WW0' ML1 CB RR0' CC OM0' OF0' MK0' CD M20 YY1 M21 NG0' E0.0' NM0' CE L5 ST RP0' F0.0' NL0' XL0.0' E0.1' F0.1'""".split()
+ROTA = (4, 5, 6, 7, 8, 9, 10, 11)
+AGAIN = """OW E0.0 NM0 E1.0v NL0 NM1 NL1 D1 D0 E0.1 F0.0 XL0.0 RP0 F0.1 X0.0v DA0 PA0.0 TA0 DA1 PB0.0 XL0.1 E1.1 AB0.0 F1.1 TB0.1 TA1 X0.1 F1.0 AM0.0 TB1.0 XL1.0 AB0.1 AM0.1 TB1.1 RP1 XL1.1 GO0 X1.0 GV0 GM0 AB1.0 PF0 PW0 PQ0 X1.1 PC0 M10 ML0 AM1.0 YM0 AB1.1 OT AM1.1 GO1v XO0 MK0' GV1 WW0' RR0' GM1 PF1 OM0' PQ1 YM1 OF0' PW1 YY0 PC1 M20 NG0' E0.0' YY1v M11 NM0' XO1 ML1 CA E0.1' M21 F0.0' RP0' CB CC ST CD NL0' CE XL0.0' F0.1'""".split()
+LAST = """D0 RR1 MK1v WW1v RP1 NG1 DA0 OM1 X0.0 OF1 XL0.1 NM1 TA0 TB0.1 NL1 PA0.0 PZ0 PB0.0 E1.0 D1 F1.0 X0.1 DA1 AB0.0 AB0.1 TA1 EE AM0.0 XL1.0 TB1.0 EK E1.1 EF X1.0 AM0.1 GO0v F1.1 TB1.1 GV0 EG GM0 XL1.1 YM0 X1.1 AB1.0 PF0 PW0 PQ0 EH AB1.1 AM1.0 PC0 YY0v XO0 FL0 AM1.1 M10 ML0 EI GO1v GV1 M20 GM1 PF1 EJ PQ1 FL1 PZ1 PW1 SA SD SG PC1 YM1 YY1 SE SF XO1 M11 M21 ML1 SB ST CA CB CC SC CD CE RS""".split()
+ORDER = """D0 RR1 MK1 PZ0 DA0 NG1 TA0 WW1v NM1 TB0.1 NL1 OM1 XL0.1 X0.0 D1 OF1 PB0.0 DA1 PA0.0 E1.0 X0.1 AB0.0 TA1 AB0.1 E1.1v F1.0 AM0.0 TB1.0 TB1.1 XL1.0 AM0.1 F1.1 X1.0 GO0 GV0 XL1.1 GM0 PF0 PW0 PQ0 X1.1 AB1.0 YM0 RP1 AB1.1 PC0 M10 ML0 AM1.0 YY0v AM1.1 XO0 GO1v WW0' GV1 GM1 PZ1 PF1 PW1 YM1 RR0' MK0' OM0' PQ1 PC1 OF0' E0.0' YY1v M20 NG0' M11 XO1 HI RP0' NM0' ML1 CA M21 F0.0' CB ST E0.1' CC XL0.0' CD F0.1' NL0' CE""".split()
+TBQ = ('gva', 'vgv', 'ggv', 'ggg')
+DROT = (1,)
 
 SCRATCH = {}
 for _n, _w, _d in (
@@ -43,7 +60,7 @@ for _n, _w, _d in (
         ("af", 1, "float32"), ("ai", 2, "int32"), ("lim", 1, "float32"), ("thi", 1, "int32"), ("thf", 1, "float32"),
         ("jj", L, "int32"), ("jf", L, "float32"), ("jt", 128, "int32"), ("kb", 32, "int32"), ("wf", 64, "float32"),
         ("pi", 4, "int32"), ("pf", 16, "float32"), ("u16", 16, "float32"), ("tw", 16, "bfloat16"), ("tm", 16, "bfloat16"),
-        ("se", 2048 + 32, "float16"), ("sz", 144, "float16"), ("idn", 128, "float16"), ("ib", 128, "bfloat16"), ("bo", 128, "float16"), ("bm", 128, "float16"),
+        ("se", 2048 + 32, "float16"), ("sz", 432, "float16"), ("idn", 128, "float16"), ("ib", 128, "bfloat16"), ("bo", 128, "float16"), ("bm", 128, "float16"),
         ("bh", 128, "bfloat16"), ("bn", 128, "bfloat16"), ("b15", 128, "bfloat16"), ("b0", 128, "float16"), ("d5", 128, "float16"),
         ("lt", 128, "float16"), ("l2", 128, "float16"), ("one", 128, "float16"), ("rt", 384, "float16"), ("r2", 384, "float16"), ("jr", 384, "int32"),
         ("fo", 3 * L, "float32")):
@@ -79,7 +96,7 @@ def rank_program(g, core, T, topo):
             for name, lo, hi in rs:
                 ps = name in PSUM
                 for l, h, q2, (s, n) in lists.get(name, ()):
-                    if (q2 != q if ps else (l < hi and lo < h)) and n > known[q].get(s, 0) and n > best.get(s, 0):
+                    if ((ps and q2 != q) or (l < hi and lo < h and q2 + q != "pp")) and n > known[q].get(s, 0) and n > best.get(s, 0):
                         best[s] = n
         look(wr, reads + writes)
         look(rd, writes + [r for r in reads if r[0] in PSUM])
@@ -120,6 +137,7 @@ def rank_program(g, core, T, topo):
         for s, tok in toks:
             if len(pairs) > 1:
                 wr[reg[0]] = list(wr.get(reg[0], ())) + [reg[1:3] + (s, tok)]
+                note(s, reads, [], tok)
             else:
                 note(s, reads, [] if out else [reg], tok)
 
@@ -202,8 +220,8 @@ def rank_program(g, core, T, topo):
         b, ib = side(rhs)
         op("p", lambda t: t.matmul(o, a, b, start, stop), ia + ib + list(more), io)
 
-    def onto(a):
-        return ("sz", 15 - a, 143 - a)
+    def onto(a, k=0):
+        return ("sz", 144 * k + 15 - a, 144 * k + 143 - a)
 
     def move(a, b):
         return ("se", 16 + 129 * a - b, 144 + 129 * a - b)
@@ -211,23 +229,35 @@ def rank_program(g, core, T, topo):
     nxt = T.cores[(rank + 1) % N]
     XR = ("xr", 0, XW + 1)
 
-    H = GW // 2
-    for lo in (0, H):
+    H = GW // 4
+    fill(("w1",), 1.0)
+    fill(("xr", ZC, ZC + 8), 0.0)
+    for lo in range(0, GW, H):
         dma([(T.gi[:, lo:lo + H], T.gn[:, lo:lo + H])], [], R("gi", lo, lo + H))
-    dma([(T.n4[:, 0:GW], T.nb[:])], [], R("n4", 0, GW))
-    dma([(T.thi[:], T.th[:])], [], R("thi"))
+    h = 8 * CUT[0][1]
+    dma([(T.n4[:, 0:h], T.nb[:, 0:h])], [], R("n4", 0, h))
     dma([(T.an[:, 0:L], T.a0[:])], [], R("an", 0, L))
     dma([(T.xr[:, 0:ZC], T.x[:, 0:ZC])], [], R("xr", 0, ZC))
+    dma([(T.n4[:, h:GW], T.nb[:, h:GW])], [], R("n4", h, GW))
+    dma([(T.xr[:, ZC + 1:XW + 1], T.x[:, ZC:XW])], [], R("xr", ZC, XW + 1))
+    dma([(T.thi[:], T.th[:])], [], R("thi"))
     iota(("pi", 0, 1), [[0, 1]], 0, 1)
     iota(("jj",), [[1, L]], 0, 0)
-    fill(("xr", ZC, ZC + 8), 0.0)
-    fill(("w1",), 1.0)
-    dma([(T.xr[:, ZC + 1:XW + 1], T.x[:, ZC:XW])], [], R("xr", ZC, XW + 1))
     for k in range(1, 4):
-        reg = R("n4", k * GW, (k + 1) * GW)
-        dma([(T.n4[k:128, reg[1]:reg[2]], T.nb[0:128 - k, :])], [], reg)
-        rows = [(T.n4[u::16, reg[1]:reg[2]], T.nb[16 - k + u::16, :]) for u in range(k)]
-        dma(rows, [], reg)
+        dma([(T.n4[k:128, k * GW:(k + 1) * GW], T.nb[0:128 - k, :])], [], R("n4", k * GW, (k + 1) * GW))
+
+    def turn_all():
+        for s in DROT:
+            d = (4 * s + 7) % 16 - 7
+            dma([(T.g4[max(0, -d):128 - max(0, d), s * GW:(s + 1) * GW], T.g4[max(0, d):128 - max(0, -d), 0:GW])], [R("g4", 0, GW)], R("g4", s * GW, (s + 1) * GW))
+
+    def turn_rest():
+        for k in range(1, 4):
+            dma([(T.n4[u::16, k * GW:(k + 1) * GW], T.nb[16 - k + u::16, :]) for u in range(k)], [], R("n4", k * GW, (k + 1) * GW))
+        for s in DROT:
+            d = (4 * s + 7) % 16 - 7
+            rows = [(T.g4[u::16, s * GW:(s + 1) * GW], T.g4[(u + d) % 16::16, 0:GW]) for u in range(16) if not 0 <= u + d < 16]
+            dma(rows, [R("g4", 0, GW)], R("g4", s * GW, (s + 1) * GW))
     op("g", lambda q: q.affine_select(T.se[:, 16:2064], T.w1[:], [[-1024, 16], [16, 8], [1025, 16]], OP.is_equal, 0.0, 0, -1), [R("w1")], [R("se", 16, 2064)])
     iota(("jr",), [[4, 3], [32, 8], [1, 16]], 4, 0)
     ts(("pi", 1, 2), ("pi", 0, 1), 15, OP.bitwise_and)
@@ -238,62 +268,71 @@ def rank_program(g, core, T, topo):
     ts(("idn",), ("jf", 0, 128), ("pf", 0, 1), OP.is_equal)
     ts(("jt",), ("jj", 0, 128), 4, OP.arith_shift_right)
     ts(("bo",), ("jt",), GRP, OP.is_equal)
-    ts(("sz",), ("w1", 0, 144), 0.0, OP.mult)
-    cp(("sz", 15, 128, 16), ("bo", 0, 128, 16))
+    ts(("sz",), ("w1", 0, 432), 0.0, OP.mult)
+    for k, c in enumerate((1.0, -1.0, 2.0)):
+        ts(("sz", 144 * k + 15, 144 * k + 128, 16), ("bo", 0, 128, 16), c, OP.mult)
     for lo in (0, 2064):
         ts(("se", lo, lo + 16), ("w1", 0, 16), 0.0, OP.mult)
-    for lo in (0, H):
-        ts(("g4", lo, lo + H), ("gi", lo, lo + H), 1.0 + 2.0 ** -12, OP.mult, MAGIC, OP.add)
-        act(("g4", lo, lo + H), ("g4", lo, lo + H), AF.Copy, bias=-(MAGIC + 2048.0))
-        if lo == 0:
-            ts(("u16",), ("jf", 0, 16), ROW, OP.is_equal)
-            cp(("tm",), ("u16",))
-            ts(("pf", 3, 4), ROW, 8.0, OP.mult, 1024.0, OP.add)
-            ts(("pf", 4, 5), ROW, 16.0, OP.mult)
-            ts(("pf", 5, 6), ROW, 2048.0, OP.mult, 33.0 * 1024.0, OP.add)
-            ts(("pf", 6, 7), ROW, 5.0, OP.is_ge)
-            ts(("pf", 7, 8), GRP, 16.0, OP.mult, ("pf", 0, 1), OP.add)
-            ts(("pf", 8, 9), ROW, 15.0, OP.is_equal, 0.25, OP.mult)
-            ts(("pf", 9, 10), ROW, 0.0, OP.is_equal)
-            ts(("pf", 10, 11), ROW, -1.0, OP.add)
+    ts(("u16",), ("jf", 0, 16), ROW, OP.is_equal)
+    ts(("pf", 3, 4), ROW, 8.0, OP.mult, 1024.0, OP.add)
+    ts(("pf", 4, 5), ROW, 16.0, OP.mult)
+    ts(("pf", 5, 6), ROW, 2048.0, OP.mult, 33.0 * 1024.0, OP.add)
+    ts(("pf", 6, 7), ROW, 5.0, OP.is_ge)
+    ts(("pf", 7, 8), GRP, 16.0, OP.mult, ("pf", 0, 1), OP.add)
+    ts(("pf", 8, 9), ROW, 15.0, OP.is_equal, 0.25, OP.mult)
+    ts(("pf", 9, 10), ROW, 0.0, OP.is_equal)
 
-    def constants():
-        fill(("wf", 0, 16), 0.5)
-        fill(("wf", 16, 32), 0.0)
-        scan(("wf", 32, 48), ("wf", 0, 16), ("wf", 16, 32), 2.0 * BIG)
-        tt(("wf", 48, 64), ("wf", 32, 48), ("u16",), OP.mult)
-        total(("pf", 11, 12), ("wf", 48, 64))
-        ts(("kb", 0, 16), ("jj", 0, 16), 3, OP.bitwise_and)
-        ts(("kb", 16, 32), ("jj", 0, 16), 2, OP.arith_shift_right)
-        ts(("wf", 0, 16), ("kb", 0, 16), ROW, OP.is_gt, 2.0 ** -20 - 1.0, OP.mult)
-        ts(("wf", 16, 32), ("kb", 16, 32), ("pf", 8, 9), OP.mult, 1.0, OP.add)
-        ts(("wf", 0, 16), ("wf", 0, 16), 1.0, OP.add, ("pf", 11, 12), OP.mult)
-        tt(("tw",), ("wf", 0, 16), ("wf", 16, 32), OP.mult)
-        ts(("w0",), ("w1", 0, L), ("pf", 11, 12), OP.mult)
-        ts(("bh",), ("bo",), 0.5, OP.mult)
-        ts(("bn",), ("bo",), -0.5, OP.mult)
-        ts(("bm",), ("bo",), -1.0, OP.mult)
-        ts(("b15",), ("bo",), ("pf", 8, 9), OP.mult, 2.0 ** -10, OP.mult)
-        ts(("b0",), ("bo",), ("pf", 9, 10), OP.mult)
-        ts(("d5",), ("idn",), ("pf", 6, 7), OP.mult)
-        cp(("ib",), ("idn",))
-        ts(("cb",), ("jf", 0, 16), 256.0, OP.mult, ("pf", 4, 5), OP.add)
-        ts(("cb", 8, 16), ("cb", 8, 16), 1.0, OP.add)
-        ts(("ob",), ("jf", 0, 16), 16.0, OP.mult, ROW, OP.add)
-        fill(("z0",), 1024.0)
-        for c0, c1, _ in CUT:
-            ts(("z0", c0 // 8, c0 // 16 + c1 // 16), ("jf", c0 // 16, c1 // 16), 128.0, OP.mult, ("pf", 3, 4), OP.add)
-        cp(("one",), ("w1", 0, 128))
-        cp(("on",), ("w1", 0, L))
-        ts(("jt",), ("jj", 0, 128), 15, OP.bitwise_and)
-        ts(("l2",), ("jt",), ROW, OP.is_gt)
-        tt(("lt",), ("l2",), ("bo",), OP.mult)
-        ts(("thf",), ("thi",), 1.0, OP.add)
-        ts(("lim",), ("thf",), BIG, OP.mult)
-        own_columns()
-        cp(("wn", OG, OG + L), ("g4", 0, GW, 8), "a")
-        cp(("o0",), ("n4", 0, GW, 8))
-        cp(("r0",), ("n4", 0, GW, 8))
+    def prepare(tok):
+        k = int(tok[1:])
+        if tok[0] == "G":
+            ts(("g4", k * H, k * H + H), ("gi", k * H, k * H + H), 1.0 + 2.0 ** -12, OP.mult, MAGIC, OP.add)
+            act(("g4", k * H, k * H + H), ("g4", k * H, k * H + H), AF.Copy, bias=-(MAGIC + 2048.0))
+        elif tok[0] == "O":
+            cp(("o0",) + CUT[k][0:2], ("n4", 8 * CUT[k][0], 8 * CUT[k][1], 8))
+        elif tok[0] == "R":
+            cp(("r0",) + CUT[k][0:2], ("n4", 8 * CUT[k][0], 8 * CUT[k][1], 8))
+        elif k == 0:
+            fill(("wf", 0, 16), 0.5)
+            fill(("wf", 16, 32), 0.0)
+            ts(("kb", 0, 16), ("jj", 0, 16), 3, OP.bitwise_and)
+            scan(("wf", 32, 48), ("wf", 0, 16), ("wf", 16, 32), 2.0)
+            ts(("kb", 16, 32), ("jj", 0, 16), 2, OP.arith_shift_right)
+            tt(("wf", 48, 64), ("wf", 32, 48), ("u16",), OP.mult)
+            ts(("wf", 0, 16), ("kb", 0, 16), ROW, OP.is_gt, 2.0 ** -20 - 1.0, OP.mult)
+            total(("pf", 11, 12), ("wf", 48, 64))
+            ts(("wf", 16, 32), ("kb", 16, 32), ("pf", 8, 9), OP.mult, 1.0, OP.add)
+            ts(("wf", 0, 16), ("wf", 0, 16), 1.0, OP.add, ("pf", 11, 12), OP.mult)
+            ts(("w0",), ("w1", 0, L), ("pf", 11, 12), OP.mult)
+            tt(("tw",), ("wf", 0, 16), ("wf", 16, 32), OP.mult)
+        elif k == 1:
+            cp(("ib",), ("idn",))
+            ts(("bh",), ("bo",), 0.5, OP.mult)
+            ts(("bn",), ("bo",), -2.0 ** 31, OP.mult)
+        elif k == 2:
+            fill(("z0",), 1024.0)
+            ts(("cb",), ("jf", 0, 16), 256.0, OP.mult, ("pf", 4, 5), OP.add)
+            for c0, c1, _ in CUT:
+                ts(("z0", c0 // 8, c0 // 16 + c1 // 16), ("jf", c0 // 16, c1 // 16), 128.0, OP.mult, ("pf", 3, 4), OP.add)
+            ts(("cb", 8, 16), ("cb", 8, 16), 1.0, OP.add)
+        elif k == 3:
+            ts(("thf",), ("thi",), 1.0, OP.add)
+            ts(("lim",), ("thi",), 1.0, OP.add)
+        elif k == 4:
+            cp(("tm",), ("u16",))
+            ts(("b15",), ("bo",), ("pf", 8, 9), OP.mult, 2.0 ** 30, OP.mult)
+            cp(("one",), ("w1", 0, 128))
+        elif k == 5:
+            ts(("bm",), ("bo",), -1.0, OP.mult)
+            ts(("b0",), ("bo",), ("pf", 9, 10), OP.mult)
+            ts(("d5",), ("idn",), ("pf", 6, 7), OP.mult)
+            ts(("ob",), ("jf", 0, 16), 16.0, OP.mult, ROW, OP.add)
+            cp(("on",), ("w1", 0, L))
+        elif k == 6:
+            ts(("jt",), ("jj", 0, 128), 15, OP.bitwise_and)
+            ts(("l2",), ("jt",), ROW, OP.is_gt)
+            tt(("lt",), ("l2",), ("bo",), OP.mult)
+        else:
+            cp(("wn", OG, OG + L), ("o16",), "a")
 
     def own_columns():
         cp(("o16",), ("g4", 0, GW, 8), "a")
@@ -314,13 +353,11 @@ def rank_program(g, core, T, topo):
             bank = ("pa", "pb")[s % 2]
             mm((bank, 0, L), ("rt", (s - 1) * 128, s * 128), ("o16",))
             cp(("g4", s * GW, (s + 1) * GW, 8), (bank, 0, L), "av"[s % 2])
-        cp(("wn", OG, OG + L), ("o16",), "a")
 
     def run(tok, tau):
         gen, t = divmod(tau, ST)
-        tok, _, js = tok.partition(".")
-        eng = js[1:] or "a"
-        js = js[0:1]
+        eng = "v" if tok[-1] == "v" else "a"
+        tok, _, js = tok.rstrip("v").partition(".")
         kind = tok.rstrip("0123456789") if tok[0:2] not in ("M1", "M2") else tok[0:2]
         b = int(tok[len(kind):]) if tok[len(kind):] else 0
         c0, c1, subs = CUT[b]
@@ -331,6 +368,7 @@ def rank_program(g, core, T, topo):
         e0 = c0 + sum(subs[0:int(js)]) if js else 0
         e1 = e0 + subs[int(js)] if js else 0
         plain = js and (b, int(js)) in PLAIN
+        most = js and (b, int(js)) in MOST
         q = 3 * c0
         sco = (pd, 256, 256 + n)
         rp = (pn, 192, 192 + n)
@@ -346,20 +384,21 @@ def rank_program(g, core, T, topo):
         zz = "zz" if t else "z0"
         yi = ("yi", l0, l1)
         last = t == ST - 1
-        if kind in ("RR", "WW", "MK", "PZ") and t == 0:
+        if kind in ("RR", "WW", "MK", "PZ", "OM", "OF") and t == 0:
             return
         if kind == "RR":
             cp(("rr", c0, c1), (("n4",), ln[0]))
         elif kind == "WW":
-            cp(ww, (("tw",), ln[2]), "a")
+            cp(ww, (("tw",), ln[2]), eng)
+        elif kind == "OM":
+            mm((pn, 0, n), ("idn",), ("rr", c0, c1), True, False)
+            mm((pn, 0, n), ("b15",), ww, False, True)
         elif kind == "OF":
-            if t:
-                mm((pn, 0, n), ("idn",), ("rr", c0, c1), True, False)
-                mm((pn, 0, n), ("b15",), ww, False, True)
-                ts(("of", c0, c1), (pn, 0, n), -8192.0, OP.add)
+            ts(("of", c0, c1), (pn, 0, n), -8192.0, OP.add)
+        elif kind == "RP":
             mm(rp, ("idn",), ("rr" if t else "r0", c0, c1))
         elif kind == "MK":
-            cp(("m0", c0, c1), (("tm",), ln[2]), "a")
+            cp(("m0", c0, c1), (("tm",), ln[2]), eng)
         elif kind == "NG":
             if t:
                 tt(("ng", c0, c1), (("g4", 0, GW), ln[3]), ("m0", c0, c1), OP.mult)
@@ -403,29 +442,47 @@ def rank_program(g, core, T, topo):
             if plain:
                 for h in range(2):
                     act(("ab", 16 * e0 + 512 * h, 16 * e0 + 512 * h + 512), (("pa", "pb")[h],), AF.Abs, bias=-255.0)
+            elif most:
+                ts(("ab", 16 * e0, 16 * e1), ("uu", 16 * e0, 16 * e1), 255.0, OP.max, -127.5, OP.add)
             else:
                 act(("ab", 16 * e0, 16 * e1), ("uu", 16 * e0, 16 * e1), AF.Abs, bias=-255.0)
+        elif kind == "AU":
+            for s in range(16):
+                mm((pd, e0 - c0, e1 - c0), onto(s, 1), ("uu", 16 * e0 + s, 16 * e1, 16), s == 0, False)
         elif kind == "AM":
             for s in range(16):
                 rhs = ("ab", 16 * e0 + 64 * s, 16 * e0 + 64 * s + 64) if plain else ("ab", 16 * e0 + s, 16 * e1, 16)
-                mm((pd, e0 - c0, e1 - c0), onto(s), rhs, s == 0, s == 15)
+                mm((pd, e0 - c0, e1 - c0), onto(s, 2 if most else 0), rhs, s == 0 and not most, s == 15)
         elif kind == "GO":
-            act((pd, 0, n), (pd, 0, n), AF.Relu, bias=("lim",), scale=-BIG)
+            if eng == "a":
+                act((pd, 0, n), (pd, 0, n), AF.Relu, bias=("lim",), scale=-1.0)
+            else:
+                ts((pd, 0, n), (pd, 0, n), ("lim",), OP.is_lt)
         elif kind == "GV":
             tt(("ok", c0, c1), (pd, 0, n), ww, OP.min)
+        elif kind == "GM":
             mm(sco, ("bh",), ("ok", c0, c1))
-        elif kind == "PK":
+        elif kind == "PF":
             tt(("ff", c0, c1), ("ok", c0, c1), sco, OP.is_gt)
-            act(("qq", q + 2 * n, q + 3 * n), ("ff", c0, c1), AF.Copy, scale=("pf", 5, 6))
+        elif kind == "PW":
+            if eng == "a":
+                act(("qq", q + 2 * n, q + 3 * n), ("ff", c0, c1), AF.Copy, scale=("pf", 5, 6))
+            else:
+                ts(("qq", q + 2 * n, q + 3 * n), ("ff", c0, c1), ("pf", 5, 6), OP.mult)
+        elif kind == "PQ":
             tt(("qq", q, q + n), ("ff", c0, c1), (pe, 0, n), OP.mult)
             tt(("qq", q + n, q + 2 * n), ("ff", c0, c1), rp, OP.mult)
         elif kind == "PC":
             for a in range(16):
                 mm((pn, 400, 400 + 3 * lc), onto(a), ("qq", q + a, q + 3 * n, 16), a == 0, a == 15)
-        elif kind == "YY":
+        elif kind == "YM":
             mm((pd, 0, n), ("ib",), ("tr", 16 * c0, 16 * c1, 16), True, False, [("t0", c0, c1)])
             mm((pd, 0, n), ("bn",), ("ok", c0, c1), False, True)
-            act(("yy", c0, c1), (pd, 0, n), AF.Relu)
+        elif kind == "YY":
+            if eng == "a":
+                act(("yy", c0, c1), (pd, 0, n), AF.Relu)
+            else:
+                ts(("yy", c0, c1), (pd, 0, n), 0.0, OP.max)
         elif kind == "M1":
             tt(("ti", l0, l1), ls, (zz, 2 * l0, 2 * l0 + lc), OP.max)
             tt(("ti", 16 + l0, 16 + l1), lr, (zz, 2 * l0 + lc, 2 * l1), OP.add)
@@ -434,12 +491,13 @@ def rank_program(g, core, T, topo):
             o = LW * tau
             ts(li[2], yi, 11, OP.arith_shift_right, 15, OP.bitwise_and)
             if not last:
-                for k, m in ((0, 8191), (3, 2047), (1, 24576)):
-                    ts(li[k], yi, m, OP.bitwise_and)
+                ts(li[0], yi, 8191, OP.bitwise_and)
             tt(("li", cs, cs + lc), li[2], ("cb", l0, l1), OP.add)
             if last:
                 cp(("lo", o + cs, o + cs + lc), ("li", cs, cs + lc))
             else:
+                for k, m in ((3, 2047), (1, 24576)):
+                    ts(li[k], yi, m, OP.bitwise_and)
                 cp(("lo", o + 5 * l0, o + 5 * l1), ("li", 5 * l0, 5 * l1))
                 send(nxt, "lo", o + lb, o + lb + 4 * lc, "ln", o + LW + lb, "li%d_%d" % (tau, b))
         elif kind == "XO":
@@ -452,19 +510,23 @@ def rank_program(g, core, T, topo):
         elif kind == "ST":
             o = LW * tau + CUT[0][1] // 4
             cp((XR, ("lo", o, o + 16)), ("ao", L * tau, L * tau + L))
-            if tau == TAU - 1:
-                registers_and_sums()
         elif kind == "HI":
             if t in (1, 2, 3):
                 send(T.cores[(rank - t) % N], "ho", 32 * tau, 32 * tau + 32, "hn", 32 * tau, "h%d" % tau)
-        elif kind == "CO":
-            if tau < TAU - 1:
+        elif kind in ("CA", "CB", "CC", "CD", "CE"):
+            if tau == TAU - 1:
+                return
+            if kind == "CA":
                 ts(("hc",), (hist, 32 * tau, 32 * tau + 16), float(ZC), OP.is_equal)
                 mm(("pa", 256, 272), ("one",), ("hc",))
+            elif kind == "CB":
                 total(("af",), ("pa", 256, 272))
+            elif kind == "CC":
                 cp(("ai", 0, 1), ("af",))
+            elif kind == "CD":
                 ts(("ai", 1, 2), ("ai", 0, 1), 63, OP.bitwise_and)
-                ts(("lim",), ("ai", 1, 2), ("thf",), OP.add, BIG, OP.mult)
+            else:
+                ts(("lim",), ("ai", 1, 2), ("thf",), OP.add)
         elif not last:
             return
         elif kind == "EE":
@@ -475,14 +537,17 @@ def rank_program(g, core, T, topo):
             tt(("e1",), ("hf", 0, 48), ("hf", 64, 112), OP.add)
             tt(("hw", 0, 112), ("hv", 0, 112), ("hm", 0, 112), OP.add)
             tt(("er",), ("e1", 0, 16), ("e1", 32, 48), OP.add)
+        elif kind == "EF":
             mm(("pa", 0, L), ("b0",), ("on",), True, False)
             for a in range(16):
                 mm(("pa", a, L, 16), move(a, 0), ("er",), False, a == 15)
             cp(("eb",), ("pa", 0, L), "a")
-            mm(("pb", 0, L), ("d5",), ("o16",), True, False)
-            for s in range(4):
-                for a in range(16):
-                    mm(("pb", a, L, 16), move(a, s), ("hw", 32 * s, 32 * s + 16), False, False)
+        elif kind in ("EG", "EH", "EI", "EJ"):
+            s = "GHIJ".index(kind[1])
+            if s == 0:
+                mm(("pb", 0, L), ("d5",), ("o16",), True, False)
+            for a in range(16):
+                mm(("pb", a, L, 16), move(a, s), ("hw", 32 * s, 32 * s + 16), False, False)
         elif kind == "FL":
             fl = (pe, 256, 256 + n)
             mm(fl, ("b0",), ("on", c0, c1), True, False)
@@ -495,10 +560,25 @@ def rank_program(g, core, T, topo):
                 mm(("pb", c0, c1), onto(4), ("qq", 3 * c0, 2 * c0 + c1), False, False)
             mm(("pb", 0, L), onto(4), ("nf",), False, True)
             ts(("ind",), ("pa", 0, L), ROW, OP.is_equal)
-            cp(("da",), ("pb", 0, L), "a")
+        elif kind == "SG":
+            if gen < GENS - 1:
+                cp(("da",), ("pb", 0, L), "a")
+            else:
+                ts(("fo", 0, L), ("pb", 0, L), 0.0, OP.is_le, 2047.0, OP.add)
+                tt(("da",), ("fo", 0, L), ("pb", 0, L), OP.add)
+        elif kind == "EK":
+            if gen == GENS - 1:
+                ts(("x1",), ("o16",), 0.0, OP.is_le, 2047.0, OP.add)
+                tt(("wn", OG, OG + L), ("x1",), ("o16",), OP.add)
+        elif kind == "RS":
+            if gen == GENS - 1:
+                registers_and_sums()
+        elif kind == "SD":
             scan(("pre",), ("on",), ("ind",), 0.0)
             mm(("pa", 300, 301), ("lt",), ("pre", L - 1, L))
+        elif kind == "SE":
             ts(("x1",), ("pre",), ("pa", 300, 301), OP.add, -1.0, OP.add)
+        elif kind == "SF":
             tt(("x2",), ("x1",), ("ind",), OP.mult)
             for a in range(16):
                 mm(("pa", 320, 336), onto(a), ("x2", a, L, 16), a == 0, a == 15)
@@ -529,15 +609,19 @@ def rank_program(g, core, T, topo):
 
     for tau in range(TAU):
         gen, t = divmod(tau, ST)
-        for tok in (ORDER if t else AGAIN if tau else FIRST):
+        for tok in (LAST if t == ST - 1 else ORDER if t else AGAIN if tau else FIRST):
             if tok[0] == "Q":
                 turn(int(tok[1:]))
+            elif tok[0] in "GORL" and tok[1:].isdigit():
+                prepare(tok)
             elif tok == "RT":
                 turns()
-            elif tok == "LC":
-                constants()
+            elif tok == "RA":
+                turn_all()
+            elif tok == "RB":
+                turn_rest()
             elif tok == "GC":
-                cp(("g16",), ("g4", 0, GW), "a")
+                cp(("g16", 0, GW), ("g4", 0, GW), "g")
             elif tok == "OW":
                 own_columns()
             elif tok == "OT":
@@ -548,10 +632,8 @@ def rank_program(g, core, T, topo):
                 run(tok[0:-1], tau + 1)
         if t == ST - 1:
             new = (("wn", min(SR, BI[gen]), OG + L), ("pr",))
-            cp(("g4", 0, GW, 8) if gen < GENS - 1 else ("da",), new)
+            cp(("g4", 0, GW, 8) if gen < GENS - 1 else ("fo", 0, L), new)
 
-    ts(("fo", 0, L), ("da",), 0.0, OP.is_le, 2047.0, OP.add)
-    tt(("fo", 0, L), ("fo", 0, L), ("da",), OP.add)
     dma([(T.yg[:], T.fo[:, 0:L])], [R("fo", 0, L)], None, True)
     for i in range(nd[0]):
         if known["s"].get("d%d" % i, 0) < 16:

@@ -5,44 +5,33 @@ N, GENS, ST, K = 4, 2, 5, 64
 L, GW, XW = 256, 2048, 4096
 ZC = 2048
 MAGIC = 12582913.0
-BIG = 2.0 ** 40
 TAU = GENS * ST
 CUT = [(0, 128, (64, 64)), (128, 256, (64, 64))]
-PLAIN = ((0, 0),)
-MOST = ((1, 1),)
-NCH = len(CUT)
-DMAS = 44
-DROT = (1, 3, 2)
+PLAIN = ((0, 0), (1, 0))
+EDGE = ((0, 0),)
+DMAS = 32
 LW = 80
 SR, BI, OG = 64, (320, 0), 384
-ORDER = """D0 DA0 RR1 WW1 TA0 OF1 TB0.0 MK1 NG1 TB0.1 X0.0 E1.0 NL1 D1 DA1 X0.1 E1.1 TA1 TB1.0 TB1.1 AB0.0 AB0.1 PZ0 PZ1 X1.0 GO0 GV0 PK0 YY0 PC0 X1.1
- AB1.0 M10 ML0 FL0 XO0 M20 AB1.1 EE RR0' WW0' OF0' MK0' GO1 GV1 PK1 E0.0' FL1 YY1 PC1 NG0' SA M11 ML1 XO1 SB M21 ST E0.1' SC CO HI NL0'""".split()
-FIRST = """LC OF0 NG0 NL0 E0.0 E1.0v E0.1 RT GC OF1 NG1 NL1 D0 DA0 TA0 TB0.0 TB0.1 D1 DA1 E1.1 X0.0 TA1 TB1.0 TB1.1 X0.1 AB0.0 Q0 Q1 AB0.1 X1.0 GO0 GV0 PK0 YY0 PC0
- M10 ML0 X1.1 AB1.0 Q2 Q3 XO0 M20 Q4 Q5 AB1.1 Q6 Q7 GO1 GV1 PK1 YY1 PC1 Q8 Q9 M11 ML1 Q10 Q11 XO1 M21 RR0' WW0' OF0' MK0' E0.0' NG0' ST E0.1' CO NL0'""".split()
-AGAIN = """OW E0.0 E1.0v OF0 NG0 NL0 E0.1 OF1 NG1 NL1 D0 DA0 TA0 TB0.0 TB0.1 D1 DA1 E1.1 X0.0 TA1 TB1.0 TB1.1 X0.1 AB0.0 AB0.1 OT X1.0 GO0 GV0 PK0 YY0 PC0
- X1.1 AB1.0 M10 ML0 XO0 M20 AB1.1 GO1 GV1 PK1 YY1 PC1 RR0' WW0' OF0' MK0' M11 ML1 XO1 E0.0' M21 NG0' ST E0.1' CO NL0'""".split()
-ROTA = (0, 2, 3, 4, 8, 10, 11)
-TBQ = ("gvg", "vgv", "gvg", "vgv")
-ORDER = """D0 MK1 RR1 NG1 WW1 PZ1 XL0.1 OF1 DA0 TA0 E1.1v NM1 NL1 TB0.1 X0.0 PA0.0 D1 E1.0 X0.1 DA1 PB0.0 F1.0 F1.1 AB0.0 TA1 AB0.1 PZ0 AM0.0 AM0.1 EE TB1.0 XL1.0 TB1.1 XL1.1 X1.0 GO0 GV0 X1.1 AB1.0 PK0 AM1.0 PC0 AB1.1 M10 ML0 AM1.1 GO1 GV1 PK1 YY0 FL0 XO0 WW0' YY1 FL1 PC1 M20 MK0' RR0' M11 SA OF0' E0.0' NG0' ML1 NM0' XO1 E0.1' HI M21 NL0' SB F0.0' ST SC CO XL0.0' F0.1'""".split()
-AGAIN = """E1.0v OW E0.0 NM0 NL0 NM1 D0 DA0 F0.0 F1.0 NL1 D1 E0.1 TA0 OF0 XL0.0 F0.1 X0.0v PA0.0 DA1 TB0.1 PB0.0 OF1 XL0.1 TA1 E1.1 X0.1 TB1.0 F1.1 AB0.0 AB0.1 AM0.0 XL1.0 TB1.1 AM0.1 XL1.1 GO0 X1.0 GV0 PK0 AB1.0 X1.1 PC0 AM1.0 M10 ML0 AB1.1 OT AM1.1 GO1 GV1 YY0 XO0 PK1 WW0' MK0' RR0' M20 YY1 PC1 M11 OF0' XO1 E0.0' NG0' E0.1' NM0' ML1 CO M21 ST F0.0' XL0.0' NL0' F0.1'""".split()
-FIRST = """LC NM1 E0.0v NL1 F0.0 GC E1.1 NM0 NL0 E1.0v D0 OF0 F1.1 E0.1 DA0 XL0.0 TA0 TB0.1 X0.0 OF1 F0.1 D1 RT PA0.0 PB0.0 F1.0 AB0.0 DA1 AM0.0 TA1 XL0.1 X0.1 TB1.1 AB0.1 TB1.0 XL1.1 AM0.1 GO0 X1.1 Q0 XL1.0 X1.0 Q1 Q3 Q2 GV0 PK0 PC0 Q5 M10 AB1.1 AM1.1 Q7 Q9 Q4 AB1.0 Q11 AM1.0 ML0 GO1 Q6 GV1 PK1 MK0' WW0' XO0 NG0' YY0 PC1 YY1 Q8 M11 M20 XO1 NM0' Q10 ML1 CO M21 NL0' ST RR0' OF0' E0.0v' F0.0' E0.1' XL0.0' F0.1'""".split()
-ROTA = (1, 2, 4, 7, 8, 10, 11)
-TBQ = ('gga', 'ggv', 'gvv', 'gvg')
-AGAIN = """OW NM0 E0.0 E1.0v NL0 NM1 D0 DA0 F0.0 NL1 E0.1 RP1 D1 DA1 TA0 XL0.0 F1.0 X0.0v F0.1 PA0.0 E1.1 TB0.1 PB0.0 XL0.1 TA1 XL1.0 X0.1 RP0 AB0.0 F1.1 AB0.1 TB1.0 AM0.0 X1.0 TB1.1 AB1.0 XL1.1 AM0.1 GO0v GV0 GM0 PF0 PW0 PQ0 YM0 X1.1 PC0 AM1.0 M10 XO0 ML0 AB1.1 OT YY0v AM1.1 GO1 GV1 GM1 PF1 PW1 PQ1 YM1 WW0' MK0' PC1 M20 RR0' YY1 OM0' XO1 OF0' M11 CA E0.0' NG0' NM0' CB ML1 E0.1' M21 ST CC CD F0.0' RP0' XL0.0' NL0' F0.1' CE""".split()
-FIRST = """LC E0.0v E1.1 NM0 F0.0 F1.1 NM1 E0.1 F0.1 NL0 XL0.0 E1.0 NL1 GC X0.0v D1 DA1 D0 DA0 TA1 TA0 RP0 XL1.1 F1.0 TB0.1 PB0.0 RT XL0.1 X0.1 PA0.0 TB1.0 AB0.0 XL1.0 TB1.1 Q0 AB0.1 X1.1 AM0.0 AM0.1 X1.0 GO0 GV0 Q2 RP1 Q1 Q3 GM0 AB1.1 PF0 PQ0 YM0 PW0v PC0 M10 ML0 YY0v AB1.0 Q5 AM1.1 AM1.0 GO1v Q4 GV1 GM1 PF1 Q7 YM1 PQ1 PW1v Q9 XO0 PC1 Q6 MK0v' M11 Q8 WW0v' NG0' Q10 ML1 M20 YY1 XO1 NM0' CA Q11 M21 CB NL0' CC CD ST RR0' OM0' OF0' RP0' E0.1' CE E0.0v' F0.0' XL0.0' F0.1'""".split()
-ORDER = """MK1 D0 RR1 NG1 PZ0 DA0 WW1 TA0 TB0.1 XL0.1 NM1 X0.0 NL1 OM1 D1 PA0.0 OF1 X0.1 DA1 TA1 E1.0 PB0.0 AB0.0 F1.0 AB0.1 E1.1v RP1 XL1.0 AM0.0 TB1.0 AM0.1 EE GO0 X1.0 F1.1 TB1.1 EF GV0 XL1.1 GM0 PF0 PW0 AB1.0 PQ0 EG X1.1 YM0 PC0 FL0 AB1.1 EH AM1.0 M10 AM1.1 ML0 GO1 YY0 GV1 XO0 EI GM1 PZ1 WW0' PF1 EJ PW1 RR0' PQ1 MK0' OM0' OF0' FL1 YM1 M20 NG0' SA SD PC1 SE SF YY1 NM0' M11 XO1 E0.0' ML1 HI CA M21 SB ST F0.0' CB E0.1' CC XL0.0' SC RP0' CD NL0' F0.1' CE""".split()
-TBQ = ('aaa', 'vvg', 'vgg', 'gaa')
-MOST = ()
-LAST = """MK1 D0 RR1 NG1 PZ0 DA0 WW1 TA0 TB0.1 XL0.1 NM1 X0.0 NL1 OM1 D1 PA0.0 OF1 X0.1 DA1 TA1 E1.0 PB0.0 AB0.0 F1.0 AB0.1 E1.1v RP1 XL1.0 AM0.0 TB1.0 AM0.1 EE EK GO0 X1.0 F1.1 TB1.1 EF GV0 XL1.1 GM0 PF0 PW0 AB1.0 PQ0 EG X1.1 YM0 PC0 FL0 AB1.1 EH EI EJ AM1.0 M10 AM1.1 ML0 GO1 YY0 GV1 XO0 GM1 PZ1 PF1 PW1 PQ1 FL1 YM1 M20 SA SG SD PC1 SE SF YY1 M11 XO1 ML1 CA M21 SB ST RS CB CC SC CD CE""".split()
-ORDER = [_t for _t in ORDER if _t[0:2] not in ("EE", "EF", "EG", "EH", "EI", "EJ", "FL", "SA", "SB", "SC", "SD", "SE", "SF")]
-FIRST = """L0 G0 L1 G1 L2 G2 G3 RA OW O0 E0.0v E0.1 L4 L5 NM0 F0.0 O1 R0 R1 NM1 F0.1 NL0 XL0.0 E1.0 E1.1v NL1 RB X0.0 D0 D1 DA0 DA1 F1.0 F1.1 TA0 TA1 RP0 TB0.1 PA0.0 PB0.0 XL0.1 X0.1 TB1.0 AB0.0 XL1.0 XL1.1 TB1.1 AB0.1 X1.0 AM0.0 AM0.1 L3 GO0 GV0 RP1 GM0 PF0 PQ0 YM0 PW0 PC0 X1.1 M10 ML0 YY0 AB1.0 AM1.0 AB1.1 AM1.1 L6 L7 RT GO1 GV1 GM1 PF1 YM1 PQ1 PW1 XO0 PC1 MK0' M11 WW0' NG0' ML1 M20 YY1 XO1 NM0' CA M21 CB NL0' CC CD ST RR0' OM0' OF0' RP0' E0.1' CE E0.0v' F0.0' XL0.0' F0.1'""".split()
-FIRST = """G0 G1 G2 G3 RA RB L0 O0 L2 OW RT NM0 R0 NM1 NL1 E0.1 L1 NL0 O1 F0.1 E1.0v E0.0 D0 GC F0.0 D1 XL0.0 F1.0 E1.1 DA0 L3 DA1 F1.1 XL0.1 X0.0 TA0 PA0.0 PB0.0 RP0 TA1 TB0.1 XL1.0 TB1.1 XL1.1 AB0.0 X0.1 TB1.0 X1.1 X1.0 AM0.0 AB0.1 AM0.1 AB1.1 GO0 GV0 Q5 GM0 PF0 PW0 PQ0 AB1.0 AM1.1 R1 L7 PC0 Q4 RP1 AM1.0 GO1 YM0 Q7 Q6 M10 ML0 GV1 XO0 GM1 Q9 PF1 PQ1 PW1v YY0v PC1 Q8 Q11 YM1 XO1 Q10 M11 L6 L4 CA WW0' ML1 CB RR0' CC OM0' OF0' MK0' CD M20 YY1 M21 NG0' E0.0' NM0' CE L5 ST RP0' F0.0' NL0' XL0.0' E0.1' F0.1'""".split()
-ROTA = (4, 5, 6, 7, 8, 9, 10, 11)
-AGAIN = """OW E0.0 NM0 E1.0v NL0 NM1 NL1 D1 D0 E0.1 F0.0 XL0.0 RP0 F0.1 X0.0v DA0 PA0.0 TA0 DA1 PB0.0 XL0.1 E1.1 AB0.0 F1.1 TB0.1 TA1 X0.1 F1.0 AM0.0 TB1.0 XL1.0 AB0.1 AM0.1 TB1.1 RP1 XL1.1 GO0 X1.0 GV0 GM0 AB1.0 PF0 PW0 PQ0 X1.1 PC0 M10 ML0 AM1.0 YM0 AB1.1 OT AM1.1 GO1v XO0 MK0' GV1 WW0' RR0' GM1 PF1 OM0' PQ1 YM1 OF0' PW1 YY0 PC1 M20 NG0' E0.0' YY1v M11 NM0' XO1 ML1 CA E0.1' M21 F0.0' RP0' CB CC ST CD NL0' CE XL0.0' F0.1'""".split()
-LAST = """D0 RR1 MK1v WW1v RP1 NG1 DA0 OM1 X0.0 OF1 XL0.1 NM1 TA0 TB0.1 NL1 PA0.0 PZ0 PB0.0 E1.0 D1 F1.0 X0.1 DA1 AB0.0 AB0.1 TA1 EE AM0.0 XL1.0 TB1.0 EK E1.1 EF X1.0 AM0.1 GO0v F1.1 TB1.1 GV0 EG GM0 XL1.1 YM0 X1.1 AB1.0 PF0 PW0 PQ0 EH AB1.1 AM1.0 PC0 YY0v XO0 FL0 AM1.1 M10 ML0 EI GO1v GV1 M20 GM1 PF1 EJ PQ1 FL1 PZ1 PW1 SA SD SG PC1 YM1 YY1 SE SF XO1 M11 M21 ML1 SB ST CA CB CC SC CD CE RS""".split()
-ORDER = """D0 RR1 MK1 PZ0 DA0 NG1 TA0 WW1v NM1 TB0.1 NL1 OM1 XL0.1 X0.0 D1 OF1 PB0.0 DA1 PA0.0 E1.0 X0.1 AB0.0 TA1 AB0.1 E1.1v F1.0 AM0.0 TB1.0 TB1.1 XL1.0 AM0.1 F1.1 X1.0 GO0 GV0 XL1.1 GM0 PF0 PW0 PQ0 X1.1 AB1.0 YM0 RP1 AB1.1 PC0 M10 ML0 AM1.0 YY0v AM1.1 XO0 GO1v WW0' GV1 GM1 PZ1 PF1 PW1 YM1 RR0' MK0' OM0' PQ1 PC1 OF0' E0.0' YY1v M20 NG0' M11 XO1 HI RP0' NM0' ML1 CA M21 F0.0' CB ST E0.1' CC XL0.0' CD F0.1' NL0' CE""".split()
-TBQ = ('gva', 'vgv', 'ggv', 'ggg')
 DROT = (1,)
+ROTA = (5, 6, 7, 8, 11)
+TBQ = ("", "vvg", "gav", "ggg")
+FIRST = """G0 G1 G2 G3 RA RB O0 E0.0 L0 OW E0.1v R0 NM0 F0.0 NL0 XL0.0 X0.0 NM1 D0 DA0 L1 NL1 D1 GC L2 O1 F0.1 L3 DA1 PB0.0 XL0.1 TA0 TA1 TB0.1
+ PA0.0 RT E1.1 F1.1 E1.0 X0.1 AB0.0 F1.0 AC0.0 RP0 AM0.0 XL1.1 TB1.1 AB0.1 AC0.1 AN0.0 AM0.1 L4 AN0.1 X1.1 XL1.0 GO0 AB1.1 GV0 TB1.0 GM0
+ PF0 PW0 AC1.1 AM1.1 PQ0 Q5 PC0 X1.0 M10 AB1.0 XO0 AC1.0 ML0 AN1.1 Q7 Q4 AM1.0 L6 AN1.0 GO1v Q6 GV1 Q9 GM1 Q8 Q11 YM1 R1 PF1 PW1 RP1 PQ1
+ Q10 YM0 PC1 YY1 YY0 M20 RR0' L7 WW0' MK0' OM0' XO1 M11 OF0' E0.0' CA M21 NG0' CB E0.1' NM0' ML1 CC L5 CD RP0' F0.0' ST NL0' XL0.0'
+ F0.1' CE""".split()
+ORDER = """D0 RR1 WW1v MK1v OM1 DA0 X0.0 NG1 OF1 NM1 PZ0 E1.0 TA0 PZ1 TB0.1 NL1 XL0.1 D1 PB0.0 DA1 X0.1 PA0.0 F1.0 AC0.0 AB0.0 RP1 AM0.0 AN0.0
+ TA1 AB0.1 AM0.1 XL1.0 AC0.1 E1.1v AN0.1 GO0v X1.0 F1.1 GV0 GM0 TB1.0 PF0 PB1.0 TB1.1 XL1.1 PW0 AC1.0 PA1.0 PQ0 X1.1 AB1.0 AB1.1 AC1.1 PC0
+ AM1.0 AN1.0 M10 ML0 AM1.1 AN1.1 GO1v YM0 XO0 GV1 GM1 PF1 YY0 PQ1 WW0' RR0' YM1 PW1v OM0' PC1 M20 MK0' OF0' YY1 RP0' NG0' M11 NM0' XO1
+ ML1 CA M21 CB E0.0' E0.1' NL0' HI CC ST CD F0.0' XL0.0' CE F0.1'""".split()
+LAST = """RR1 D0 WW1v OM1 MK1v NG1 OF1 X0.0 DA0 E1.0 NM1 PB0.0 TA0 TB0.1 NL1 D1 XL0.1 DA1 E1.1 TA1 TB1.0 F1.0 PA0.0 AB0.0 XL1.0 F1.1 X0.1 AC0.0
+ X1.0 AC0.1 AM0.0 AB0.1 XL1.1 AC1.0 AB1.0 TB1.1 YS AN0.0 X1.1 AM0.1 AN0.1 AB1.1 AM1.0 GO0 AN1.0 EE GV0 AC1.1 AM1.1 GM0 EL EJv EIv AN1.1
+ PF0 GO1v EH YM0 GV1 FL0 GM1 PF1 EF PW0 PQ0 PQ1 SA EG YY0 SD PZ1 SE FL1 PC0 PZ0 PW1 SH SF M10 XO0 PC1 ML0 YO0 M20 SG SB XO1 EK YM1 M11
+ YY1 CA M21 CB YA ML1 YO1 YD0 CC SC ST YD1 YE CD SN CE""".split()
+AGAIN = """E0.0 OW E1.0v NM0 NM1 NL0 D0 NL1 D1 DA0 F0.0 TA0 XL0.0 E0.1 F1.0 X0.0v DA1 F0.1 XL0.1 RP0 PA0.0 E1.1 AB0.0 PB0.0 TB0.1 F1.1 TA1 X0.1
+ TB1.0 AC0.0 XL1.0 AM0.0 X1.0 AN0.0 AB0.1 AC0.1 AM0.1 AN0.1 GO0 GV0 GM0 AB1.0 XL1.1 PF0 PW0 AC1.0 PQ0 TB1.1 X1.1 AM1.0 AB1.1 YM0 PC0 AC1.1
+ AN1.0 M10 ML0 OT AM1.1 AN1.1 GO1v GV1 YY0 GM1 XO0 WW0' PF1 RP1 RR0' YM1 PW1 PQ1 OM0' M20 OF0' MK0' PC1 YY1 NG0' E0.0' NM0' RP0' M11 XO1
+ ML1 CA F0.0' M21 CB ST CC NL0' CD XL0.0' CE E0.1' F0.1'""".split()
 
 SCRATCH = {}
 for _n, _w, _d in (
@@ -53,23 +42,23 @@ for _n, _w, _d in (
         ("ok", L, "bfloat16"), ("ff", L, "float16"), ("qq", 3 * L, "float16"), ("yy", L, "bfloat16"), ("ti", 32, "float32"),
         ("yi", 16, "int32"), ("li", LW, "int32"), ("zz", 32, "float32"), ("z0", 32, "float32"), ("cb", 16, "float32"),
         ("lo", LW * TAU, "uint16"), ("ln", LW * TAU, "uint16"), ("ao", L * TAU, "bfloat16"), ("an", L * TAU, "bfloat16"),
-        ("ho", 32 * TAU, "uint16"), ("hn", 32 * TAU, "uint16"), ("hv", 128, "float16"), ("hf", 128, "float16"), ("hm", 128, "float16"), ("hw", 128, "float16"),
-        ("hc", 16, "float16"), ("e1", 48, "float16"), ("er", 16, "float16"), ("eb", L, "float16"),
+        ("ho", 32 * TAU, "uint16"), ("hn", 32 * TAU, "uint16"), ("hv", 128, "float16"), ("hf", 128, "float16"), ("hm", 128, "float16"), ("hw", 80, "float16"),
+        ("hc", 16, "float16"), ("e1", 48, "float16"), ("ed", 5 * L, "float16"),
         ("wn", OG + L, "float32"), ("da", L, "float32"), ("o16", L, "float16"), ("ind", L, "float16"), ("pre", L, "float16"), ("on", L, "float16"),
         ("x1", L, "float16"), ("x2", L, "float16"), ("pl", 16, "uint16"), ("pr", 16, "uint16"), ("kr", 32, "int32"), ("kf", 64, "float32"), ("ob", 16, "float32"),
         ("af", 1, "float32"), ("ai", 2, "int32"), ("lim", 1, "float32"), ("thi", 1, "int32"), ("thf", 1, "float32"),
         ("jj", L, "int32"), ("jf", L, "float32"), ("jt", 128, "int32"), ("kb", 32, "int32"), ("wf", 64, "float32"),
         ("pi", 4, "int32"), ("pf", 16, "float32"), ("u16", 16, "float32"), ("tw", 16, "bfloat16"), ("tm", 16, "bfloat16"),
-        ("se", 2048 + 32, "float16"), ("sz", 432, "float16"), ("idn", 128, "float16"), ("ib", 128, "bfloat16"), ("bo", 128, "float16"), ("bm", 128, "float16"),
-        ("bh", 128, "bfloat16"), ("bn", 128, "bfloat16"), ("b15", 128, "bfloat16"), ("b0", 128, "float16"), ("d5", 128, "float16"),
-        ("lt", 128, "float16"), ("l2", 128, "float16"), ("one", 128, "float16"), ("rt", 384, "float16"), ("r2", 384, "float16"), ("jr", 384, "int32"),
-        ("fo", 3 * L, "float32")):
+        ("se", 2048 + 32, "float16"), ("sz", 144, "float16"), ("idn", 128, "float16"), ("ib", 128, "bfloat16"), ("ibn", 128, "bfloat16"),
+        ("bo", 128, "float16"), ("bm", 128, "float16"), ("bh", 128, "bfloat16"), ("bn", 128, "bfloat16"), ("b15", 128, "bfloat16"), ("b0", 128, "float16"),
+        ("d5", 128, "float16"), ("lt", 128, "float16"), ("l2", 128, "float16"), ("one", 128, "float16"),
+        ("rt", 384, "float16"), ("r2", 384, "float16"), ("jr", 384, "int32"), ("fo", 3 * L, "float32")):
     SCRATCH[_n] = ("sbuf", [128, _w], _d)
 PSUM = ["pe0", "pe1", "pd0", "pd1", "pl0", "pl1", "pa", "pb"]
 for _n in PSUM:
     SCRATCH[_n] = ("psum", [128, 512], "float32")
 SEMAPHORES = ["v", "a", "p", "gc", "loc", "b0", "b1"] + ["d%d" % i for i in range(DMAS)] + ["h%d" % i for i in range(TAU)]
-for _b in range(NCH):
+for _b in range(len(CUT)):
     SEMAPHORES += ["li%d_%d" % (_t, _b) for _t in range(TAU)] + ["ar%d_%d" % (_t, _b) for _t in range(TAU)]
 
 
@@ -165,8 +154,9 @@ def rank_program(g, core, T, topo):
     def sc(s):
         return (X(s)[0], [X(s)[1]]) if isinstance(s, tuple) else (s, [])
 
-    def ts(out, src, s1, op0, s2=None, op1=None):
+    def ts(out, src, s1, op0, s2=None, op1=None, tag=None):
         o, io = side(out)
+        io = [tag] if tag else io
         a, ia = side(src)
         c1, i1 = sc(s1)
         c2, i2 = sc(s2)
@@ -200,6 +190,12 @@ def rank_program(g, core, T, topo):
         c, ic = sc(scale)
         op("a", lambda s: s.activation(o, a, f, bias=b, scale=c), ia + ib + ic, [tag] if tag else io)
 
+    def times(q, out, src, c, tag=None):
+        if q == "a":
+            act(out, src, AF.Copy, scale=c, tag=tag)
+        else:
+            ts(out, src, c, OP.mult, tag=tag)
+
     def iota(out, pattern, base, ch):
         o, io = side(out)
         op("g", lambda q: q.iota(o, pattern, base, ch), [], io)
@@ -220,8 +216,8 @@ def rank_program(g, core, T, topo):
         b, ib = side(rhs)
         op("p", lambda t: t.matmul(o, a, b, start, stop), ia + ib + list(more), io)
 
-    def onto(a, k=0):
-        return ("sz", 144 * k + 15 - a, 144 * k + 143 - a)
+    def onto(a):
+        return ("sz", 15 - a, 143 - a)
 
     def move(a, b):
         return ("se", 16 + 129 * a - b, 144 + 129 * a - b)
@@ -238,8 +234,8 @@ def rank_program(g, core, T, topo):
     dma([(T.n4[:, 0:h], T.nb[:, 0:h])], [], R("n4", 0, h))
     dma([(T.an[:, 0:L], T.a0[:])], [], R("an", 0, L))
     dma([(T.xr[:, 0:ZC], T.x[:, 0:ZC])], [], R("xr", 0, ZC))
-    dma([(T.n4[:, h:GW], T.nb[:, h:GW])], [], R("n4", h, GW))
     dma([(T.xr[:, ZC + 1:XW + 1], T.x[:, ZC:XW])], [], R("xr", ZC, XW + 1))
+    dma([(T.n4[:, h:GW], T.nb[:, h:GW])], [], R("n4", h, GW))
     dma([(T.thi[:], T.th[:])], [], R("thi"))
     iota(("pi", 0, 1), [[0, 1]], 0, 1)
     iota(("jj",), [[1, L]], 0, 0)
@@ -248,16 +244,15 @@ def rank_program(g, core, T, topo):
 
     def turn_all():
         for s in DROT:
-            d = (4 * s + 7) % 16 - 7
-            dma([(T.g4[max(0, -d):128 - max(0, d), s * GW:(s + 1) * GW], T.g4[max(0, d):128 - max(0, -d), 0:GW])], [R("g4", 0, GW)], R("g4", s * GW, (s + 1) * GW))
+            dma([(T.g4[0:128 - 4 * s, s * GW:(s + 1) * GW], T.g4[4 * s:128, 0:GW])], [R("g4", 0, GW)], R("g4", s * GW, (s + 1) * GW))
 
     def turn_rest():
         for k in range(1, 4):
             dma([(T.n4[u::16, k * GW:(k + 1) * GW], T.nb[16 - k + u::16, :]) for u in range(k)], [], R("n4", k * GW, (k + 1) * GW))
         for s in DROT:
-            d = (4 * s + 7) % 16 - 7
-            rows = [(T.g4[u::16, s * GW:(s + 1) * GW], T.g4[(u + d) % 16::16, 0:GW]) for u in range(16) if not 0 <= u + d < 16]
+            rows = [(T.g4[u::16, s * GW:(s + 1) * GW], T.g4[u + 4 * s - 16::16, 0:GW]) for u in range(16 - 4 * s, 16)]
             dma(rows, [R("g4", 0, GW)], R("g4", s * GW, (s + 1) * GW))
+
     op("g", lambda q: q.affine_select(T.se[:, 16:2064], T.w1[:], [[-1024, 16], [16, 8], [1025, 16]], OP.is_equal, 0.0, 0, -1), [R("w1")], [R("se", 16, 2064)])
     iota(("jr",), [[4, 3], [32, 8], [1, 16]], 4, 0)
     ts(("pi", 1, 2), ("pi", 0, 1), 15, OP.bitwise_and)
@@ -268,9 +263,8 @@ def rank_program(g, core, T, topo):
     ts(("idn",), ("jf", 0, 128), ("pf", 0, 1), OP.is_equal)
     ts(("jt",), ("jj", 0, 128), 4, OP.arith_shift_right)
     ts(("bo",), ("jt",), GRP, OP.is_equal)
-    ts(("sz",), ("w1", 0, 432), 0.0, OP.mult)
-    for k, c in enumerate((1.0, -1.0, 2.0)):
-        ts(("sz", 144 * k + 15, 144 * k + 128, 16), ("bo", 0, 128, 16), c, OP.mult)
+    ts(("sz",), ("w1", 0, 144), 0.0, OP.mult)
+    cp(("sz", 15, 128, 16), ("bo", 0, 128, 16))
     for lo in (0, 2064):
         ts(("se", lo, lo + 16), ("w1", 0, 16), 0.0, OP.mult)
     ts(("u16",), ("jf", 0, 16), ROW, OP.is_equal)
@@ -287,10 +281,13 @@ def rank_program(g, core, T, topo):
         if tok[0] == "G":
             ts(("g4", k * H, k * H + H), ("gi", k * H, k * H + H), 1.0 + 2.0 ** -12, OP.mult, MAGIC, OP.add)
             act(("g4", k * H, k * H + H), ("g4", k * H, k * H + H), AF.Copy, bias=-(MAGIC + 2048.0))
-        elif tok[0] == "O":
-            cp(("o0",) + CUT[k][0:2], ("n4", 8 * CUT[k][0], 8 * CUT[k][1], 8))
-        elif tok[0] == "R":
-            cp(("r0",) + CUT[k][0:2], ("n4", 8 * CUT[k][0], 8 * CUT[k][1], 8))
+        elif tok[0] in "OR":
+            cp((tok[0].lower() + "0",) + CUT[k][0:2], ("n4", 8 * CUT[k][0], 8 * CUT[k][1], 8))
+        elif tok[0] == "Q":
+            s, lo = 1 + k // 4, 512 * (k % 4)
+            bank = ("pa", "pb")[k % 2]
+            mm((bank,), ("rt", (s - 1) * 128, s * 128), ("g16", lo, lo + 512))
+            cp(("g4", s * GW + lo, s * GW + lo + 512), (bank,), "a" if k in ROTA else "v")
         elif k == 0:
             fill(("wf", 0, 16), 0.5)
             fill(("wf", 16, 32), 0.0)
@@ -322,6 +319,7 @@ def rank_program(g, core, T, topo):
             ts(("b15",), ("bo",), ("pf", 8, 9), OP.mult, 2.0 ** 30, OP.mult)
             cp(("one",), ("w1", 0, 128))
         elif k == 5:
+            ts(("ibn",), ("idn",), -1.0, OP.mult)
             ts(("bm",), ("bo",), -1.0, OP.mult)
             ts(("b0",), ("bo",), ("pf", 9, 10), OP.mult)
             ts(("d5",), ("idn",), ("pf", 6, 7), OP.mult)
@@ -332,21 +330,12 @@ def rank_program(g, core, T, topo):
             ts(("l2",), ("jt",), ROW, OP.is_gt)
             tt(("lt",), ("l2",), ("bo",), OP.mult)
         else:
-            cp(("wn", OG, OG + L), ("o16",), "a")
-
-    def own_columns():
-        cp(("o16",), ("g4", 0, GW, 8), "a")
+            cp(("wn", OG, OG + L), ("o16",), "g")
 
     def turns():
         ts(("rt",), ("jr",), ("pf", 7, 8), OP.is_equal)
         ts(("r2",), ("jr",), -16.0, OP.add, ("pf", 7, 8), OP.is_equal)
         tt(("rt",), ("rt",), ("r2",), OP.add)
-
-    def turn(n):
-        s, lo = 1 + n // 4, 512 * (n % 4)
-        bank = ("pa", "pb")[n % 2]
-        mm((bank,), ("rt", (s - 1) * 128, s * 128), ("g16", lo, lo + 512))
-        cp(("g4", s * GW + lo, s * GW + lo + 512), (bank,), "a" if n in ROTA else "v")
 
     def turn_own():
         for s in range(1, 4):
@@ -356,6 +345,7 @@ def rank_program(g, core, T, topo):
 
     def run(tok, tau):
         gen, t = divmod(tau, ST)
+        last = t == ST - 1
         eng = "v" if tok[-1] == "v" else "a"
         tok, _, js = tok.rstrip("v").partition(".")
         kind = tok.rstrip("0123456789") if tok[0:2] not in ("M1", "M2") else tok[0:2]
@@ -367,8 +357,9 @@ def rank_program(g, core, T, topo):
         pe, pd, pn = "pe%d" % b, "pd%d" % b, "pl%d" % b
         e0 = c0 + sum(subs[0:int(js)]) if js else 0
         e1 = e0 + subs[int(js)] if js else 0
-        plain = js and (b, int(js)) in PLAIN
-        most = js and (b, int(js)) in MOST
+        plain = js and (b, int(js)) in (EDGE if last or t == 0 else PLAIN)
+        copies = [("t%d" % k, e0, e1) for k in (0, 1, 2, 3, 4, 8)]
+        spread = [("ed%d" % a, 0, 1) for a in range(16)]
         q = 3 * c0
         sco = (pd, 256, 256 + n)
         rp = (pn, 192, 192 + n)
@@ -380,12 +371,11 @@ def rank_program(g, core, T, topo):
         li = [("li", lb + k * lc, lb + (k + 1) * lc) for k in range(4)]
         ln = [("ln", LW * tau + r[1], LW * tau + r[2]) for r in li]
         cs = 5 * l0 + (4 * lc if b == 0 else 0)
+        put = ("lo", LW * tau + cs, LW * tau + cs + lc)
         ww = ("ww" if t else "w0", c0, c1)
         zz = "zz" if t else "z0"
         yi = ("yi", l0, l1)
-        last = t == ST - 1
-        if kind in ("RR", "WW", "MK", "PZ", "OM", "OF") and t == 0:
-            return
+        ao = L * tau
         if kind == "RR":
             cp(("rr", c0, c1), (("n4",), ln[0]))
         elif kind == "WW":
@@ -396,12 +386,12 @@ def rank_program(g, core, T, topo):
         elif kind == "OF":
             ts(("of", c0, c1), (pn, 0, n), -8192.0, OP.add)
         elif kind == "RP":
-            mm(rp, ("idn",), ("rr" if t else "r0", c0, c1))
+            if not last:
+                mm(rp, ("idn",), ("rr" if t else "r0", c0, c1))
         elif kind == "MK":
             cp(("m0", c0, c1), (("tm",), ln[2]), eng)
         elif kind == "NG":
-            if t:
-                tt(("ng", c0, c1), (("g4", 0, GW), ln[3]), ("m0", c0, c1), OP.mult)
+            tt(("ng", c0, c1), (("g4", 0, GW), ln[3]), ("m0", c0, c1), OP.mult)
         elif kind == "NM":
             for a in range(16):
                 mm((pn, 384, 384 + lc), onto(a) if t else move(0, a), ("ng" if t else "o16", c0 + a, c1, 16), a == 0, a == 15)
@@ -415,12 +405,12 @@ def rank_program(g, core, T, topo):
             for s in range(16):
                 mm((pe, e0 - c0, e1 - c0), move(s, s), ("eg", 16 * e0 + s, 16 * e1, 16), s == 0, s == 15)
         elif kind == "D":
-            an, ao = ("an", L * tau) if t or tau == 0 else ("ao", L * (tau - 1))
-            tt(("dd", c0, c1), (XR, nl), (an, ao + c0, ao + c1), OP.subtract)
+            an, o = ("an", ao) if t or tau == 0 else ("ao", ao - L)
+            tt(("dd", c0, c1), (XR, nl), (an, o + c0, o + c1), OP.subtract)
         elif kind == "DA":
             act(("tr", 16 * c0, 16 * c1, 16), ("dd", c0, c1), AF.Abs, tag=("t0", c0, c1))
         elif kind == "TA":
-            f0 = c0 + sum(m for j, m in enumerate(subs) if (b, j) in PLAIN)
+            f0 = c0 if b else c0 + subs[0]
             cp(("tr", 16 * f0 + 8, 16 * c1, 16), ("tr", 16 * f0, 16 * c1, 16), tag=("t8", f0, c1), more=[("t0", f0, c1)])
             cp(("tr", 16 * f0 + 4, 16 * c1, 8), ("tr", 16 * f0, 16 * c1, 8), tag=("t4", f0, c1), more=[("t0", f0, c1), ("t8", f0, c1)])
         elif kind == "TB":
@@ -429,30 +419,30 @@ def rank_program(g, core, T, topo):
         elif kind == "XL":
             ts(("xl", e0, e1), (pe, e0 - c0, e1 - c0), 2048.0, OP.add)
         elif kind == "X":
+            out = ("uu", 16 * e0, 16 * e1)
             if plain:
-                cp(("uu", 16 * e0, 16 * e1), (XR, ("xl", e0, e1)), eng)
+                cp(out, (XR, ("xl", e0, e1)), eng)
             else:
-                tt(("uu", 16 * e0, 16 * e1), (XR, ("xl", e0, e1)), ("tr", 16 * e0, 16 * e1), OP.add, more=[("t%d" % k, e0, e1) for k in (0, 1, 2, 3, 4, 8)])
+                tt(out, (XR, ("xl", e0, e1)), ("tr", 16 * e0, 16 * e1), OP.add, more=copies)
         elif kind in ("PA", "PB"):
-            for s in range(8):
+            h = int(kind == "PB")
+            if b:
+                mm((kind.lower(),), ("idn",), ("uu", 16 * e0 + h, 16 * e1, 2), True, False)
+                mm((kind.lower(),), ("ib",), ("tr", 16 * e0 + h, 16 * e1, 2), False, True, copies)
+            for s in range(0 if b else 8):
                 o = (kind.lower(), 64 * s, 64 * s + 64)
-                mm(o, ("idn",), ("uu", 16 * e0 + s + 8 * (kind == "PB"), 16 * e1, 16), True, False)
+                mm(o, ("idn",), ("uu", 16 * e0 + s + 8 * h, 16 * e1, 16), True, False)
                 mm(o, ("ib",), ("tr", 16 * e0, 16 * e1, 16), False, True, [("t0", e0, e1)])
-        elif kind == "AB":
-            if plain:
-                for h in range(2):
-                    act(("ab", 16 * e0 + 512 * h, 16 * e0 + 512 * h + 512), (("pa", "pb")[h],), AF.Abs, bias=-255.0)
-            elif most:
-                ts(("ab", 16 * e0, 16 * e1), ("uu", 16 * e0, 16 * e1), 255.0, OP.max, -127.5, OP.add)
-            else:
-                act(("ab", 16 * e0, 16 * e1), ("uu", 16 * e0, 16 * e1), AF.Abs, bias=-255.0)
-        elif kind == "AU":
-            for s in range(16):
-                mm((pd, e0 - c0, e1 - c0), onto(s, 1), ("uu", 16 * e0 + s, 16 * e1, 16), s == 0, False)
-        elif kind == "AM":
-            for s in range(16):
-                rhs = ("ab", 16 * e0 + 64 * s, 16 * e0 + 64 * s + 64) if plain else ("ab", 16 * e0 + s, 16 * e1, 16)
-                mm((pd, e0 - c0, e1 - c0), onto(s, 2 if most else 0), rhs, s == 0 and not most, s == 15)
+        elif kind in ("AB", "AC"):
+            h = int(kind == "AC")
+            src = (("pa", "pb")[h],) if plain else ("uu", 16 * e0 + h, 16 * e1, 2)
+            act(("ab", 8 * (e0 + (e1 if h else e0)), 8 * (e1 + (e1 if h else e0))), src, AF.Abs, bias=-255.0)
+        elif kind in ("AM", "AN"):
+            h = int(kind == "AN")
+            o, m = 8 * (e0 + (e1 if h else e0)), e1 - e0
+            for s in range(8):
+                rhs = ("ab", o + s, o + 8 * m, 8) if e0 else ("ab", o + m * s, o + m * s + m)
+                mm((pd, e0 - c0, e1 - c0), onto(2 * s + h if e0 else 8 * h + s), rhs, s + h == 0, s + h == 8)
         elif kind == "GO":
             if eng == "a":
                 act((pd, 0, n), (pd, 0, n), AF.Relu, bias=("lim",), scale=-1.0)
@@ -465,13 +455,11 @@ def rank_program(g, core, T, topo):
         elif kind == "PF":
             tt(("ff", c0, c1), ("ok", c0, c1), sco, OP.is_gt)
         elif kind == "PW":
-            if eng == "a":
-                act(("qq", q + 2 * n, q + 3 * n), ("ff", c0, c1), AF.Copy, scale=("pf", 5, 6))
-            else:
-                ts(("qq", q + 2 * n, q + 3 * n), ("ff", c0, c1), ("pf", 5, 6), OP.mult)
+            times(eng, ("qq", q + 2 * n, q + 3 * n), ("ff", c0, c1), ("pf", 5, 6))
         elif kind == "PQ":
             tt(("qq", q, q + n), ("ff", c0, c1), (pe, 0, n), OP.mult)
-            tt(("qq", q + n, q + 2 * n), ("ff", c0, c1), rp, OP.mult)
+            if not last:
+                tt(("qq", q + n, q + 2 * n), ("ff", c0, c1), rp, OP.mult)
         elif kind == "PC":
             for a in range(16):
                 mm((pn, 400, 400 + 3 * lc), onto(a), ("qq", q + a, q + 3 * n, 16), a == 0, a == 15)
@@ -485,8 +473,9 @@ def rank_program(g, core, T, topo):
                 ts(("yy", c0, c1), (pd, 0, n), 0.0, OP.max)
         elif kind == "M1":
             tt(("ti", l0, l1), ls, (zz, 2 * l0, 2 * l0 + lc), OP.max)
-            tt(("ti", 16 + l0, 16 + l1), lr, (zz, 2 * l0 + lc, 2 * l1), OP.add)
-            tt(yi, ("ti", l0, l1), ("ti", 16 + l0, 16 + l1), OP.add)
+            if not last:
+                tt(("ti", 16 + l0, 16 + l1), lr, (zz, 2 * l0 + lc, 2 * l1), OP.add)
+            tt(yi, ("ti", l0, l1), (zz, 2 * l0 + lc, 2 * l1) if last else ("ti", 16 + l0, 16 + l1), OP.add)
         elif kind == "ML":
             o = LW * tau
             ts(li[2], yi, 11, OP.arith_shift_right, 15, OP.bitwise_and)
@@ -494,7 +483,7 @@ def rank_program(g, core, T, topo):
                 ts(li[0], yi, 8191, OP.bitwise_and)
             tt(("li", cs, cs + lc), li[2], ("cb", l0, l1), OP.add)
             if last:
-                cp(("lo", o + cs, o + cs + lc), ("li", cs, cs + lc))
+                cp(put, ("li", cs, cs + lc))
             else:
                 for k, m in ((3, 2047), (1, 24576)):
                     ts(li[k], yi, m, OP.bitwise_and)
@@ -503,83 +492,70 @@ def rank_program(g, core, T, topo):
         elif kind == "XO":
             ts(xo, le, 2048.0, OP.add)
         elif kind == "M2":
-            ao = L * tau
             tt(("ao", ao + c0, ao + c1), (XR, xo), ("yy", c0, c1), OP.max)
             if not last:
                 send(nxt, "ao", ao + c0, ao + c1, "an", ao + L + c0, "ar%d_%d" % (tau, b))
-        elif kind == "ST":
-            o = LW * tau + CUT[0][1] // 4
-            cp((XR, ("lo", o, o + 16)), ("ao", L * tau, L * tau + L))
         elif kind == "HI":
-            if t in (1, 2, 3):
-                send(T.cores[(rank - t) % N], "ho", 32 * tau, 32 * tau + 32, "hn", 32 * tau, "h%d" % tau)
-        elif kind in ("CA", "CB", "CC", "CD", "CE"):
-            if tau == TAU - 1:
-                return
-            if kind == "CA":
-                ts(("hc",), (hist, 32 * tau, 32 * tau + 16), float(ZC), OP.is_equal)
-                mm(("pa", 256, 272), ("one",), ("hc",))
-            elif kind == "CB":
-                total(("af",), ("pa", 256, 272))
-            elif kind == "CC":
-                cp(("ai", 0, 1), ("af",))
-            elif kind == "CD":
-                ts(("ai", 1, 2), ("ai", 0, 1), 63, OP.bitwise_and)
-            else:
-                ts(("lim",), ("ai", 1, 2), ("thf",), OP.add)
-        elif not last:
+            send(T.cores[(rank - t) % N], "ho", 32 * tau, 32 * tau + 32, "hn", 32 * tau, "h%d" % tau)
+        elif kind in ("ST", "CA", "CB", "CC", "CD", "CE") and tau == TAU - 1:
             return
+        elif kind == "ST":
+            cp((XR, ("lo", put[1], put[1] + 16)), ("ao", ao, ao + L))
+        elif kind == "CA":
+            ts(("hc",), (hist, 32 * tau, 32 * tau + 16), float(ZC), OP.is_equal)
+            mm(("pa", 256, 272), ("one",), ("hc",))
+        elif kind == "CB":
+            total(("af",), ("pa", 256, 272))
+        elif kind == "CC":
+            cp(("ai", 0, 1), ("af",))
+        elif kind == "CD":
+            ts(("ai", 1, 2), ("ai", 0, 1), 63, OP.bitwise_and)
+        elif kind == "CE":
+            ts(("lim",), ("ai", 1, 2), ("thf",), OP.add)
         elif kind == "EE":
             o = 32 * ST * gen
             ts(("hv",), ("hn", o, o + 128), -2048.0, OP.add)
             ts(("hf",), ("hv",), 0.0, OP.is_equal)
             tt(("hm", 0, 112), ("hf", 0, 112), ("hv", 16, 128), OP.mult)
             tt(("e1",), ("hf", 0, 48), ("hf", 64, 112), OP.add)
-            tt(("hw", 0, 112), ("hv", 0, 112), ("hm", 0, 112), OP.add)
-            tt(("er",), ("e1", 0, 16), ("e1", 32, 48), OP.add)
+            for s in range(4):
+                tt(("hw", 16 * s, 16 * s + 16), ("hv", 32 * s, 32 * s + 16), ("hm", 32 * s, 32 * s + 16), OP.add)
+            tt(("hw", 64, 80), ("e1", 0, 16), ("e1", 32, 48), OP.add)
+        elif kind in ("EH", "EI", "EJ", "EL"):
+            for a in range("HIJL".index(kind[1]), 16, 4):
+                times(eng, ("ed", a, 5 * L, 16), ("hw",), ("u16", a, a + 1), spread[a])
         elif kind == "EF":
             mm(("pa", 0, L), ("b0",), ("on",), True, False)
-            for a in range(16):
-                mm(("pa", a, L, 16), move(a, 0), ("er",), False, a == 15)
-            cp(("eb",), ("pa", 0, L), "a")
-        elif kind in ("EG", "EH", "EI", "EJ"):
-            s = "GHIJ".index(kind[1])
-            if s == 0:
-                mm(("pb", 0, L), ("d5",), ("o16",), True, False)
-            for a in range(16):
-                mm(("pb", a, L, 16), move(a, s), ("hw", 32 * s, 32 * s + 16), False, False)
+            mm(("pa", 0, L), ("bo",), ("ed", 4 * L, 5 * L), False, False, spread)
+        elif kind == "EG":
+            mm(("pb", 0, L), ("d5",), ("o16",), True, False)
+            for s in range(4):
+                mm(("pb", 0, L), onto(s), ("ed", s * L, s * L + L), False, False, spread)
         elif kind == "FL":
             fl = (pe, 256, 256 + n)
             mm(fl, ("b0",), ("on", c0, c1), True, False)
             mm(fl, ("bm",), ("ff", c0, c1), False, True)
             tt(("nf", c0, c1), ("ng", c0, c1), fl, OP.mult)
-        elif kind == "SA":
-            mm(("pa", 0, L), ("b0",), ("eb",), True, False)
-            mm(("pa", 0, L), ("bm",), ("ff",), False, True)
+        elif kind == "SH":
             for c0, c1, _ in CUT:
                 mm(("pb", c0, c1), onto(4), ("qq", 3 * c0, 2 * c0 + c1), False, False)
             mm(("pb", 0, L), onto(4), ("nf",), False, True)
-            ts(("ind",), ("pa", 0, L), ROW, OP.is_equal)
         elif kind == "SG":
             if gen < GENS - 1:
                 cp(("da",), ("pb", 0, L), "a")
             else:
                 ts(("fo", 0, L), ("pb", 0, L), 0.0, OP.is_le, 2047.0, OP.add)
                 tt(("da",), ("fo", 0, L), ("pb", 0, L), OP.add)
-        elif kind == "EK":
-            if gen == GENS - 1:
-                ts(("x1",), ("o16",), 0.0, OP.is_le, 2047.0, OP.add)
-                tt(("wn", OG, OG + L), ("x1",), ("o16",), OP.add)
-        elif kind == "RS":
-            if gen == GENS - 1:
-                registers_and_sums()
+        elif kind == "SA":
+            mm(("pa", 0, L), ("bm",), ("ff",), False, True)
+            ts(("ind",), ("pa", 0, L), ROW, OP.is_equal)
         elif kind == "SD":
             scan(("pre",), ("on",), ("ind",), 0.0)
             mm(("pa", 300, 301), ("lt",), ("pre", L - 1, L))
         elif kind == "SE":
-            ts(("x1",), ("pre",), ("pa", 300, 301), OP.add, -1.0, OP.add)
+            ts(("pa", 0, L), ("pre",), ("pa", 300, 301), OP.add, -1.0, OP.add)
         elif kind == "SF":
-            tt(("x2",), ("x1",), ("ind",), OP.mult)
+            tt(("x2",), ("ind",), ("pa", 0, L), OP.mult)
             for a in range(16):
                 mm(("pa", 320, 336), onto(a), ("x2", a, L, 16), a == 0, a == 15)
         elif kind == "SB":
@@ -596,45 +572,47 @@ def rank_program(g, core, T, topo):
             tt(("kf", 48, 64), ("kf", 32, 48), ("kf", 16, 32), OP.add)
             tt(("kf", 0, 16), ("kf", 48, 64), ("ob",), OP.min)
             ts(("pr",), ("kf", 0, 16), float(OG - w), OP.add)
+        elif kind == "SN":
+            cp(("g4", 0, GW, 8) if gen < GENS - 1 else ("fo", 0, L), (("wn", min(SR, BI[gen]), OG + L), ("pr",)))
+            if gen == GENS - 1:
+                dma([(T.yg[:], T.fo[:, 0:L])], [R("fo", 0, L)], None, True)
+        elif gen < GENS - 1:
+            return
+        elif kind == "EK":
+            ts(("x1",), ("o16",), 0.0, OP.is_le, 2047.0, OP.add)
+            tt(("wn", OG, OG + L), ("x1",), ("o16",), OP.add)
+        elif kind == "YS":
+            for h in range(2):
+                o = h * (ZC + 1)
+                for s in range(16):
+                    mm(("pa", 128 * h, 128 * h + 128), ("ib",), ("xr", o + s, o + ZC, 16), s == 0, s == 15)
+            cp(("fo", 2 * L, 3 * L), ("pa", 0, L), "a")
+        elif kind == "YO":
+            cp(("dd", c0, c1), (XR, put), eng)
+        elif kind == "YD":
+            mm((pe, 0, n), ("ib",), ("ao", ao + c0, ao + c1), True, False)
+            mm((pe, 0, n), ("ibn",), ("dd", c0, c1), False, True)
+            tt(("fo", 2 * L + c0, 2 * L + c1), ("fo", 2 * L + c0, 2 * L + c1), (pe, 0, n), OP.add)
+        elif kind == "YE":
+            dma([(T.ys[:], T.fo[:, 2 * L:3 * L])], [R("fo", 2 * L, 3 * L)], None, True)
+        elif kind == "YA":
+            cp(("fo", L, 2 * L), ("ao", ao, ao + L), "a")
+            dma([(T.ya[:], T.fo[:, L:2 * L])], [R("fo", L, 2 * L)], None, True)
 
-    def registers_and_sums():
-        cp(("fo", L, 2 * L), ("ao", L * (TAU - 1), L * TAU), "a")
-        dma([(T.ya[:], T.fo[:, L:2 * L])], [R("fo", L, 2 * L)], None, True)
-        for h in range(2):
-            o = h * (ZC + 1)
-            for s in range(16):
-                mm(("pe0", 128 * h, 128 * h + 128), ("ib",), ("xr", o + s, o + ZC, 16), s == 0, s == 15)
-        cp(("fo", 2 * L, 3 * L), ("pe0", 0, L), "a")
-        dma([(T.ys[:], T.fo[:, 2 * L:3 * L])], [R("fo", 2 * L, 3 * L)], None, True)
-
+    once = {"RT": turns, "RA": turn_all, "RB": turn_rest, "OT": turn_own,
+            "GC": lambda: cp(("g16", 0, GW), ("g4", 0, GW), "g"), "OW": lambda: cp(("o16", 0, L), ("g4", 0, GW, 8), "g")}
     for tau in range(TAU):
-        gen, t = divmod(tau, ST)
+        t = tau % ST
         for tok in (LAST if t == ST - 1 else ORDER if t else AGAIN if tau else FIRST):
-            if tok[0] == "Q":
-                turn(int(tok[1:]))
-            elif tok[0] in "GORL" and tok[1:].isdigit():
+            if tok[0] in "GORLQ" and tok[1:].isdigit():
                 prepare(tok)
-            elif tok == "RT":
-                turns()
-            elif tok == "RA":
-                turn_all()
-            elif tok == "RB":
-                turn_rest()
-            elif tok == "GC":
-                cp(("g16", 0, GW), ("g4", 0, GW), "g")
-            elif tok == "OW":
-                own_columns()
-            elif tok == "OT":
-                turn_own()
-            elif tok[-1] != "'":
-                run(tok, tau)
-            elif t < ST - 1:
+            elif tok in once:
+                once[tok]()
+            elif tok[-1] == "'":
                 run(tok[0:-1], tau + 1)
-        if t == ST - 1:
-            new = (("wn", min(SR, BI[gen]), OG + L), ("pr",))
-            cp(("g4", 0, GW, 8) if gen < GENS - 1 else ("fo", 0, L), new)
+            else:
+                run(tok, tau)
 
-    dma([(T.yg[:], T.fo[:, 0:L])], [R("fo", 0, L)], None, True)
     for i in range(nd[0]):
         if known["s"].get("d%d" % i, 0) < 16:
             g.sync.wait_ge(T.sem["d%d" % i], 16)

@@ -7,52 +7,49 @@ ZC = 2048
 MAGIC = 12582913.0
 TAU = GENS * ST
 CUT = [(0, 128, (64, 64)), (128, 256, (64, 64))]
-PLAIN = ((0, 0), (1, 0))
-EDGE = ((0, 0),)
-DMAS = 32
-LW = 80
+DMAS = 24
+DROT = (1, 3)
+LW = 64
 SR, BI, OG = 64, (320, 0), 384
-DROT = (1,)
-ROTA = (5, 6, 7, 8, 11)
-TBQ = ("", "vvg", "gav", "ggg")
-FIRST = """G0 G1 G2 G3 RA RB O0 E0.0 L0 OW E0.1v R0 NM0 F0.0 NL0 XL0.0 X0.0 NM1 D0 DA0 L1 NL1 D1 GC L2 O1 F0.1 L3 DA1 PB0.0 XL0.1 TA0 TA1 TB0.1
- PA0.0 RT E1.1 F1.1 E1.0 X0.1 AB0.0 F1.0 AC0.0 RP0 AM0.0 XL1.1 TB1.1 AB0.1 AC0.1 AN0.0 AM0.1 L4 AN0.1 X1.1 XL1.0 GO0 AB1.1 GV0 TB1.0 GM0
- PF0 PW0 AC1.1 AM1.1 PQ0 Q5 PC0 X1.0 M10 AB1.0 XO0 AC1.0 ML0 AN1.1 Q7 Q4 AM1.0 L6 AN1.0 GO1v Q6 GV1 Q9 GM1 Q8 Q11 YM1 R1 PF1 PW1 RP1 PQ1
- Q10 YM0 PC1 YY1 YY0 M20 RR0' L7 WW0' MK0' OM0' XO1 M11 OF0' E0.0' CA M21 NG0' CB E0.1' NM0' ML1 CC L5 CD RP0' F0.0' ST NL0' XL0.0'
- F0.1' CE""".split()
-ORDER = """D0 RR1 WW1v MK1v OM1 DA0 X0.0 NG1 OF1 NM1 PZ0 E1.0 TA0 PZ1 TB0.1 NL1 XL0.1 D1 PB0.0 DA1 X0.1 PA0.0 F1.0 AC0.0 AB0.0 RP1 AM0.0 AN0.0
- TA1 AB0.1 AM0.1 XL1.0 AC0.1 E1.1v AN0.1 GO0v X1.0 F1.1 GV0 GM0 TB1.0 PF0 PB1.0 TB1.1 XL1.1 PW0 AC1.0 PA1.0 PQ0 X1.1 AB1.0 AB1.1 AC1.1 PC0
- AM1.0 AN1.0 M10 ML0 AM1.1 AN1.1 GO1v YM0 XO0 GV1 GM1 PF1 YY0 PQ1 WW0' RR0' YM1 PW1v OM0' PC1 M20 MK0' OF0' YY1 RP0' NG0' M11 NM0' XO1
- ML1 CA M21 CB E0.0' E0.1' NL0' HI CC ST CD F0.0' XL0.0' CE F0.1'""".split()
-LAST = """RR1 D0 WW1v OM1 MK1v NG1 OF1 X0.0 DA0 E1.0 NM1 PB0.0 TA0 TB0.1 NL1 D1 XL0.1 DA1 E1.1 TA1 TB1.0 F1.0 PA0.0 AB0.0 XL1.0 F1.1 X0.1 AC0.0
- X1.0 AC0.1 AM0.0 AB0.1 XL1.1 AC1.0 AB1.0 TB1.1 YS AN0.0 X1.1 AM0.1 AN0.1 AB1.1 AM1.0 GO0 AN1.0 EE GV0 AC1.1 AM1.1 GM0 EL EJv EIv AN1.1
- PF0 GO1v EH YM0 GV1 FL0 GM1 PF1 EF PW0 PQ0 PQ1 SA EG YY0 SD PZ1 SE FL1 PC0 PZ0 PW1 SH SF M10 XO0 PC1 ML0 YO0 M20 SG SB XO1 EK YM1 M11
- YY1 CA M21 CB YA ML1 YO1 YD0 CC SC ST YD1 YE CD SN CE""".split()
-AGAIN = """E0.0 OW E1.0v NM0 NM1 NL0 D0 NL1 D1 DA0 F0.0 TA0 XL0.0 E0.1 F1.0 X0.0v DA1 F0.1 XL0.1 RP0 PA0.0 E1.1 AB0.0 PB0.0 TB0.1 F1.1 TA1 X0.1
- TB1.0 AC0.0 XL1.0 AM0.0 X1.0 AN0.0 AB0.1 AC0.1 AM0.1 AN0.1 GO0 GV0 GM0 AB1.0 XL1.1 PF0 PW0 AC1.0 PQ0 TB1.1 X1.1 AM1.0 AB1.1 YM0 PC0 AC1.1
- AN1.0 M10 ML0 OT AM1.1 AN1.1 GO1v GV1 YY0 GM1 XO0 WW0' PF1 RP1 RR0' YM1 PW1 PQ1 OM0' M20 OF0' MK0' PC1 YY1 NG0' E0.0' NM0' RP0' M11 XO1
- ML1 CA F0.0' M21 CB ST CC NL0' CD XL0.0' CE E0.1' F0.1'""".split()
+FIRST = """G0 G1 G2 G3 RA OWg NM0 O0 E0.0 C0g L7 F0.0 L1 L0 O1 E1.0 NM1 E0.1v NL0 XL0.0 F1.0 D0 DA0 F0.1 X0.0v TA0.1 PB0.0 T20.1g PA0.0 NL1 T10.1g
+ T30.1v D1 E1.1 XL0.1 L8 X0.1 AC0.0 AN0.0 AC0.1v AB0.0 DA1 AB0.1 XL1.0 AM0.0 L3 L2 TA1.1g X1.0 AV0.1 AN0.1 AM0.1 R0 F1.1 T21.1g GO0v RP0 GV0
+ T11.1v GM0 XL1.1 T31.1 PA1.0 PF0 PW0 C1 PQ0 AB1.0 R1 C3 X1.1.1 PC0 PB1.0 M10 ML0 AM1.0 YM0 X1.1.0 YY0v AC1.0 AB1.1v AN1.0 RT AU1.1 L4 AC1.1
+ AM1.1 XO0 AN1.1 Q4 GO1v GV1 RP1 Q1 M20 GM1 PF1 C2 PW1v PQ1 Q10v UC0' YM1 YY1 PC1 WW0' RR0' XO1 Q7 OM0' CA M11 CB OF0' E0.0' RP0' MK0v' ML1
+ E0.1' NG0' CC CE M21 CS NM0' NL0' F0.0' ST XL0.0' F0.1'""".split()
+ORDER = """D0 DA0 PZ0 UC1 WW1v X0.0 RR1 MK1v NG1 TA0.1g T10.1g OM1 OF1 T20.1v NM1 E1.0 E1.1.0v NL1 PB0.0 XL0.1 D1 PA0.0 AC0.0 T30.1g X0.1 AB0.0 DA1 F1.0
+ AN0.0 AB0.1 XL1.0 AC0.1v E1.1.1v AM0.0 AV0.1 TA1.1g AN0.1 AM0.1 L6 GO0v GV0 PZ1 F1.1 GM0 T31.1g L9 T11.1v X1.0 PA1.0 XL1.1 PF0 T21.1 PW0
+ AB1.0 YM0 PQ0 X1.1.0 PB1.0 PC0 X1.1.1 AC1.0 AM1.0 AN1.0 M10 ML0 XO0 AB1.1v AC1.1 AU1.1 AN1.1 L5 YY0 AM1.1 GO1v GV1 RP1 GM1 M20 PF1 UC0' RR0'
+ YM1 WW0' OM0' PW1 MK0' PQ1 OF0' E0.0' PC1 YY1v NG0' RP0' M11 ML1 NM0' XO1 E0.1.1' CA CB M21 HI CS NL0' ST CC F0.0' XL0.0' CE E0.1.0' F0.1'""".split()
+LAST = """D0 UC1 DA0 WW1v RR1 OM1 MK1v NG1 OF1 X0.0 PZ0 NM1 XL0.1 E1.0 E1.1v NL1 PB0.0 AC0.0 PA0.0 F1.0 AB0.0 EE TA0.1g T20.1g T30.1g D1 DA1 EC EG
+ XL1.0 X1.0 T10.1g X0.1 AN0.0 F1.1 AM0.0 TA1.1g AC0.1 T21.1v XL1.1 PA1.0 T11.1g T31.1v AB0.1 PZ1 PB1.0 AN0.1 AB1.0 X1.1 AM0.1 AC1.0 AC1.1
+ AM1.0 EI0v GO0v AN1.0 ED AB1.1 AN1.1 GV0 GM0 AM1.1 EK PF0 GO1v GV1 EF EI2 EI1 PQ0 PW0v GM1 YM0 PF1 PQ1 EI3 FL0 SA PW1 YM1 FL1 EJ SD PY PC2 SH
+ SE SF M12 SGv SB ML2 XO2 YY0 CA YY1 CB CS YO2 M22 SC YAv YS CC YD1 CE YD0 YE SMv SN RP0' OW' E0.1' E0.0v' ST NM0'""".split()
+AGAIN = """NL0 E1.0 NM1 NL1 D0 DA0 F0.0 XL0.0 D1 F0.1 DA1 F1.0 TA0.1 X0.0v PA0.0 PB0.0 XL0.1 T10.1g T20.1v E1.1 T30.1v XL1.0 X0.1 AB0.0 F1.1 X1.0v XL1.1
+ TA1.1g AC0.0 T21.1v T11.1g AN0.0 AM0.0 AB0.1 AM0.1 AC0.1 AN0.1 PA1.0 AB1.0 GO0v GV0 GM0 YM0 PB1.0 T31.1g X1.1.0 PF0 AM1.0 PQ0 X1.1.1 YY0v PW0
+ PC0 M10 AC1.0 XO0 RP1 AN1.0 ML0 OT2v AC1.1 AN1.1 AB1.1 M20 AM1.1 OT1 GO1v GV1 UC0' GM1 PF1 WW0' PW1 OT3 YM1 RR0' OM0' PQ1 YY1 OF0' MK0v' PC1
+ NG0' E0.0' M11 XO1 ML1 RP0' NM0' CA M21 CS F0.0' NL0' ST CB CC XL0.0' E0.1' F0.1' CE""".split()
 
 SCRATCH = {}
 for _n, _w, _d in (
         ("gi", GW, "int32"), ("g4", 4 * GW, "float32"), ("n4", 4 * GW, "int32"), ("g16", GW, "float16"), ("xr", XW + 16, "bfloat16"), ("w1", GW, "bfloat16"),
         ("eg", 16 * L, "float16"), ("uu", 16 * L, "float16"), ("ab", 16 * L, "float16"), ("tr", 16 * L, "bfloat16"),
-        ("rr", L, "float16"), ("ww", L, "bfloat16"), ("m0", L, "bfloat16"), ("of", L, "uint16"), ("ng", L, "float16"), ("nf", L, "float16"),
+        ("rr", L, "float16"), ("ww", L, "bfloat16"), ("m0", L, "bfloat16"), ("of", L, "uint16"), ("nf", L, "float16"),
         ("r0", L, "float16"), ("o0", L, "uint16"), ("w0", L, "bfloat16"), ("dd", L, "bfloat16"), ("xl", L, "uint16"),
-        ("ok", L, "bfloat16"), ("ff", L, "float16"), ("qq", 3 * L, "float16"), ("yy", L, "bfloat16"), ("ti", 32, "float32"),
-        ("yi", 16, "int32"), ("li", LW, "int32"), ("zz", 32, "float32"), ("z0", 32, "float32"), ("cb", 16, "float32"),
-        ("lo", LW * TAU, "uint16"), ("ln", LW * TAU, "uint16"), ("ao", L * TAU, "bfloat16"), ("an", L * TAU, "bfloat16"),
-        ("ho", 32 * TAU, "uint16"), ("hn", 32 * TAU, "uint16"), ("hv", 128, "float16"), ("hf", 128, "float16"), ("hm", 128, "float16"), ("hw", 80, "float16"),
-        ("hc", 16, "float16"), ("e1", 48, "float16"), ("ed", 5 * L, "float16"),
+        ("ok", L, "bfloat16"), ("ff", L, "float16"), ("qq", 4 * L, "float16"), ("ti", 32, "float32"), ("yy", L, "bfloat16"),
+        ("yi", 16, "int32"), ("zz", 32, "float32"), ("z0", 16, "float32"), ("cb", 16, "float32"), ("c2", 24, "float16"),
+        ("li", LW * TAU, "int32"), ("lm", LW * TAU, "int32"), ("lo", 16 * TAU, "uint16"), ("ln", LW * TAU, "uint16"), ("ao", L * TAU, "bfloat16"), ("an", L * TAU, "bfloat16"),
+        ("ho", 32 * TAU, "uint16"), ("hn", 32 * TAU, "uint16"), ("hv", 128, "float16"), ("hf", 128, "float16"), ("hm", 128, "float16"), ("hw", 128, "float16"),
+        ("hc", 16, "float16"), ("e1", 48, "float16"), ("sa", 2048, "float16"), ("ed", 7 * L, "float16"),
         ("wn", OG + L, "float32"), ("da", L, "float32"), ("o16", L, "float16"), ("ind", L, "float16"), ("pre", L, "float16"), ("on", L, "float16"),
-        ("x1", L, "float16"), ("x2", L, "float16"), ("pl", 16, "uint16"), ("pr", 16, "uint16"), ("kr", 32, "int32"), ("kf", 64, "float32"), ("ob", 16, "float32"),
-        ("af", 1, "float32"), ("ai", 2, "int32"), ("lim", 1, "float32"), ("thi", 1, "int32"), ("thf", 1, "float32"),
+        ("x1", L, "float16"), ("x2", L, "float16"), ("pl", 16, "uint16"), ("pr", 16, "uint16"), ("kf", 64, "float32"), ("ob", 16, "float32"),
+        ("af", 1, "float32"), ("ai", 1, "int32"), ("lim", 1, "float32"), ("thi", 1, "int32"), ("thf", 2, "float32"),
         ("jj", L, "int32"), ("jf", L, "float32"), ("jt", 128, "int32"), ("kb", 32, "int32"), ("wf", 64, "float32"),
         ("pi", 4, "int32"), ("pf", 16, "float32"), ("u16", 16, "float32"), ("tw", 16, "bfloat16"), ("tm", 16, "bfloat16"),
-        ("se", 2048 + 32, "float16"), ("sz", 144, "float16"), ("idn", 128, "float16"), ("ib", 128, "bfloat16"), ("ibn", 128, "bfloat16"),
+        ("se", 2048 + 32, "float16"), ("sz", 144, "float16"), ("sz2", 144, "float16"), ("szn", 144, "float16"),
+        ("km", 32, "int32"), ("idn", 128, "float16"), ("ib", 128, "bfloat16"), ("ibn", 128, "bfloat16"),
         ("bo", 128, "float16"), ("bm", 128, "float16"), ("bh", 128, "bfloat16"), ("bn", 128, "bfloat16"), ("b15", 128, "bfloat16"), ("b0", 128, "float16"),
         ("d5", 128, "float16"), ("lt", 128, "float16"), ("l2", 128, "float16"), ("one", 128, "float16"),
-        ("rt", 384, "float16"), ("r2", 384, "float16"), ("jr", 384, "int32"), ("fo", 3 * L, "float32")):
+        ("rt", 384, "float16"), ("r2", 384, "float16"), ("jr", 384, "bfloat16"), ("fo", 3 * L, "float32")):
     SCRATCH[_n] = ("sbuf", [128, _w], _d)
 PSUM = ["pe0", "pe1", "pd0", "pd1", "pl0", "pl1", "pa", "pb"]
 for _n in PSUM:
@@ -72,7 +69,8 @@ def rank_program(g, core, T, topo):
     known = {q: {} for q in queues}
     clock = {}
     wr, rd = {}, {}
-    nd = [0]
+    nd = []
+    open_ = {}
     locs = [0]
 
     def R(name, lo=0, hi=None):
@@ -116,19 +114,13 @@ def rank_program(g, core, T, topo):
 
     def dma(pairs, reads, reg, out=False):
         need("s", reads, [] if out else [reg])
-        toks = []
+        s = "d%d" % len(nd)
         for o, src in pairs:
-            s = "d%d" % nd[0]
-            nd[0] += 1
             g.sync.dma_start(o, src).then_inc(T.sem[s], 16)
-            clock[(s, 16)] = dict(known["s"])
-            toks.append((s, (s, 16)))
-        for s, tok in toks:
-            if len(pairs) > 1:
-                wr[reg[0]] = list(wr.get(reg[0], ())) + [reg[1:3] + (s, tok)]
-                note(s, reads, [], tok)
-            else:
-                note(s, reads, [] if out else [reg], tok)
+        tok = (s, 16 * len(pairs))
+        nd.append(tok)
+        clock[tok] = dict(known["s"])
+        note(s, reads, [] if out else [reg], tok)
 
     def send(dst, name, lo, hi, to, lo2, sem):
         need("g", [(name, lo, hi)], [])
@@ -190,15 +182,9 @@ def rank_program(g, core, T, topo):
         c, ic = sc(scale)
         op("a", lambda s: s.activation(o, a, f, bias=b, scale=c), ia + ib + ic, [tag] if tag else io)
 
-    def times(q, out, src, c, tag=None):
-        if q == "a":
-            act(out, src, AF.Copy, scale=c, tag=tag)
-        else:
-            ts(out, src, c, OP.mult, tag=tag)
-
-    def iota(out, pattern, base, ch):
+    def iota(out, pattern, base, ch, **kw):
         o, io = side(out)
-        op("g", lambda q: q.iota(o, pattern, base, ch), [], io)
+        op("g", lambda q: q.iota(o, pattern, base, ch, **kw), [], io)
 
     def fill(out, c):
         o, io = side(out)
@@ -216,8 +202,12 @@ def rank_program(g, core, T, topo):
         b, ib = side(rhs)
         op("p", lambda t: t.matmul(o, a, b, start, stop), ia + ib + list(more), io)
 
-    def onto(a):
-        return ("sz", 15 - a, 143 - a)
+    def acc(key, whole, out, lhsT, rhs):
+        open_[key] = open_.get(key, 0) + 1
+        mm(out, lhsT, rhs, open_[key] == 1, open_[key] == whole)
+
+    def onto(a, m="sz"):
+        return (m, 15 - a, 143 - a)
 
     def move(a, b):
         return ("se", 16 + 129 * a - b, 144 + 129 * a - b)
@@ -232,29 +222,23 @@ def rank_program(g, core, T, topo):
         dma([(T.gi[:, lo:lo + H], T.gn[:, lo:lo + H])], [], R("gi", lo, lo + H))
     h = 8 * CUT[0][1]
     dma([(T.n4[:, 0:h], T.nb[:, 0:h])], [], R("n4", 0, h))
-    dma([(T.an[:, 0:L], T.a0[:])], [], R("an", 0, L))
+    dma([(T.n4[:, h:GW], T.nb[:, h:GW])], [], R("n4", h, GW))
     dma([(T.xr[:, 0:ZC], T.x[:, 0:ZC])], [], R("xr", 0, ZC))
     dma([(T.xr[:, ZC + 1:XW + 1], T.x[:, ZC:XW])], [], R("xr", ZC, XW + 1))
-    dma([(T.n4[:, h:GW], T.nb[:, h:GW])], [], R("n4", h, GW))
+    dma([(T.an[:, 0:L], T.a0[:])], [], R("an", 0, L))
     dma([(T.thi[:], T.th[:])], [], R("thi"))
     iota(("pi", 0, 1), [[0, 1]], 0, 1)
     iota(("jj",), [[1, L]], 0, 0)
+    iota(("jr",), [[4, 3], [32, 8], [1, 16]], 4, 0, allow_small_or_imprecise_dtypes=True)
     for k in range(1, 4):
-        dma([(T.n4[k:128, k * GW:(k + 1) * GW], T.nb[0:128 - k, :])], [], R("n4", k * GW, (k + 1) * GW))
+        dma([(T.n4[u::16, k * GW:(k + 1) * GW], T.nb[(u - k) % 16::16, :]) for u in range(16)], [], R("n4", k * GW, (k + 1) * GW))
 
     def turn_all():
         for s in DROT:
-            dma([(T.g4[0:128 - 4 * s, s * GW:(s + 1) * GW], T.g4[4 * s:128, 0:GW])], [R("g4", 0, GW)], R("g4", s * GW, (s + 1) * GW))
-
-    def turn_rest():
-        for k in range(1, 4):
-            dma([(T.n4[u::16, k * GW:(k + 1) * GW], T.nb[16 - k + u::16, :]) for u in range(k)], [], R("n4", k * GW, (k + 1) * GW))
-        for s in DROT:
-            rows = [(T.g4[u::16, s * GW:(s + 1) * GW], T.g4[u + 4 * s - 16::16, 0:GW]) for u in range(16 - 4 * s, 16)]
-            dma(rows, [R("g4", 0, GW)], R("g4", s * GW, (s + 1) * GW))
+            dma([(T.g4[u::16, s * GW:(s + 1) * GW], T.g4[(u + 4 * s) % 16::16, 0:GW]) for u in range(16)], [R("g4", 0, GW)], R("g4", s * GW, (s + 1) * GW))
 
     op("g", lambda q: q.affine_select(T.se[:, 16:2064], T.w1[:], [[-1024, 16], [16, 8], [1025, 16]], OP.is_equal, 0.0, 0, -1), [R("w1")], [R("se", 16, 2064)])
-    iota(("jr",), [[4, 3], [32, 8], [1, 16]], 4, 0)
+    iota(("km", 0, 16), [[4, 4], [-3, 4]], 16, 0)
     ts(("pi", 1, 2), ("pi", 0, 1), 15, OP.bitwise_and)
     ts(("pi", 2, 3), ("pi", 0, 1), 4, OP.arith_shift_right)
     cp(("pf", 0, 3), ("pi", 0, 3))
@@ -268,26 +252,30 @@ def rank_program(g, core, T, topo):
     for lo in (0, 2064):
         ts(("se", lo, lo + 16), ("w1", 0, 16), 0.0, OP.mult)
     ts(("u16",), ("jf", 0, 16), ROW, OP.is_equal)
-    ts(("pf", 3, 4), ROW, 8.0, OP.mult, 1024.0, OP.add)
+    ts(("pf", 3, 4), ROW, 8.0, OP.mult)
     ts(("pf", 4, 5), ROW, 16.0, OP.mult)
-    ts(("pf", 5, 6), ROW, 2048.0, OP.mult, 33.0 * 1024.0, OP.add)
+    ts(("pf", 5, 6), ROW, 2048.0, OP.mult, 32768.0, OP.add)
     ts(("pf", 6, 7), ROW, 5.0, OP.is_ge)
-    ts(("pf", 7, 8), GRP, 16.0, OP.mult, ("pf", 0, 1), OP.add)
+    ts(("pf", 10, 11), GRP, 16.0, OP.mult, ("pf", 0, 1), OP.add)
+    ts(("pf", 7, 8), ("pf", 10, 11), -1.0, OP.mult, -8.0, OP.add)
     ts(("pf", 8, 9), ROW, 15.0, OP.is_equal, 0.25, OP.mult)
     ts(("pf", 9, 10), ROW, 0.0, OP.is_equal)
 
     def prepare(tok):
-        k = int(tok[1:])
+        eng = tok[-1] if tok[-1] in "vg" else "a"
+        k = int(tok.rstrip("vg")[1:])
         if tok[0] == "G":
             ts(("g4", k * H, k * H + H), ("gi", k * H, k * H + H), 1.0 + 2.0 ** -12, OP.mult, MAGIC, OP.add)
             act(("g4", k * H, k * H + H), ("g4", k * H, k * H + H), AF.Copy, bias=-(MAGIC + 2048.0))
         elif tok[0] in "OR":
             cp((tok[0].lower() + "0",) + CUT[k][0:2], ("n4", 8 * CUT[k][0], 8 * CUT[k][1], 8))
+        elif tok[0] == "C":
+            cp(("g16", k * H, k * H + H), ("g4", k * H, k * H + H), eng)
         elif tok[0] == "Q":
-            s, lo = 1 + k // 4, 512 * (k % 4)
-            bank = ("pa", "pb")[k % 2]
-            mm((bank,), ("rt", (s - 1) * 128, s * 128), ("g16", lo, lo + 512))
-            cp(("g4", s * GW + lo, s * GW + lo + 512), (bank,), "a" if k in ROTA else "v")
+            s, lo = 1 + k % 3, H * (k // 3)
+            bank = ("pa", "pb", "pd0", "pd1")[k % 4]
+            mm((bank,), ("rt", (s - 1) * 128, s * 128), ("g16", lo, lo + H))
+            cp(("g4", s * GW + lo, s * GW + lo + H), (bank,), eng)
         elif k == 0:
             fill(("wf", 0, 16), 0.5)
             fill(("wf", 16, 32), 0.0)
@@ -306,16 +294,18 @@ def rank_program(g, core, T, topo):
             ts(("bh",), ("bo",), 0.5, OP.mult)
             ts(("bn",), ("bo",), -2.0 ** 31, OP.mult)
         elif k == 2:
-            fill(("z0",), 1024.0)
             ts(("cb",), ("jf", 0, 16), 256.0, OP.mult, ("pf", 4, 5), OP.add)
-            for c0, c1, _ in CUT:
-                ts(("z0", c0 // 8, c0 // 16 + c1 // 16), ("jf", c0 // 16, c1 // 16), 128.0, OP.mult, ("pf", 3, 4), OP.add)
+            ts(("z0",), ("jf", 0, 16), 128.0, OP.mult, ("pf", 3, 4), OP.add)
+            ts(("c2",), ("jt", 8, 32), 1.0, OP.is_equal, 2048.0, OP.mult)
+            ts(("c2", 16, 24), ("c2", 0, 8), 0.0, OP.mult)
             ts(("cb", 8, 16), ("cb", 8, 16), 1.0, OP.add)
         elif k == 3:
-            ts(("thf",), ("thi",), 1.0, OP.add)
+            ts(("thf", 0, 1), ("thi",), 1.0, OP.add, 1.0 / 16, OP.mult)
+            ts(("thf", 1, 2), ("thi",), 32.5, OP.add)
             ts(("lim",), ("thi",), 1.0, OP.add)
         elif k == 4:
-            cp(("tm",), ("u16",))
+            ts(("km", 16, 32), ("km", 0, 16), 15, OP.bitwise_and)
+            ts(("tm",), ("km", 16, 32), ROW, OP.is_equal)
             ts(("b15",), ("bo",), ("pf", 8, 9), OP.mult, 2.0 ** 30, OP.mult)
             cp(("one",), ("w1", 0, 128))
         elif k == 5:
@@ -329,54 +319,61 @@ def rank_program(g, core, T, topo):
             ts(("jt",), ("jj", 0, 128), 15, OP.bitwise_and)
             ts(("l2",), ("jt",), ROW, OP.is_gt)
             tt(("lt",), ("l2",), ("bo",), OP.mult)
-        else:
+        elif k == 7:
             cp(("wn", OG, OG + L), ("o16",), "g")
+        elif k == 8:
+            ts(("sz2",), ("sz",), 2.0, OP.mult)
+            ts(("szn",), ("sz",), -1.0, OP.mult)
+        else:
+            op("g", lambda q: q.affine_select(T.sa[:], T.w1[:], [[1, 16], [16, 8], [0, 16]], OP.is_equal, 0.0, 0, -1), [R("w1")], [R("sa")])
 
     def turns():
-        ts(("rt",), ("jr",), ("pf", 7, 8), OP.is_equal)
-        ts(("r2",), ("jr",), -16.0, OP.add, ("pf", 7, 8), OP.is_equal)
-        tt(("rt",), ("rt",), ("r2",), OP.add)
+        act(("r2",), ("jr",), AF.Abs, bias=("pf", 7, 8))
+        ts(("rt",), ("r2",), 8.0, OP.is_equal)
 
-    def turn_own():
-        for s in range(1, 4):
-            bank = ("pa", "pb")[s % 2]
-            mm((bank, 0, L), ("rt", (s - 1) * 128, s * 128), ("o16",))
-            cp(("g4", s * GW, (s + 1) * GW, 8), (bank, 0, L), "av"[s % 2])
-
-    def run(tok, tau):
+    def run(tok, tau, toks):
         gen, t = divmod(tau, ST)
         last = t == ST - 1
-        eng = "v" if tok[-1] == "v" else "a"
-        tok, _, js = tok.rstrip("v").partition(".")
-        kind = tok.rstrip("0123456789") if tok[0:2] not in ("M1", "M2") else tok[0:2]
-        b = int(tok[len(kind):]) if tok[len(kind):] else 0
-        c0, c1, subs = CUT[b]
+        eng = tok[-1] if tok[-1] in "vg" else "a"
+        tok, _, js = tok.rstrip("vg").partition(".")
+        js, _, hs = js.partition(".")
+        kind = tok.rstrip("0123456789") if tok[0:2] not in ("M1", "M2", "T1", "T2", "T3") else tok[0:2]
+        num = int(tok[len(kind):]) if tok[len(kind):] else 0
+        b = 0 if kind in ("EH", "EI", "OT") else num
+        c0, c1, subs = (CUT + [(0, L, ())])[b]
         n = c1 - c0
         l0, l1 = c0 // 16, c1 // 16
         lc = l1 - l0
         pe, pd, pn = "pe%d" % b, "pd%d" % b, "pl%d" % b
-        e0 = c0 + sum(subs[0:int(js)]) if js else 0
-        e1 = e0 + subs[int(js)] if js else 0
-        plain = js and (b, int(js)) in (EDGE if last or t == 0 else PLAIN)
+        e0 = c0 + sum(subs[0:int(js)]) if js else c0
+        e1 = e0 + subs[int(js)] if js else c1
+        plain = "PA%d.%s" % (b, js) in toks
+        halves = ["%s%d.%sv" % (k, b, js) in toks for k in ("AB", "AC")]
+        if hs:
+            e0, e1 = e0 + 32 * int(hs), e0 + 32 * int(hs) + 32
         copies = [("t%d" % k, e0, e1) for k in (0, 1, 2, 3, 4, 8)]
-        spread = [("ed%d" % a, 0, 1) for a in range(16)]
-        q = 3 * c0
+        qe, qr, qs = [("qq", o, o + n) for o in ((c0, 0, L + c0) if last else (3 * c0, 3 * c0 + n, 3 * c0 + 2 * n))]
+        ng = ("qq", 3 * L + c0, 3 * L + c1)
         sco = (pd, 256, 256 + n)
-        rp = (pn, 192, 192 + n)
-        le, lr, ls = [(pn, 400 + k * lc, 400 + (k + 1) * lc) for k in range(3)]
+        rp = (pe, 256, 256 + n)
+        le, lr, ls = [("pl1" if last else pn, 400 + k * lc, 400 + (k + 1) * lc) for k in ((0, 0, 1) if last else (0, 1, 2))]
         hist = "ho" if t in (1, 2, 3) else "hn"
         xo = (hist, 32 * tau + l0, 32 * tau + l1)
         nl = (hist, 32 * tau + 16 + l0, 32 * tau + 16 + l1)
-        lb = 5 * l0 + b * lc
-        li = [("li", lb + k * lc, lb + (k + 1) * lc) for k in range(4)]
-        ln = [("ln", LW * tau + r[1], LW * tau + r[2]) for r in li]
-        cs = 5 * l0 + (4 * lc if b == 0 else 0)
-        put = ("lo", LW * tau + cs, LW * tau + cs + lc)
+        li = [("li", LW * tau + 3 * l0 + k * lc, LW * tau + 3 * l0 + (k + 1) * lc) for k in ((1, 0, 2), (1, 2, 0), (1, 1, 1))[b]]
+        lm, ln = [[(m,) + r[1:] for r in li] for m in ("lm", "ln")]
+        both = (min(li[0][1], li[2][1]), max(li[0][2], li[2][2]))
+        put = ("lo", 16 * tau + l0, 16 * tau + l1)
         ww = ("ww" if t else "w0", c0, c1)
-        zz = "zz" if t else "z0"
-        yi = ("yi", l0, l1)
+        yi = ("yi",) if last else li[1]
         ao = L * tau
-        if kind == "RR":
+        if kind == "OW":
+            cp(("o16", 0, L), ("g4", 0, GW, 8), eng)
+        elif kind == "OT":
+            bank = ("pa", "pb")[num % 2]
+            mm((bank, 0, L), ("rt", (num - 1) * 128, num * 128), ("o16",))
+            cp(("g4", num * GW, (num + 1) * GW, 8), (bank, 0, L), eng)
+        elif kind == "RR":
             cp(("rr", c0, c1), (("n4",), ln[0]))
         elif kind == "WW":
             cp(ww, (("tw",), ln[2]), eng)
@@ -391,14 +388,19 @@ def rank_program(g, core, T, topo):
         elif kind == "MK":
             cp(("m0", c0, c1), (("tm",), ln[2]), eng)
         elif kind == "NG":
-            tt(("ng", c0, c1), (("g4", 0, GW), ln[3]), ("m0", c0, c1), OP.mult)
+            tt(ng, (("g4",), ln[0]), ("m0", c0, c1), OP.mult)
         elif kind == "NM":
             for a in range(16):
-                mm((pn, 384, 384 + lc), onto(a) if t else move(0, a), ("ng" if t else "o16", c0 + a, c1, 16), a == 0, a == 15)
+                rhs = ("qq", ng[1] + a, ng[2], 16) if t else ("o16", c0 + a, c1, 16)
+                mm((pn, 384, 384 + lc), onto(a) if t else move(0, a), rhs, a == 0, a == 15)
         elif kind == "NL":
             ts(nl, (pn, 384, 384 + lc), 2048.0, OP.add)
         elif kind == "PZ":
-            ts(("zz", 2 * l0, 2 * l1), ("ln", ln[0][1], ln[1][2]), 1024.0, OP.add)
+            tt(("zz", l0, l1), lm[1], lm[0], OP.subtract)
+        elif kind == "PY":
+            ts(("zz", 16, 32), ("zz", 0, 16), 2048.0, OP.add)
+        elif kind == "UC":
+            cp(("ln",) + both, ("lm",) + both)
         elif kind == "E":
             cp(("eg", 16 * e0, 16 * e1), (("g4", 0, 4 * GW if t else GW), ("of" if t else "o0", e0, e1)), eng)
         elif kind == "F":
@@ -410,12 +412,11 @@ def rank_program(g, core, T, topo):
         elif kind == "DA":
             act(("tr", 16 * c0, 16 * c1, 16), ("dd", c0, c1), AF.Abs, tag=("t0", c0, c1))
         elif kind == "TA":
-            f0 = c0 if b else c0 + subs[0]
-            cp(("tr", 16 * f0 + 8, 16 * c1, 16), ("tr", 16 * f0, 16 * c1, 16), tag=("t8", f0, c1), more=[("t0", f0, c1)])
-            cp(("tr", 16 * f0 + 4, 16 * c1, 8), ("tr", 16 * f0, 16 * c1, 8), tag=("t4", f0, c1), more=[("t0", f0, c1), ("t8", f0, c1)])
-        elif kind == "TB":
-            for s, w in enumerate(TBQ[e0 // 64]):
-                cp(("tr", 16 * e0 + s + 1, 16 * e1, 4), ("tr", 16 * e0, 16 * e1, 4), w, ("t%d" % (s + 1), e0, e1), [("t%d" % k, e0, e1) for k in (0, 4, 8)])
+            cp(("tr", 16 * e0 + 8, 16 * e1, 16), ("tr", 16 * e0, 16 * e1, 16), eng, ("t8", e0, e1), [("t0", e0, e1)])
+            cp(("tr", 16 * e0 + 4, 16 * e1, 8), ("tr", 16 * e0, 16 * e1, 8), eng, ("t4", e0, e1), [("t0", e0, e1), ("t8", e0, e1)])
+        elif kind in ("T1", "T2", "T3"):
+            s = int(kind[1])
+            cp(("tr", 16 * e0 + s, 16 * e1, 4), ("tr", 16 * e0, 16 * e1, 4), eng, ("t%d" % s, e0, e1), [("t%d" % k, e0, e1) for k in (0, 4, 8)])
         elif kind == "XL":
             ts(("xl", e0, e1), (pe, e0 - c0, e1 - c0), 2048.0, OP.add)
         elif kind == "X":
@@ -426,23 +427,30 @@ def rank_program(g, core, T, topo):
                 tt(out, (XR, ("xl", e0, e1)), ("tr", 16 * e0, 16 * e1), OP.add, more=copies)
         elif kind in ("PA", "PB"):
             h = int(kind == "PB")
-            if b:
-                mm((kind.lower(),), ("idn",), ("uu", 16 * e0 + h, 16 * e1, 2), True, False)
+            wide = "T1%d.%s" % (b, js) in [k.rstrip("vg") for k in toks]
+            mm((kind.lower(),), ("idn",), ("uu", 16 * e0 + h, 16 * e1, 2), True, False)
+            if wide:
                 mm((kind.lower(),), ("ib",), ("tr", 16 * e0 + h, 16 * e1, 2), False, True, copies)
-            for s in range(0 if b else 8):
-                o = (kind.lower(), 64 * s, 64 * s + 64)
-                mm(o, ("idn",), ("uu", 16 * e0 + s + 8 * h, 16 * e1, 16), True, False)
-                mm(o, ("ib",), ("tr", 16 * e0, 16 * e1, 16), False, True, [("t0", e0, e1)])
+            for s in range(0 if wide else 8):
+                mm((kind.lower(), s, 512, 8), ("ib",), ("tr", 16 * e0, 16 * e1, 16), False, s == 7, [("t0", e0, e1)])
         elif kind in ("AB", "AC"):
             h = int(kind == "AC")
             src = (("pa", "pb")[h],) if plain else ("uu", 16 * e0 + h, 16 * e1, 2)
-            act(("ab", 8 * (e0 + (e1 if h else e0)), 8 * (e1 + (e1 if h else e0))), src, AF.Abs, bias=-255.0)
-        elif kind in ("AM", "AN"):
-            h = int(kind == "AN")
+            out = ("ab", 8 * (e0 + (e1 if h else e0)), 8 * (e1 + (e1 if h else e0)))
+            if eng == "a":
+                act(out, src, AF.Abs, bias=-255.0)
+            else:
+                ts(out, src, 255.0, OP.max, -127.5, OP.add)
+        elif kind in ("AM", "AN", "AU", "AV"):
+            h = int(kind in ("AN", "AV"))
             o, m = 8 * (e0 + (e1 if h else e0)), e1 - e0
             for s in range(8):
-                rhs = ("ab", o + s, o + 8 * m, 8) if e0 else ("ab", o + m * s, o + m * s + m)
-                mm((pd, e0 - c0, e1 - c0), onto(2 * s + h if e0 else 8 * h + s), rhs, s + h == 0, s + h == 8)
+                u = 2 * s + h
+                if kind in ("AU", "AV"):
+                    lhs, rhs = onto(u, "szn"), ("uu", 16 * e0 + u, 16 * e1, 16)
+                else:
+                    lhs, rhs = onto(u, "sz2" if halves[h] else "sz"), ("ab", o + s, o + 8 * m, 8)
+                acc((tau, e0), 16 + 8 * sum(halves), (pd, e0 - c0, e1 - c0), lhs, rhs)
         elif kind == "GO":
             if eng == "a":
                 act((pd, 0, n), (pd, 0, n), AF.Relu, bias=("lim",), scale=-1.0)
@@ -455,14 +463,19 @@ def rank_program(g, core, T, topo):
         elif kind == "PF":
             tt(("ff", c0, c1), ("ok", c0, c1), sco, OP.is_gt)
         elif kind == "PW":
-            times(eng, ("qq", q + 2 * n, q + 3 * n), ("ff", c0, c1), ("pf", 5, 6))
+            if eng == "a":
+                act(qs, ("ff", c0, c1), AF.Copy, scale=("pf", 5, 6))
+            else:
+                ts(qs, ("ff", c0, c1), ("pf", 5, 6), OP.mult)
         elif kind == "PQ":
-            tt(("qq", q, q + n), ("ff", c0, c1), (pe, 0, n), OP.mult)
+            tt(qe, ("ff", c0, c1), (pe, 0, n), OP.mult)
             if not last:
-                tt(("qq", q + n, q + 2 * n), ("ff", c0, c1), rp, OP.mult)
+                tt(qr, ("ff", c0, c1), rp, OP.mult)
         elif kind == "PC":
+            if not last:
+                mm((le[0], le[1], ls[2]), ("idn",), ("c2",), True, False)
             for a in range(16):
-                mm((pn, 400, 400 + 3 * lc), onto(a), ("qq", q + a, q + 3 * n, 16), a == 0, a == 15)
+                mm((le[0], le[1], ls[2]), onto(a), ("qq", qe[1] + a, qs[2], 16), last and a == 0, a == 15)
         elif kind == "YM":
             mm((pd, 0, n), ("ib",), ("tr", 16 * c0, 16 * c1, 16), True, False, [("t0", c0, c1)])
             mm((pd, 0, n), ("bn",), ("ok", c0, c1), False, True)
@@ -472,23 +485,25 @@ def rank_program(g, core, T, topo):
             else:
                 ts(("yy", c0, c1), (pd, 0, n), 0.0, OP.max)
         elif kind == "M1":
-            tt(("ti", l0, l1), ls, (zz, 2 * l0, 2 * l0 + lc), OP.max)
-            if not last:
-                tt(("ti", 16 + l0, 16 + l1), lr, (zz, 2 * l0 + lc, 2 * l1), OP.add)
-            tt(yi, ("ti", l0, l1), (zz, 2 * l0 + lc, 2 * l1) if last else ("ti", 16 + l0, 16 + l1), OP.add)
+            if last:
+                for o, m in ((0, 8), (8, 32)):
+                    tt(("ti", o, o + 8), (ls[0], ls[1] + o, ls[1] + o + 8), ("lm", LW * tau + m, LW * tau + m + 8), OP.max)
+                tt(yi, ("ti", 0, 16), ("zz", 16, 32), OP.add)
+            else:
+                tt(("ti", l0, l1), ls, lm[0] if t else ("z0", l0, l1), OP.max)
+                if t:
+                    tt(("ti", 16 + l0, 16 + l1), lr, ("zz", l0, l1), OP.add)
+                tt(yi, ("ti", l0, l1), ("ti", 16 + l0, 16 + l1) if t else lr, OP.add)
         elif kind == "ML":
-            o = LW * tau
+            o = LW * tau + 3 * l0
             ts(li[2], yi, 11, OP.arith_shift_right, 15, OP.bitwise_and)
             if not last:
                 ts(li[0], yi, 8191, OP.bitwise_and)
-            tt(("li", cs, cs + lc), li[2], ("cb", l0, l1), OP.add)
-            if last:
-                cp(put, ("li", cs, cs + lc))
-            else:
-                for k, m in ((3, 2047), (1, 24576)):
-                    ts(li[k], yi, m, OP.bitwise_and)
-                cp(("lo", o + 5 * l0, o + 5 * l1), ("li", 5 * l0, 5 * l1))
-                send(nxt, "lo", o + lb, o + lb + 4 * lc, "ln", o + LW + lb, "li%d_%d" % (tau, b))
+                send(nxt, "li", o, o + 3 * lc, "lm", o + LW, "li%d_%d" % (tau, b))
+        elif kind == "CS":
+            o = LW * tau
+            tt(("li", o + 48, o + 64), ("li", o + 16, o + 32), ("cb",), OP.add)
+            cp(("lo", put[1], put[1] + 16), ("li", o + 48, o + 64))
         elif kind == "XO":
             ts(xo, le, 2048.0, OP.add)
         elif kind == "M2":
@@ -497,7 +512,7 @@ def rank_program(g, core, T, topo):
                 send(nxt, "ao", ao + c0, ao + c1, "an", ao + L + c0, "ar%d_%d" % (tau, b))
         elif kind == "HI":
             send(T.cores[(rank - t) % N], "ho", 32 * tau, 32 * tau + 32, "hn", 32 * tau, "h%d" % tau)
-        elif kind in ("ST", "CA", "CB", "CC", "CD", "CE") and tau == TAU - 1:
+        elif kind in ("ST", "CA", "CB", "CC", "CE") and tau == TAU - 1:
             return
         elif kind == "ST":
             cp((XR, ("lo", put[1], put[1] + 16)), ("ao", ao, ao + L))
@@ -505,47 +520,54 @@ def rank_program(g, core, T, topo):
             ts(("hc",), (hist, 32 * tau, 32 * tau + 16), float(ZC), OP.is_equal)
             mm(("pa", 256, 272), ("one",), ("hc",))
         elif kind == "CB":
-            total(("af",), ("pa", 256, 272))
+            op("a", lambda s: s.activation(T.wf[:, 0:16], T.pa[:, 256:272], AF.Identity, bias=T.thf[:, 0:1], accum_out=T.af[:]),
+               [("pa", 256, 272), R("thf")], [("wf", 0, 16), R("af")])
         elif kind == "CC":
-            cp(("ai", 0, 1), ("af",))
-        elif kind == "CD":
-            ts(("ai", 1, 2), ("ai", 0, 1), 63, OP.bitwise_and)
+            ts(("ai",), ("af",), ("thf", 1, 2), OP.subtract, 1.0 / 64, OP.mult)
         elif kind == "CE":
-            ts(("lim",), ("ai", 1, 2), ("thf",), OP.add)
+            ts(("lim",), ("ai",), -64.0, OP.mult, ("af",), OP.add)
         elif kind == "EE":
             o = 32 * ST * gen
             ts(("hv",), ("hn", o, o + 128), -2048.0, OP.add)
             ts(("hf",), ("hv",), 0.0, OP.is_equal)
+        elif kind == "EC":
             tt(("hm", 0, 112), ("hf", 0, 112), ("hv", 16, 128), OP.mult)
+            tt(("hw", 0, 112), ("hv", 0, 112), ("hm", 0, 112), OP.add)
+        elif kind == "ED":
             tt(("e1",), ("hf", 0, 48), ("hf", 64, 112), OP.add)
-            for s in range(4):
-                tt(("hw", 16 * s, 16 * s + 16), ("hv", 32 * s, 32 * s + 16), ("hm", 32 * s, 32 * s + 16), OP.add)
-            tt(("hw", 64, 80), ("e1", 0, 16), ("e1", 32, 48), OP.add)
-        elif kind in ("EH", "EI", "EJ", "EL"):
-            for a in range("HIJL".index(kind[1]), 16, 4):
-                times(eng, ("ed", a, 5 * L, 16), ("hw",), ("u16", a, a + 1), spread[a])
+            tt(("hw", 112, 128), ("e1", 0, 16), ("e1", 32, 48), OP.add)
         elif kind == "EF":
             mm(("pa", 0, L), ("b0",), ("on",), True, False)
-            mm(("pa", 0, L), ("bo",), ("ed", 4 * L, 5 * L), False, False, spread)
+            for a in range(16):
+                mm(("pa", a, L, 16), ("sa", 128 * a, 128 * a + 128), ("hw", 112, 128), False, False)
         elif kind == "EG":
-            mm(("pb", 0, L), ("d5",), ("o16",), True, False)
+            mm(("pl0", 0, L), ("d5",), ("o16",), True, False)
+        elif kind == "EH":
+            for a in range(16):
+                mm(("pl0", a, L, 16), move(a, num), ("hw", 32 * num, 32 * num + 16), False, False)
+        elif kind == "EI":
+            for a in range(num, 16, 4):
+                if eng == "a":
+                    act(("ed", a, 7 * L, 16), ("hw", 0, 112), AF.Copy, scale=("u16", a, a + 1), tag=("ed%d" % a, 0, 1))
+                else:
+                    ts(("ed", a, 7 * L, 16), ("hw", 0, 112), ("u16", a, a + 1), OP.mult, tag=("ed%d" % a, 0, 1))
+        elif kind == "EJ":
             for s in range(4):
-                mm(("pb", 0, L), onto(s), ("ed", s * L, s * L + L), False, False, spread)
+                mm(("pl0", 0, L), onto(s), ("ed", 2 * s * L, 2 * s * L + L), False, False, [("ed%d" % a, 0, 1) for a in range(16)])
         elif kind == "FL":
             fl = (pe, 256, 256 + n)
             mm(fl, ("b0",), ("on", c0, c1), True, False)
             mm(fl, ("bm",), ("ff", c0, c1), False, True)
-            tt(("nf", c0, c1), ("ng", c0, c1), fl, OP.mult)
+            tt(("nf", c0, c1), ng, fl, OP.mult)
         elif kind == "SH":
-            for c0, c1, _ in CUT:
-                mm(("pb", c0, c1), onto(4), ("qq", 3 * c0, 2 * c0 + c1), False, False)
-            mm(("pb", 0, L), onto(4), ("nf",), False, True)
+            mm(("pl0", 0, L), onto(4), ("qq", 0, L), False, False)
+            mm(("pl0", 0, L), onto(4), ("nf",), False, True)
         elif kind == "SG":
             if gen < GENS - 1:
-                cp(("da",), ("pb", 0, L), "a")
+                cp(("da",), ("pl0", 0, L), eng)
             else:
-                ts(("fo", 0, L), ("pb", 0, L), 0.0, OP.is_le, 2047.0, OP.add)
-                tt(("da",), ("fo", 0, L), ("pb", 0, L), OP.add)
+                ts(("fo", 0, L), ("pl0", 0, L), 0.0, OP.is_le, 2047.0, OP.add)
+                tt(("da",), ("fo", 0, L), ("pl0", 0, L), OP.add)
         elif kind == "SA":
             mm(("pa", 0, L), ("bm",), ("ff",), False, True)
             ts(("ind",), ("pa", 0, L), ROW, OP.is_equal)
@@ -563,17 +585,15 @@ def rank_program(g, core, T, topo):
             cp((("wn", SR, SR + L), ("pl",)), ("da",))
             send(nxt, "wn", SR, SR + K, "wn", BI[gen], "b%d" % gen)
         elif kind == "SC":
-            w = min(SR, BI[gen])
-            ts(("kr", 0, 16), ("pa", 320, 336), -1.0, OP.mult, 255.0, OP.add)
-            ts(("kr", 16, 32), ("kr", 0, 16), 1, OP.bitwise_and)
-            ts(("kf", 0, 16), ("kr", 0, 16), float(K), OP.is_ge, 4096.0, OP.mult)
-            ts(("kf", 16, 32), ("kr", 16, 32), float(BI[gen] - SR), OP.mult, float(SR - OG), OP.add)
-            tt(("kf", 32, 48), ("kf", 0, 16), ("kr", 0, 16), OP.add)
-            tt(("kf", 48, 64), ("kf", 32, 48), ("kf", 16, 32), OP.add)
-            tt(("kf", 0, 16), ("kf", 48, 64), ("ob",), OP.min)
-            ts(("pr",), ("kf", 0, 16), float(OG - w), OP.add)
+            ts(("kf", 0, 16), ("pa", 320, 336), float(L - K), OP.is_lt, 4096.0, OP.mult)
+            ts(("kf", 16, 32), ("pa", 320, 336), -1.0, OP.mult, float(L - 1 + BI[gen] - OG), OP.add)
+            tt(("kf", 32, 48), ("kf", 0, 16), ("kf", 16, 32), OP.add)
+            tt(("kf", 48, 64), ("kf", 32, 48), ("ob",), OP.min)
+            ts(("pr",), ("kf", 48, 64), float(OG - BI[gen]), OP.add)
+        elif kind == "SM":
+            cp(("wn", BI[gen], BI[gen] + K, 2), ("wn", SR, SR + K, 2), eng)
         elif kind == "SN":
-            cp(("g4", 0, GW, 8) if gen < GENS - 1 else ("fo", 0, L), (("wn", min(SR, BI[gen]), OG + L), ("pr",)))
+            cp(("g4", 0, GW, 8) if gen < GENS - 1 else ("fo", 0, L), (("wn", BI[gen], OG + L), ("pr",)))
             if gen == GENS - 1:
                 dma([(T.yg[:], T.fo[:, 0:L])], [R("fo", 0, L)], None, True)
         elif gen < GENS - 1:
@@ -585,8 +605,8 @@ def rank_program(g, core, T, topo):
             for h in range(2):
                 o = h * (ZC + 1)
                 for s in range(16):
-                    mm(("pa", 128 * h, 128 * h + 128), ("ib",), ("xr", o + s, o + ZC, 16), s == 0, s == 15)
-            cp(("fo", 2 * L, 3 * L), ("pa", 0, L), "a")
+                    mm(("pb", 128 * h, 128 * h + 128), ("ib",), ("xr", o + s, o + ZC, 16), s == 0, s == 15)
+            cp(("fo", 2 * L, 3 * L), ("pb", 0, L), eng)
         elif kind == "YO":
             cp(("dd", c0, c1), (XR, put), eng)
         elif kind == "YD":
@@ -596,26 +616,29 @@ def rank_program(g, core, T, topo):
         elif kind == "YE":
             dma([(T.ys[:], T.fo[:, 2 * L:3 * L])], [R("fo", 2 * L, 3 * L)], None, True)
         elif kind == "YA":
-            cp(("fo", L, 2 * L), ("ao", ao, ao + L), "a")
+            cp(("fo", L, 2 * L), ("ao", ao, ao + L), eng)
             dma([(T.ya[:], T.fo[:, L:2 * L])], [R("fo", L, 2 * L)], None, True)
 
-    once = {"RT": turns, "RA": turn_all, "RB": turn_rest, "OT": turn_own,
-            "GC": lambda: cp(("g16", 0, GW), ("g4", 0, GW), "g"), "OW": lambda: cp(("o16", 0, L), ("g4", 0, GW, 8), "g")}
+    once = {"RT": turns, "RA": turn_all}
     for tau in range(TAU):
         t = tau % ST
-        for tok in (LAST if t == ST - 1 else ORDER if t else AGAIN if tau else FIRST):
-            if tok[0] in "GORLQ" and tok[1:].isdigit():
-                prepare(tok)
+        toks = LAST if t == ST - 1 else ORDER if t else AGAIN if tau else FIRST
+        for tok in toks:
+            if tok[0] in "GORLQC" and tok.rstrip("vg")[1:].isdigit():
+                if tau < 2:
+                    prepare(tok)
             elif tok in once:
-                once[tok]()
+                if t == 0 or tau == 1:
+                    once[tok]()
             elif tok[-1] == "'":
-                run(tok[0:-1], tau + 1)
+                if tau + 1 < TAU:
+                    run(tok[0:-1], tau + 1, ())
             else:
-                run(tok, tau)
+                run(tok, tau, toks)
 
-    for i in range(nd[0]):
-        if known["s"].get("d%d" % i, 0) < 16:
-            g.sync.wait_ge(T.sem["d%d" % i], 16)
+    for s, n in nd:
+        if known["s"].get(s, 0) < n:
+            g.sync.wait_ge(T.sem[s], n)
     g.wait_ge(T.sem.loc, locs[0])
     for s in ("v", "a", "p", "gc"):
         g.sync.wait_ge(T.sem[s], cnt[s])

from concourse.mybir import AluOpType, AxisListType, ActivationFunctionType
OP = AluOpType
AF = ActivationFunctionType
N, GENS, ST, K = 4, 2, 5, 64
L, GW, XW = 256, 2048, 4096
ZC = 2048
MAGIC = 12582913.0
TAU = GENS * ST
CUT = [(0, 128, (64, 64)), (128, 256, (64, 64))]
DMAS = 24
DROT = (1, 3)
LW = 64
SR, BI, OG = 64, (320, 0), 384
FIRST = """G0 G1 G2 G3 RA OWg NM0 O0 E0.0 C0g L7 F0.0 L1 L0 O1 E1.0 NM1 E0.1v NL0 XL0.0 F1.0 D0 DA0 F0.1 X0.0v TA0.1 PB0.0 T20.1g PA0.0 NL1 T10.1g
 T30.1v D1 E1.1 XL0.1 L8 X0.1 AC0.0 AN0.0 AC0.1v AB0.0 DA1 AB0.1 XL1.0 AM0.0 L3 L2 TA1.1g X1.0 AV0.1 AN0.1 AM0.1 R0 F1.1 T21.1g GO0v RP0 GV0
 T11.1v GM0 XL1.1 T31.1 PA1.0 PF0 PW0 C1 PQ0 AB1.0 R1 C3 X1.1.1 PC0 PB1.0 M10 ML0 AM1.0 YM0 X1.1.0 YY0v AC1.0 AB1.1v AN1.0 RT AU1.1 L4 AC1.1
 AM1.1 XO0 AN1.1 Q4 GO1v GV1 RP1 Q1 M20 GM1 PF1 C2 PW1v PQ1 Q10v UC0' YM1 YY1 PC1 WW0' RR0' XO1 Q7 OM0' CA M11 CB OF0' E0.0' RP0' MK0v' ML1
 E0.1' NG0' CC CE M21 CS NM0' NL0' F0.0' ST XL0.0' F0.1'""".split()
ORDER = """D0 DA0 PZ0 UC1 WW1v X0.0 RR1 MK1v NG1 TA0.1g T10.1g OM1 OF1 T20.1v NM1 E1.0 E1.1.0v NL1 PB0.0 XL0.1 D1 PA0.0 AC0.0 T30.1g X0.1 AB0.0 DA1 F1.0
 AN0.0 AB0.1 XL1.0 AC0.1v E1.1.1v AM0.0 AV0.1 TA1.1g AN0.1 AM0.1 L6 GO0v GV0 PZ1 F1.1 GM0 T31.1g L9 T11.1v X1.0 PA1.0 XL1.1 PF0 T21.1 PW0
 AB1.0 YM0 PQ0 X1.1.0 PB1.0 PC0 X1.1.1 AC1.0 AM1.0 AN1.0 M10 ML0 XO0 AB1.1v AC1.1 AU1.1 AN1.1 L5 YY0 AM1.1 GO1v GV1 RP1 GM1 M20 PF1 UC0' RR0'
 YM1 WW0' OM0' PW1 MK0' PQ1 OF0' E0.0' PC1 YY1v NG0' RP0' M11 ML1 NM0' XO1 E0.1.1' CA CB M21 HI CS NL0' ST CC F0.0' XL0.0' CE E0.1.0' F0.1'""".split()
LAST = """D0 UC1 DA0 WW1v RR1 OM1 MK1v NG1 OF1 X0.0 PZ0 NM1 XL0.1 E1.0 E1.1v NL1 PB0.0 AC0.0 PA0.0 F1.0 AB0.0 EE TA0.1g T20.1g T30.1g D1 DA1 EC EG
 XL1.0 X1.0 T10.1g X0.1 AN0.0 F1.1 AM0.0 TA1.1g AC0.1 T21.1v XL1.1 PA1.0 T11.1g T31.1v AB0.1 PZ1 PB1.0 AN0.1 AB1.0 X1.1 AM0.1 AC1.0 AC1.1
 AM1.0 EI0v GO0v AN1.0 ED AB1.1 AN1.1 GV0 GM0 AM1.1 EK PF0 GO1v GV1 EF EI2 EI1 PQ0 PW0v GM1 YM0 PF1 PQ1 EI3 FL0 SA PW1 YM1 FL1 EJ SD PY PC2 SH
 SE SF M12 SGv SB ML2 XO2 YY0 CA YY1 CB CS YO2 M22 SC YAv YS CC YD1 CE YD0 YE SMv SN RP0' OW' E0.1' E0.0v' ST NM0'""".split()
AGAIN = """NL0 E1.0 NM1 NL1 D0 DA0 F0.0 XL0.0 D1 F0.1 DA1 F1.0 TA0.1 X0.0v PA0.0 PB0.0 XL0.1 T10.1g T20.1v E1.1 T30.1v XL1.0 X0.1 AB0.0 F1.1 X1.0v XL1.1
 TA1.1g AC0.0 T21.1v T11.1g AN0.0 AM0.0 AB0.1 AM0.1 AC0.1 AN0.1 PA1.0 AB1.0 GO0v GV0 GM0 YM0 PB1.0 T31.1g X1.1.0 PF0 AM1.0 PQ0 X1.1.1 YY0v PW0
 PC0 M10 AC1.0 XO0 RP1 AN1.0 ML0 OT2v AC1.1 AN1.1 AB1.1 M20 AM1.1 OT1 GO1v GV1 UC0' GM1 PF1 WW0' PW1 OT3 YM1 RR0' OM0' PQ1 YY1 OF0' MK0v' PC1
 NG0' E0.0' M11 XO1 ML1 RP0' NM0' CA M21 CS F0.0' NL0' ST CB CC XL0.0' E0.1' F0.1' CE""".split()

SCRATCH = {}
for _n, _w, _d in (
        ("gi", GW, "int32"), ("g4", 4 * GW, "float32"), ("n4", 4 * GW, "int32"), ("g16", GW, "float16"), ("xr", XW + 16, "bfloat16"), ("w1", GW, "bfloat16"),
        ("eg", 16 * L, "float16"), ("uu", 16 * L, "float16"), ("ab", 16 * L, "float16"), ("tr", 16 * L, "bfloat16"),
        ("rr", L, "float16"), ("ww", L, "bfloat16"), ("m0", L, "bfloat16"), ("of", L, "uint16"), ("nf", L, "float16"),
        ("r0", L, "float16"), ("o0", L, "uint16"), ("w0", L, "bfloat16"), ("dd", L, "bfloat16"), ("xl", L, "uint16"),
        ("ok", L, "bfloat16"), ("ff", L, "float16"), ("qq", 4 * L, "float16"), ("ti", 32, "float32"), ("yy", L, "bfloat16"),
        ("yi", 16, "int32"), ("zz", 32, "float32"), ("z0", 16, "float32"), ("cb", 16, "float32"), ("c2", 24, "float16"),
        ("li", LW * TAU, "int32"), ("lm", LW * TAU, "int32"), ("lo", 16 * TAU, "uint16"), ("ln", LW * TAU, "uint16"), ("ao", L * TAU, "bfloat16"), ("an", L * TAU, "bfloat16"),
        ("ho", 32 * TAU, "uint16"), ("hn", 32 * TAU, "uint16"), ("hv", 128, "float16"), ("hf", 128, "float16"), ("hm", 128, "float16"), ("hw", 128, "float16"),
        ("hc", 16, "float16"), ("e1", 48, "float16"), ("sa", 2048, "float16"), ("ed", 7 * L, "float16"),
        ("wn", OG + L, "float32"), ("da", L, "float32"), ("o16", L, "float16"), ("ind", L, "float16"), ("pre", L, "float16"), ("on", L, "float16"),
        ("x1", L, "float16"), ("x2", L, "float16"), ("pl", 16, "uint16"), ("pr", 16, "uint16"), ("kf", 64, "float32"), ("ob", 16, "float32"),
        ("af", 1, "float32"), ("ai", 1, "int32"), ("lim", 1, "float32"), ("thi", 1, "int32"), ("thf", 2, "float32"),
        ("jj", L, "int32"), ("jf", L, "float32"), ("jt", 128, "int32"), ("kb", 32, "int32"), ("wf", 64, "float32"),
        ("pi", 4, "int32"), ("pf", 16, "float32"), ("u16", 16, "float32"), ("tw", 16, "bfloat16"), ("tm", 16, "bfloat16"),
        ("se", 2048 + 32, "float16"), ("sz", 144, "float16"), ("sz2", 144, "float16"), ("szn", 144, "float16"),
        ("km", 32, "int32"), ("idn", 128, "float16"), ("ib", 128, "bfloat16"), ("ibn", 128, "bfloat16"),
        ("bo", 128, "float16"), ("bm", 128, "float16"), ("bh", 128, "bfloat16"), ("bn", 128, "bfloat16"), ("b15", 128, "bfloat16"), ("b0", 128, "float16"),
        ("d5", 128, "float16"), ("lt", 128, "float16"), ("l2", 128, "float16"), ("one", 128, "float16"),
        ("rt", 384, "float16"), ("r2", 384, "float16"), ("jr", 384, "bfloat16"), ("fo", 3 * L, "float32")):
    SCRATCH[_n] = ("sbuf", [128, _w], _d)
PSUM = ["pe0", "pe1", "pd0", "pd1", "pl0", "pl1", "pa", "pb"]
for _n in PSUM:
    SCRATCH[_n] = ("psum", [128, 512], "float32")
SEMAPHORES = ["v", "a", "p", "gc", "loc", "b0", "b1"] + ["d%d" % i for i in range(DMAS)] + ["h%d" % i for i in range(TAU)]
for _b in range(len(CUT)):
    SEMAPHORES += ["li%d_%d" % (_t, _b) for _t in range(TAU)] + ["ar%d_%d" % (_t, _b) for _t in range(TAU)]


def rank_program(g, core, T, topo):
    rank = T.rank_of(core)
    if rank is None:
        return
    queues = {"v": g.vector, "a": g.scalar, "p": g.tensor, "g": g, "s": g.sync}
    own = {"v": "v", "a": "a", "p": "p", "g": "gc"}
    cnt = {"v": 0, "a": 0, "p": 0, "gc": 0}
    known = {q: {} for q in queues}
    clock = {}
    wr, rd = {}, {}
    nd = []
    open_ = {}
    locs = [0]

    def R(name, lo=0, hi=None):
        return (name, lo, SCRATCH[name][1][-1] if hi is None else hi)

    def need(q, reads, writes):
        best = {}

        def look(lists, rs):
            for name, lo, hi in rs:
                ps = name in PSUM
                for l, h, q2, (s, n) in lists.get(name, ()):
                    if ((ps and q2 != q) or (l < hi and lo < h and q2 + q != "pp")) and n > known[q].get(s, 0) and n > best.get(s, 0):
                        best[s] = n
        look(wr, reads + writes)
        look(rd, writes + [r for r in reads if r[0] in PSUM])
        for s in sorted(best):
            n = best[s]
            if n > known[q].get(s, 0):
                queues[q].wait_ge(T.sem[s], n)
                known[q][s] = n
                for s2, n2 in clock.get((s, n), {}).items():
                    if n2 > known[q].get(s2, 0):
                        known[q][s2] = n2

    def note(q, reads, writes, tok):
        for name, lo, hi in writes:
            for d in (wr, rd):
                d[name] = [e for e in d.get(name, ()) if not (lo <= e[0] and e[1] <= hi)]
            wr[name].append((lo, hi, q, tok))
        for name, lo, hi in reads:
            rd[name] = [e for e in rd.get(name, ()) if not (lo <= e[0] and e[1] <= hi and e[2] == q)] + [(lo, hi, q, tok)]

    def op(q, fn, reads, writes):
        need(q, reads, writes)
        s = own[q]
        fn(queues[q]).then_inc(T.sem[s], 1)
        cnt[s] += 1
        clock[(s, cnt[s])] = dict(known[q])
        note(q, reads, writes, (s, cnt[s]))

    def dma(pairs, reads, reg, out=False):
        need("s", reads, [] if out else [reg])
        s = "d%d" % len(nd)
        for o, src in pairs:
            g.sync.dma_start(o, src).then_inc(T.sem[s], 16)
        tok = (s, 16 * len(pairs))
        nd.append(tok)
        clock[tok] = dict(known["s"])
        note(s, reads, [] if out else [reg], tok)

    def send(dst, name, lo, hi, to, lo2, sem):
        need("g", [(name, lo, hi)], [])
        rid, pid, _ = topo.addr(dst)
        ne = len(topo.engines(core, dst))
        g.remote_dma(T[to][:, lo2:lo2 + hi - lo], T[name][:, lo:hi], T.sem[sem], T.sem.loc, pid, rid, topo.mask(core, dst))
        locs[0] += ne
        note(sem, [], [(to, lo2, lo2 + hi - lo)], (sem, ne))

    def X(r):
        if len(r) == 1:
            return T[r[0]][:], R(r[0])
        if len(r) == 4:
            return T[r[0]][:, r[1]:r[2]:r[3]], r[0:3]
        return T[r[0]][:, r[1]:r[2]], r

    def side(r):
        if len(r) == 2 and isinstance(r[0], tuple):
            return X(r[0])[0].indirect(X(r[1])[0]), [X(r[0])[1], X(r[1])[1]]
        a, i = X(r)
        return a, [i]

    def sc(s):
        return (X(s)[0], [X(s)[1]]) if isinstance(s, tuple) else (s, [])

    def ts(out, src, s1, op0, s2=None, op1=None, tag=None):
        o, io = side(out)
        io = [tag] if tag else io
        a, ia = side(src)
        c1, i1 = sc(s1)
        c2, i2 = sc(s2)
        if op1 is None:
            op("v", lambda v: v.tensor_scalar(o, a, c1, None, op0), ia + i1, io)
        else:
            op("v", lambda v: v.tensor_scalar(o, a, c1, c2, op0, op1), ia + i1 + i2, io)

    def tt(out, a, b, op0, more=()):
        o, io = side(out)
        x, ix = side(a)
        y, iy = side(b)
        op("v", lambda v: v.tensor_tensor(o, x, y, op0), ix + iy + list(more), io)

    def cp(out, src, q="v", tag=None, more=()):
        o, io = side(out)
        a, ia = side(src)
        reads = ia + list(more) + (io[1:] if len(io) > 1 else [])
        writes = [tag] if tag else io[:1]
        if q == "v":
            op("v", lambda v: v.tensor_copy(o, a), reads, writes)
        elif q == "a":
            op("a", lambda s: s.activation(o, a, AF.Copy, bias=0.0, scale=1.0), reads, writes)
        else:
            op("g", lambda s: s.affine_select(o, a, [[0, len(range(*out[1:]))]], OP.is_ge, 0.0, 0, 0), reads, writes)

    def act(out, src, f, bias=0.0, scale=1.0, tag=None):
        o, io = side(out)
        a, ia = side(src)
        b, ib = sc(bias)
        c, ic = sc(scale)
        op("a", lambda s: s.activation(o, a, f, bias=b, scale=c), ia + ib + ic, [tag] if tag else io)

    def iota(out, pattern, base, ch, **kw):
        o, io = side(out)
        op("g", lambda q: q.iota(o, pattern, base, ch, **kw), [], io)

    def fill(out, c):
        o, io = side(out)
        op("v", lambda v: v.memset(o, c), [], io)

    def scan(out, d0, d1, first):
        op("v", lambda v: v.tensor_tensor_scan(X(out)[0], X(d0)[0], X(d1)[0], first, OP.mult, OP.add), [X(d0)[1], X(d1)[1]], [X(out)[1]])

    def total(out, src):
        op("v", lambda v: v.tensor_reduce(X(out)[0], X(src)[0], AxisListType.X, OP.add), [X(src)[1]], [X(out)[1]])

    def mm(out, lhsT, rhs, start=True, stop=True, more=()):
        o, io = side(out)
        a, ia = side(lhsT)
        b, ib = side(rhs)
        op("p", lambda t: t.matmul(o, a, b, start, stop), ia + ib + list(more), io)

    def acc(key, whole, out, lhsT, rhs):
        open_[key] = open_.get(key, 0) + 1
        mm(out, lhsT, rhs, open_[key] == 1, open_[key] == whole)

    def onto(a, m="sz"):
        return (m, 15 - a, 143 - a)

    def move(a, b):
        return ("se", 16 + 129 * a - b, 144 + 129 * a - b)

    nxt = T.cores[(rank + 1) % N]
    XR = ("xr", 0, XW + 1)

    H = GW // 4
    fill(("w1",), 1.0)
    fill(("xr", ZC, ZC + 8), 0.0)
    for lo in range(0, GW, H):
        dma([(T.gi[:, lo:lo + H], T.gn[:, lo:lo + H])], [], R("gi", lo, lo + H))
    h = 8 * CUT[0][1]
    dma([(T.n4[:, 0:h], T.nb[:, 0:h])], [], R("n4", 0, h))
    dma([(T.n4[:, h:GW], T.nb[:, h:GW])], [], R("n4", h, GW))
    dma([(T.xr[:, 0:ZC], T.x[:, 0:ZC])], [], R("xr", 0, ZC))
    dma([(T.xr[:, ZC + 1:XW + 1], T.x[:, ZC:XW])], [], R("xr", ZC, XW + 1))
    dma([(T.an[:, 0:L], T.a0[:])], [], R("an", 0, L))
    dma([(T.thi[:], T.th[:])], [], R("thi"))
    iota(("pi", 0, 1), [[0, 1]], 0, 1)
    iota(("jj",), [[1, L]], 0, 0)
    iota(("jr",), [[4, 3], [32, 8], [1, 16]], 4, 0, allow_small_or_imprecise_dtypes=True)
    for k in range(1, 4):
        dma([(T.n4[u::16, k * GW:(k + 1) * GW], T.nb[(u - k) % 16::16, :]) for u in range(16)], [], R("n4", k * GW, (k + 1) * GW))

    def turn_all():
        for s in DROT:
            dma([(T.g4[u::16, s * GW:(s + 1) * GW], T.g4[(u + 4 * s) % 16::16, 0:GW]) for u in range(16)], [R("g4", 0, GW)], R("g4", s * GW, (s + 1) * GW))

    op("g", lambda q: q.affine_select(T.se[:, 16:2064], T.w1[:], [[-1024, 16], [16, 8], [1025, 16]], OP.is_equal, 0.0, 0, -1), [R("w1")], [R("se", 16, 2064)])
    iota(("km", 0, 16), [[4, 4], [-3, 4]], 16, 0)
    ts(("pi", 1, 2), ("pi", 0, 1), 15, OP.bitwise_and)
    ts(("pi", 2, 3), ("pi", 0, 1), 4, OP.arith_shift_right)
    cp(("pf", 0, 3), ("pi", 0, 3))
    ROW, GRP = ("pf", 1, 2), ("pf", 2, 3)
    cp(("jf",), ("jj",))
    ts(("idn",), ("jf", 0, 128), ("pf", 0, 1), OP.is_equal)
    ts(("jt",), ("jj", 0, 128), 4, OP.arith_shift_right)
    ts(("bo",), ("jt",), GRP, OP.is_equal)
    ts(("sz",), ("w1", 0, 144), 0.0, OP.mult)
    cp(("sz", 15, 128, 16), ("bo", 0, 128, 16))
    for lo in (0, 2064):
        ts(("se", lo, lo + 16), ("w1", 0, 16), 0.0, OP.mult)
    ts(("u16",), ("jf", 0, 16), ROW, OP.is_equal)
    ts(("pf", 3, 4), ROW, 8.0, OP.mult)
    ts(("pf", 4, 5), ROW, 16.0, OP.mult)
    ts(("pf", 5, 6), ROW, 2048.0, OP.mult, 32768.0, OP.add)
    ts(("pf", 6, 7), ROW, 5.0, OP.is_ge)
    ts(("pf", 10, 11), GRP, 16.0, OP.mult, ("pf", 0, 1), OP.add)
    ts(("pf", 7, 8), ("pf", 10, 11), -1.0, OP.mult, -8.0, OP.add)
    ts(("pf", 8, 9), ROW, 15.0, OP.is_equal, 0.25, OP.mult)
    ts(("pf", 9, 10), ROW, 0.0, OP.is_equal)

    def prepare(tok):
        eng = tok[-1] if tok[-1] in "vg" else "a"
        k = int(tok.rstrip("vg")[1:])
        if tok[0] == "G":
            ts(("g4", k * H, k * H + H), ("gi", k * H, k * H + H), 1.0 + 2.0 ** -12, OP.mult, MAGIC, OP.add)
            act(("g4", k * H, k * H + H), ("g4", k * H, k * H + H), AF.Copy, bias=-(MAGIC + 2048.0))
        elif tok[0] in "OR":
            cp((tok[0].lower() + "0",) + CUT[k][0:2], ("n4", 8 * CUT[k][0], 8 * CUT[k][1], 8))
        elif tok[0] == "C":
            cp(("g16", k * H, k * H + H), ("g4", k * H, k * H + H), eng)
        elif tok[0] == "Q":
            s, lo = 1 + k % 3, H * (k // 3)
            bank = ("pa", "pb", "pd0", "pd1")[k % 4]
            mm((bank,), ("rt", (s - 1) * 128, s * 128), ("g16", lo, lo + H))
            cp(("g4", s * GW + lo, s * GW + lo + H), (bank,), eng)
        elif k == 0:
            fill(("wf", 0, 16), 0.5)
            fill(("wf", 16, 32), 0.0)
            ts(("kb", 0, 16), ("jj", 0, 16), 3, OP.bitwise_and)
            scan(("wf", 32, 48), ("wf", 0, 16), ("wf", 16, 32), 2.0)
            ts(("kb", 16, 32), ("jj", 0, 16), 2, OP.arith_shift_right)
            tt(("wf", 48, 64), ("wf", 32, 48), ("u16",), OP.mult)
            ts(("wf", 0, 16), ("kb", 0, 16), ROW, OP.is_gt, 2.0 ** -20 - 1.0, OP.mult)
            total(("pf", 11, 12), ("wf", 48, 64))
            ts(("wf", 16, 32), ("kb", 16, 32), ("pf", 8, 9), OP.mult, 1.0, OP.add)
            ts(("wf", 0, 16), ("wf", 0, 16), 1.0, OP.add, ("pf", 11, 12), OP.mult)
            ts(("w0",), ("w1", 0, L), ("pf", 11, 12), OP.mult)
            tt(("tw",), ("wf", 0, 16), ("wf", 16, 32), OP.mult)
        elif k == 1:
            cp(("ib",), ("idn",))
            ts(("bh",), ("bo",), 0.5, OP.mult)
            ts(("bn",), ("bo",), -2.0 ** 31, OP.mult)
        elif k == 2:
            ts(("cb",), ("jf", 0, 16), 256.0, OP.mult, ("pf", 4, 5), OP.add)
            ts(("z0",), ("jf", 0, 16), 128.0, OP.mult, ("pf", 3, 4), OP.add)
            ts(("c2",), ("jt", 8, 32), 1.0, OP.is_equal, 2048.0, OP.mult)
            ts(("c2", 16, 24), ("c2", 0, 8), 0.0, OP.mult)
            ts(("cb", 8, 16), ("cb", 8, 16), 1.0, OP.add)
        elif k == 3:
            ts(("thf", 0, 1), ("thi",), 1.0, OP.add, 1.0 / 16, OP.mult)
            ts(("thf", 1, 2), ("thi",), 32.5, OP.add)
            ts(("lim",), ("thi",), 1.0, OP.add)
        elif k == 4:
            ts(("km", 16, 32), ("km", 0, 16), 15, OP.bitwise_and)
            ts(("tm",), ("km", 16, 32), ROW, OP.is_equal)
            ts(("b15",), ("bo",), ("pf", 8, 9), OP.mult, 2.0 ** 30, OP.mult)
            cp(("one",), ("w1", 0, 128))
        elif k == 5:
            ts(("ibn",), ("idn",), -1.0, OP.mult)
            ts(("bm",), ("bo",), -1.0, OP.mult)
            ts(("b0",), ("bo",), ("pf", 9, 10), OP.mult)
            ts(("d5",), ("idn",), ("pf", 6, 7), OP.mult)
            ts(("ob",), ("jf", 0, 16), 16.0, OP.mult, ROW, OP.add)
            cp(("on",), ("w1", 0, L))
        elif k == 6:
            ts(("jt",), ("jj", 0, 128), 15, OP.bitwise_and)
            ts(("l2",), ("jt",), ROW, OP.is_gt)
            tt(("lt",), ("l2",), ("bo",), OP.mult)
        elif k == 7:
            cp(("wn", OG, OG + L), ("o16",), "g")
        elif k == 8:
            ts(("sz2",), ("sz",), 2.0, OP.mult)
            ts(("szn",), ("sz",), -1.0, OP.mult)
        else:
            op("g", lambda q: q.affine_select(T.sa[:], T.w1[:], [[1, 16], [16, 8], [0, 16]], OP.is_equal, 0.0, 0, -1), [R("w1")], [R("sa")])

    def turns():
        act(("r2",), ("jr",), AF.Abs, bias=("pf", 7, 8))
        ts(("rt",), ("r2",), 8.0, OP.is_equal)

    def run(tok, tau, toks):
        gen, t = divmod(tau, ST)
        last = t == ST - 1
        eng = tok[-1] if tok[-1] in "vg" else "a"
        tok, _, js = tok.rstrip("vg").partition(".")
        js, _, hs = js.partition(".")
        kind = tok.rstrip("0123456789") if tok[0:2] not in ("M1", "M2", "T1", "T2", "T3") else tok[0:2]
        num = int(tok[len(kind):]) if tok[len(kind):] else 0
        b = 0 if kind in ("EH", "EI", "OT") else num
        c0, c1, subs = (CUT + [(0, L, ())])[b]
        n = c1 - c0
        l0, l1 = c0 // 16, c1 // 16
        lc = l1 - l0
        pe, pd, pn = "pe%d" % b, "pd%d" % b, "pl%d" % b
        e0 = c0 + sum(subs[0:int(js)]) if js else c0
        e1 = e0 + subs[int(js)] if js else c1
        plain = "PA%d.%s" % (b, js) in toks
        halves = ["%s%d.%sv" % (k, b, js) in toks for k in ("AB", "AC")]
        if hs:
            e0, e1 = e0 + 32 * int(hs), e0 + 32 * int(hs) + 32
        copies = [("t%d" % k, e0, e1) for k in (0, 1, 2, 3, 4, 8)]
        qe, qr, qs = [("qq", o, o + n) for o in ((c0, 0, L + c0) if last else (3 * c0, 3 * c0 + n, 3 * c0 + 2 * n))]
        ng = ("qq", 3 * L + c0, 3 * L + c1)
        sco = (pd, 256, 256 + n)
        rp = (pe, 256, 256 + n)
        le, lr, ls = [("pl1" if last else pn, 400 + k * lc, 400 + (k + 1) * lc) for k in ((0, 0, 1) if last else (0, 1, 2))]
        hist = "ho" if t in (1, 2, 3) else "hn"
        xo = (hist, 32 * tau + l0, 32 * tau + l1)
        nl = (hist, 32 * tau + 16 + l0, 32 * tau + 16 + l1)
        li = [("li", LW * tau + 3 * l0 + k * lc, LW * tau + 3 * l0 + (k + 1) * lc) for k in ((1, 0, 2), (1, 2, 0), (1, 1, 1))[b]]
        lm, ln = [[(m,) + r[1:] for r in li] for m in ("lm", "ln")]
        both = (min(li[0][1], li[2][1]), max(li[0][2], li[2][2]))
        put = ("lo", 16 * tau + l0, 16 * tau + l1)
        ww = ("ww" if t else "w0", c0, c1)
        yi = ("yi",) if last else li[1]
        ao = L * tau
        if kind == "OW":
            cp(("o16", 0, L), ("g4", 0, GW, 8), eng)
        elif kind == "OT":
            bank = ("pa", "pb")[num % 2]
            mm((bank, 0, L), ("rt", (num - 1) * 128, num * 128), ("o16",))
            cp(("g4", num * GW, (num + 1) * GW, 8), (bank, 0, L), eng)
        elif kind == "RR":
            cp(("rr", c0, c1), (("n4",), ln[0]))
        elif kind == "WW":
            cp(ww, (("tw",), ln[2]), eng)
        elif kind == "OM":
            mm((pn, 0, n), ("idn",), ("rr", c0, c1), True, False)
            mm((pn, 0, n), ("b15",), ww, False, True)
        elif kind == "OF":
            ts(("of", c0, c1), (pn, 0, n), -8192.0, OP.add)
        elif kind == "RP":
            if not last:
                mm(rp, ("idn",), ("rr" if t else "r0", c0, c1))
        elif kind == "MK":
            cp(("m0", c0, c1), (("tm",), ln[2]), eng)
        elif kind == "NG":
            tt(ng, (("g4",), ln[0]), ("m0", c0, c1), OP.mult)
        elif kind == "NM":
            for a in range(16):
                rhs = ("qq", ng[1] + a, ng[2], 16) if t else ("o16", c0 + a, c1, 16)
                mm((pn, 384, 384 + lc), onto(a) if t else move(0, a), rhs, a == 0, a == 15)
        elif kind == "NL":
            ts(nl, (pn, 384, 384 + lc), 2048.0, OP.add)
        elif kind == "PZ":
            tt(("zz", l0, l1), lm[1], lm[0], OP.subtract)
        elif kind == "PY":
            ts(("zz", 16, 32), ("zz", 0, 16), 2048.0, OP.add)
        elif kind == "UC":
            cp(("ln",) + both, ("lm",) + both)
        elif kind == "E":
            cp(("eg", 16 * e0, 16 * e1), (("g4", 0, 4 * GW if t else GW), ("of" if t else "o0", e0, e1)), eng)
        elif kind == "F":
            for s in range(16):
                mm((pe, e0 - c0, e1 - c0), move(s, s), ("eg", 16 * e0 + s, 16 * e1, 16), s == 0, s == 15)
        elif kind == "D":
            an, o = ("an", ao) if t or tau == 0 else ("ao", ao - L)
            tt(("dd", c0, c1), (XR, nl), (an, o + c0, o + c1), OP.subtract)
        elif kind == "DA":
            act(("tr", 16 * c0, 16 * c1, 16), ("dd", c0, c1), AF.Abs, tag=("t0", c0, c1))
        elif kind == "TA":
            cp(("tr", 16 * e0 + 8, 16 * e1, 16), ("tr", 16 * e0, 16 * e1, 16), eng, ("t8", e0, e1), [("t0", e0, e1)])
            cp(("tr", 16 * e0 + 4, 16 * e1, 8), ("tr", 16 * e0, 16 * e1, 8), eng, ("t4", e0, e1), [("t0", e0, e1), ("t8", e0, e1)])
        elif kind in ("T1", "T2", "T3"):
            s = int(kind[1])
            cp(("tr", 16 * e0 + s, 16 * e1, 4), ("tr", 16 * e0, 16 * e1, 4), eng, ("t%d" % s, e0, e1), [("t%d" % k, e0, e1) for k in (0, 4, 8)])
        elif kind == "XL":
            ts(("xl", e0, e1), (pe, e0 - c0, e1 - c0), 2048.0, OP.add)
        elif kind == "X":
            out = ("uu", 16 * e0, 16 * e1)
            if plain:
                cp(out, (XR, ("xl", e0, e1)), eng)
            else:
                tt(out, (XR, ("xl", e0, e1)), ("tr", 16 * e0, 16 * e1), OP.add, more=copies)
        elif kind in ("PA", "PB"):
            h = int(kind == "PB")
            wide = "T1%d.%s" % (b, js) in [k.rstrip("vg") for k in toks]
            mm((kind.lower(),), ("idn",), ("uu", 16 * e0 + h, 16 * e1, 2), True, False)
            if wide:
                mm((kind.lower(),), ("ib",), ("tr", 16 * e0 + h, 16 * e1, 2), False, True, copies)
            for s in range(0 if wide else 8):
                mm((kind.lower(), s, 512, 8), ("ib",), ("tr", 16 * e0, 16 * e1, 16), False, s == 7, [("t0", e0, e1)])
        elif kind in ("AB", "AC"):
            h = int(kind == "AC")
            src = (("pa", "pb")[h],) if plain else ("uu", 16 * e0 + h, 16 * e1, 2)
            out = ("ab", 8 * (e0 + (e1 if h else e0)), 8 * (e1 + (e1 if h else e0)))
            if eng == "a":
                act(out, src, AF.Abs, bias=-255.0)
            else:
                ts(out, src, 255.0, OP.max, -127.5, OP.add)
        elif kind in ("AM", "AN", "AU", "AV"):
            h = int(kind in ("AN", "AV"))
            o, m = 8 * (e0 + (e1 if h else e0)), e1 - e0
            for s in range(8):
                u = 2 * s + h
                if kind in ("AU", "AV"):
                    lhs, rhs = onto(u, "szn"), ("uu", 16 * e0 + u, 16 * e1, 16)
                else:
                    lhs, rhs = onto(u, "sz2" if halves[h] else "sz"), ("ab", o + s, o + 8 * m, 8)
                acc((tau, e0), 16 + 8 * sum(halves), (pd, e0 - c0, e1 - c0), lhs, rhs)
        elif kind == "GO":
            if eng == "a":
                act((pd, 0, n), (pd, 0, n), AF.Relu, bias=("lim",), scale=-1.0)
            else:
                ts((pd, 0, n), (pd, 0, n), ("lim",), OP.is_lt)
        elif kind == "GV":
            tt(("ok", c0, c1), (pd, 0, n), ww, OP.min)
        elif kind == "GM":
            mm(sco, ("bh",), ("ok", c0, c1))
        elif kind == "PF":
            tt(("ff", c0, c1), ("ok", c0, c1), sco, OP.is_gt)
        elif kind == "PW":
            if eng == "a":
                act(qs, ("ff", c0, c1), AF.Copy, scale=("pf", 5, 6))
            else:
                ts(qs, ("ff", c0, c1), ("pf", 5, 6), OP.mult)
        elif kind == "PQ":
            tt(qe, ("ff", c0, c1), (pe, 0, n), OP.mult)
            if not last:
                tt(qr, ("ff", c0, c1), rp, OP.mult)
        elif kind == "PC":
            if not last:
                mm((le[0], le[1], ls[2]), ("idn",), ("c2",), True, False)
            for a in range(16):
                mm((le[0], le[1], ls[2]), onto(a), ("qq", qe[1] + a, qs[2], 16), last and a == 0, a == 15)
        elif kind == "YM":
            mm((pd, 0, n), ("ib",), ("tr", 16 * c0, 16 * c1, 16), True, False, [("t0", c0, c1)])
            mm((pd, 0, n), ("bn",), ("ok", c0, c1), False, True)
        elif kind == "YY":
            if eng == "a":
                act(("yy", c0, c1), (pd, 0, n), AF.Relu)
            else:
                ts(("yy", c0, c1), (pd, 0, n), 0.0, OP.max)
        elif kind == "M1":
            if last:
                for o, m in ((0, 8), (8, 32)):
                    tt(("ti", o, o + 8), (ls[0], ls[1] + o, ls[1] + o + 8), ("lm", LW * tau + m, LW * tau + m + 8), OP.max)
                tt(yi, ("ti", 0, 16), ("zz", 16, 32), OP.add)
            else:
                tt(("ti", l0, l1), ls, lm[0] if t else ("z0", l0, l1), OP.max)
                if t:
                    tt(("ti", 16 + l0, 16 + l1), lr, ("zz", l0, l1), OP.add)
                tt(yi, ("ti", l0, l1), ("ti", 16 + l0, 16 + l1) if t else lr, OP.add)
        elif kind == "ML":
            o = LW * tau + 3 * l0
            ts(li[2], yi, 11, OP.arith_shift_right, 15, OP.bitwise_and)
            if not last:
                ts(li[0], yi, 8191, OP.bitwise_and)
                send(nxt, "li", o, o + 3 * lc, "lm", o + LW, "li%d_%d" % (tau, b))
        elif kind == "CS":
            o = LW * tau
            tt(("li", o + 48, o + 64), ("li", o + 16, o + 32), ("cb",), OP.add)
            cp(("lo", put[1], put[1] + 16), ("li", o + 48, o + 64))
        elif kind == "XO":
            ts(xo, le, 2048.0, OP.add)
        elif kind == "M2":
            tt(("ao", ao + c0, ao + c1), (XR, xo), ("yy", c0, c1), OP.max)
            if not last:
                send(nxt, "ao", ao + c0, ao + c1, "an", ao + L + c0, "ar%d_%d" % (tau, b))
        elif kind == "HI":
            send(T.cores[(rank - t) % N], "ho", 32 * tau, 32 * tau + 32, "hn", 32 * tau, "h%d" % tau)
        elif kind in ("ST", "CA", "CB", "CC", "CE") and tau == TAU - 1:
            return
        elif kind == "ST":
            cp((XR, ("lo", put[1], put[1] + 16)), ("ao", ao, ao + L))
        elif kind == "CA":
            ts(("hc",), (hist, 32 * tau, 32 * tau + 16), float(ZC), OP.is_equal)
            mm(("pa", 256, 272), ("one",), ("hc",))
        elif kind == "CB":
            op("a", lambda s: s.activation(T.wf[:, 0:16], T.pa[:, 256:272], AF.Identity, bias=T.thf[:, 0:1], accum_out=T.af[:]),
               [("pa", 256, 272), R("thf")], [("wf", 0, 16), R("af")])
        elif kind == "CC":
            ts(("ai",), ("af",), ("thf", 1, 2), OP.subtract, 1.0 / 64, OP.mult)
        elif kind == "CE":
            ts(("lim",), ("ai",), -64.0, OP.mult, ("af",), OP.add)
        elif kind == "EE":
            o = 32 * ST * gen
            ts(("hv",), ("hn", o, o + 128), -2048.0, OP.add)
            ts(("hf",), ("hv",), 0.0, OP.is_equal)
        elif kind == "EC":
            tt(("hm", 0, 112), ("hf", 0, 112), ("hv", 16, 128), OP.mult)
            tt(("hw", 0, 112), ("hv", 0, 112), ("hm", 0, 112), OP.add)
        elif kind == "ED":
            tt(("e1",), ("hf", 0, 48), ("hf", 64, 112), OP.add)
            tt(("hw", 112, 128), ("e1", 0, 16), ("e1", 32, 48), OP.add)
        elif kind == "EF":
            mm(("pa", 0, L), ("b0",), ("on",), True, False)
            for a in range(16):
                mm(("pa", a, L, 16), ("sa", 128 * a, 128 * a + 128), ("hw", 112, 128), False, False)
        elif kind == "EG":
            mm(("pl0", 0, L), ("d5",), ("o16",), True, False)
        elif kind == "EH":
            for a in range(16):
                mm(("pl0", a, L, 16), move(a, num), ("hw", 32 * num, 32 * num + 16), False, False)
        elif kind == "EI":
            for a in range(num, 16, 4):
                if eng == "a":
                    act(("ed", a, 7 * L, 16), ("hw", 0, 112), AF.Copy, scale=("u16", a, a + 1), tag=("ed%d" % a, 0, 1))
                else:
                    ts(("ed", a, 7 * L, 16), ("hw", 0, 112), ("u16", a, a + 1), OP.mult, tag=("ed%d" % a, 0, 1))
        elif kind == "EJ":
            for s in range(4):
                mm(("pl0", 0, L), onto(s), ("ed", 2 * s * L, 2 * s * L + L), False, False, [("ed%d" % a, 0, 1) for a in range(16)])
        elif kind == "FL":
            fl = (pe, 256, 256 + n)
            mm(fl, ("b0",), ("on", c0, c1), True, False)
            mm(fl, ("bm",), ("ff", c0, c1), False, True)
            tt(("nf", c0, c1), ng, fl, OP.mult)
        elif kind == "SH":
            mm(("pl0", 0, L), onto(4), ("qq", 0, L), False, False)
            mm(("pl0", 0, L), onto(4), ("nf",), False, True)
        elif kind == "SG":
            if gen < GENS - 1:
                cp(("da",), ("pl0", 0, L), eng)
            else:
                ts(("fo", 0, L), ("pl0", 0, L), 0.0, OP.is_le, 2047.0, OP.add)
                tt(("da",), ("fo", 0, L), ("pl0", 0, L), OP.add)
        elif kind == "SA":
            mm(("pa", 0, L), ("bm",), ("ff",), False, True)
            ts(("ind",), ("pa", 0, L), ROW, OP.is_equal)
        elif kind == "SD":
            scan(("pre",), ("on",), ("ind",), 0.0)
            mm(("pa", 300, 301), ("lt",), ("pre", L - 1, L))
        elif kind == "SE":
            ts(("pa", 0, L), ("pre",), ("pa", 300, 301), OP.add, -1.0, OP.add)
        elif kind == "SF":
            tt(("x2",), ("ind",), ("pa", 0, L), OP.mult)
            for a in range(16):
                mm(("pa", 320, 336), onto(a), ("x2", a, L, 16), a == 0, a == 15)
        elif kind == "SB":
            cp(("pl",), ("pa", 320, 336))
            cp((("wn", SR, SR + L), ("pl",)), ("da",))
            send(nxt, "wn", SR, SR + K, "wn", BI[gen], "b%d" % gen)
        elif kind == "SC":
            ts(("kf", 0, 16), ("pa", 320, 336), float(L - K), OP.is_lt, 4096.0, OP.mult)
            ts(("kf", 16, 32), ("pa", 320, 336), -1.0, OP.mult, float(L - 1 + BI[gen] - OG), OP.add)
            tt(("kf", 32, 48), ("kf", 0, 16), ("kf", 16, 32), OP.add)
            tt(("kf", 48, 64), ("kf", 32, 48), ("ob",), OP.min)
            ts(("pr",), ("kf", 48, 64), float(OG - BI[gen]), OP.add)
        elif kind == "SM":
            cp(("wn", BI[gen], BI[gen] + K, 2), ("wn", SR, SR + K, 2), eng)
        elif kind == "SN":
            cp(("g4", 0, GW, 8) if gen < GENS - 1 else ("fo", 0, L), (("wn", BI[gen], OG + L), ("pr",)))
            if gen == GENS - 1:
                dma([(T.yg[:], T.fo[:, 0:L])], [R("fo", 0, L)], None, True)
        elif gen < GENS - 1:
            return
        elif kind == "EK":
            ts(("x1",), ("o16",), 0.0, OP.is_le, 2047.0, OP.add)
            tt(("wn", OG, OG + L), ("x1",), ("o16",), OP.add)
        elif kind == "YS":
            for h in range(2):
                o = h * (ZC + 1)
                for s in range(16):
                    mm(("pb", 128 * h, 128 * h + 128), ("ib",), ("xr", o + s, o + ZC, 16), s == 0, s == 15)
            cp(("fo", 2 * L, 3 * L), ("pb", 0, L), eng)
        elif kind == "YO":
            cp(("dd", c0, c1), (XR, put), eng)
        elif kind == "YD":
            mm((pe, 0, n), ("ib",), ("ao", ao + c0, ao + c1), True, False)
            mm((pe, 0, n), ("ibn",), ("dd", c0, c1), False, True)
            tt(("fo", 2 * L + c0, 2 * L + c1), ("fo", 2 * L + c0, 2 * L + c1), (pe, 0, n), OP.add)
        elif kind == "YE":
            dma([(T.ys[:], T.fo[:, 2 * L:3 * L])], [R("fo", 2 * L, 3 * L)], None, True)
        elif kind == "YA":
            cp(("fo", L, 2 * L), ("ao", ao, ao + L), eng)
            dma([(T.ya[:], T.fo[:, L:2 * L])], [R("fo", L, 2 * L)], None, True)

    once = {"RT": turns, "RA": turn_all}
    for tau in range(TAU):
        t = tau % ST
        toks = LAST if t == ST - 1 else ORDER if t else AGAIN if tau else FIRST
        for tok in toks:
            if tok[0] in "GORLQC" and tok.rstrip("vg")[1:].isdigit():
                if tau < 2:
                    prepare(tok)
            elif tok in once:
                if t == 0 or tau == 1:
                    once[tok]()
            elif tok[-1] == "'":
                if tau + 1 < TAU:
                    run(tok[0:-1], tau + 1, ())
            else:
                run(tok, tau, toks)

    for s, n in nd:
        if known["s"].get(s, 0) < n:
            g.sync.wait_ge(T.sem[s], n)
    g.wait_ge(T.sem.loc, locs[0])
    for s in ("v", "a", "p", "gc"):
        g.sync.wait_ge(T.sem[s], cnt[s])
